import numpy as np
import ml_dtypes


def mxq(x, axis, fmt="e4m3"):
    dtype, down = {"e4m3": (ml_dtypes.float8_e4m3fn, 7), "e5m2": (ml_dtypes.float8_e5m2, 14)}[fmt]
    v = np.moveaxis(np.asarray(x, np.float32).astype(ml_dtypes.bfloat16).astype(np.float64), axis, -1)
    blocks = v.reshape(v.shape[:-1] + (-1, 32))
    amax = np.abs(blocks).max(-1, keepdims=True)
    byte = np.maximum(np.where(amax > 0, np.frexp(amax)[1] - 1 + 127, 0) - down, 1)
    scale = np.exp2(byte - 127.0)
    codes = (blocks / scale).astype(np.float32).astype(dtype).astype(np.float64)
    return np.moveaxis((codes * scale).reshape(v.shape), -1, axis)


WIDE = False


def mx_kscale(k):
    if not WIDE:
        return np.ones(k)
    levels = np.array([10, -10, 5, -5, 0])
    if k % 512:
        return np.exp2(np.random.permutation(np.resize(levels, k // 32))).repeat(32)
    a = np.empty((k // 512, 16))
    for p in range(k // 512):
        a[p, :8] = np.random.permutation(np.resize(levels, 8))
        for g in range(8):
            far = levels[np.abs(levels - a[p, g]) >= 10]
            a[p, g + 8] = far[np.random.randint(len(far))]
    return np.exp2(a.ravel()).repeat(32)


def f64(x):
    return np.asarray(x).astype(np.float64)


def striped(idx):
    return np.tile(idx.reshape(-1, 16).T, (8, 1)).astype(np.uint16)


def unstriped(offs):
    return offs[:16].T.reshape(-1).astype(np.int64)


E2M1 = np.array([0.0, 0.5, 1.0, 1.5, 2.0, 3.0, 4.0, 6.0, -0.0, -0.5, -1.0, -1.5, -2.0, -3.0, -4.0, -6.0])


def pack_weight(w, fmt):
    k, n = w.shape
    w = f64(np.asarray(w, np.float32).astype(ml_dtypes.bfloat16)).reshape(k // 32, 32, n)
    amax = np.abs(w).max(1)
    if fmt == "e4m3":
        byte = np.frexp(amax)[1] - 1 + 127 - 7
    else:
        mant, ex = np.frexp(amax / 6.0)
        byte = np.where(mant > 0.5, ex, ex - 1) + 127
    byte = np.clip(np.where(amax > 0, byte, 1), 1, 254)
    scaled = (w * np.exp2(127.0 - byte)[:, None, :]).reshape(k, n).astype(np.float32)
    by_word = np.ascontiguousarray(scaled.reshape(k // 512, 128, 4, n).transpose(0, 1, 3, 2))
    if fmt == "e4m3":
        words = by_word.astype(ml_dtypes.float8_e4m3fn).view(np.uint8)
    else:
        c = by_word.astype(ml_dtypes.float4_e2m1fn).view(np.uint8) & 0xF
        words = (c[..., 0::2] | (c[..., 1::2] << 4)).reshape(k // 512, 128, 2 * n)
    return np.ascontiguousarray(words), np.ascontiguousarray(byte.astype(np.uint8).reshape(k // 512, 16, n))


def unpack_weight(words, scales, fmt):
    g, _, n = scales.shape
    words = np.ascontiguousarray(words).reshape(g, 128, n, -1)
    if fmt == "e4m3":
        vals = words.view(ml_dtypes.float8_e4m3fn).astype(np.float64)
    else:
        nib = np.empty((g, 128, n, 4), np.uint8)
        nib[..., 0::2] = words & 0xF
        nib[..., 1::2] = words >> 4
        vals = E2M1[nib]
    vals = vals * np.repeat(np.exp2(scales.astype(np.float64) - 127.0), 8, axis=1)[..., None]
    return vals.transpose(0, 1, 3, 2).reshape(g * 512, n)


K, T, E, C, N = 128, 768, 12, 128, 1024


def by_expert(wq, xq):
    return np.concatenate([wq[e].T @ xq[:, e * C:(e + 1) * C] for e in range(E)], axis=1)


def setup_inputs():
    n = np.random.standard_normal
    s = mx_kscale(N)[:, None]
    first = np.random.permutation(np.repeat(np.arange(E), T // E))
    second = (first + 1 + np.random.permutation(np.repeat(np.arange(E - 1), -(-T // (E - 1)))[:T])) % E
    while np.bincount(second, minlength=E).max() != T // E:
        load = np.bincount(second, minlength=E); hi, lo = int(load.argmax()), int(load.argmin())
        t = np.flatnonzero((second == hi) & (first != lo))[0]; second[t] = lo
    slot_token = np.empty(E * C, np.int64); pos = np.empty((2, T), np.int64); fill = np.zeros(E, np.int64)
    place = np.stack([np.random.permutation(C) for _ in range(E)])
    for r, deal in enumerate((first, second)):
        for t in np.random.permutation(T):
            e = deal[t]; j = e * C + place[e, fill[e]]; fill[e] += 1; slot_token[j] = t; pos[r, t] = j
    g = np.random.uniform(0.2, 0.8, T)
    w_slot = np.empty(E * C); w_slot[pos[0]] = g; w_slot[pos[1]] = 1.0 - g
    w = [pack_weight(m, "e2m1") for m in n((E, N, K)) / np.sqrt(N) / s[None]]
    return {
        "dyT": (n((N, T)) * s).astype(np.float32),
        "w_words": np.stack([m[0] for m in w]),
        "w_scales": np.stack([m[1] for m in w]),
        "gate": np.tile(w_slot, (N, 1)).astype(np.float32),
        "offs": striped(slot_token),
        "pos1": striped(pos[0]),
        "pos2": striped(pos[1]),
    }


def reference(dyT, w_words, w_scales, gate, offs, pos1, pos2):
    idx = unstriped(offs)
    w = np.stack([unpack_weight(w_words[e], w_scales[e], "e2m1") for e in range(E)])
    gq = mxq(f64(gate) * f64(dyT)[:, idx], 0, "e4m3")
    dx = by_expert(w, gq)
    return dx[:, unstriped(pos1)] + dx[:, unstriped(pos2)]

@@ -1,0 +1,167 @@
+from contextlib import ExitStack
+
+import concourse.mybir as mybir
+
+F32 = mybir.dt.float32
+BF16 = mybir.dt.bfloat16
+U32 = mybir.dt.uint32
+I32 = mybir.dt.int32
+U16 = mybir.dt.uint16
+U8 = mybir.dt.uint8
+FP8X4 = mybir.dt.float8_e4m3fn_x4
+FP4X4 = mybir.dt.float4_e2m1fn_x4
+MULT = mybir.AluOpType.mult
+
+P = 128
+K, T, E, C, N = 128, 768, 12, 128, 1024
+S = E * C
+PASSES = N // 512
+PACK = 4
+
+FLOPS = 2 * N * K * S
+BYTES = 4 * N * T + E * N * K // 2 + E * N * K // 32 + 4 * S + 2 * P * (S + 2 * T) // 16 + 4 * K * T
+
+CHUNK = S // 2
+HEAD = 256
+WIDE = T + 16
+
+PIECES = (
+    (0, 0, 0, 768, 1),
+    (0, 1, 0, 768, 2),
+    (1, 0, 0, 384, 2),
+    (1, 0, 384, 768, 2),
+    (1, 1, 0, 384, 2),
+    (1, 1, 384, 576, 2),
+    (1, 1, 576, 704, 1),
+    (1, 1, 704, 768, 0),
+)
+
+
+def tile_moe_bdx_lin_none_kernel(tc, dyT, w_words, w_scales, gate, offs, pos1, pos2, out):
+    nc = tc.nc
+    with ExitStack() as ctx:
+        lists = ctx.enter_context(tc.tile_pool(name="lists", bufs=1))
+        keep = ctx.enter_context(tc.tile_pool(name="keep", bufs=1))
+        psum = ctx.enter_context(tc.psum_pool(name="psum", bufs=1))
+
+        offs_sb = lists.tile([P, S // 16], U16, name="offs_sb")
+        pos1_sb = lists.tile([P, T // 16], U16, name="pos1_sb")
+        pos2_sb = lists.tile([P, T // 16], U16, name="pos2_sb")
+
+        w_sb = keep.tile([P, E * PASSES, 2 * K], U8, name="w_sb", align_bytes=64)
+        ws_sb = keep.tile([P, E * PASSES, K], U8, name="ws_sb", align_bytes=64)
+        gate_sb = keep.tile([P, S], F32, name="gate_sb")
+        planes = {}
+        for a in range(PASSES):
+            for d in range(PACK):
+                planes[a, d] = keep.tile([P, WIDE], F32, name=f"dy_{a}_{d}")
+        dx = keep.tile([P, S], F32, name="dx")
+
+        for plane in reversed([planes[a, d] for a in range(PASSES) for d in range(PACK)]):
+            nc.gpsimd.memset(plane[:, T:WIDE], 0.0)
+
+        rows = dyT.rearrange("(a p d) t -> a d p t", a=PASSES, d=PACK)
+        nc.sync.dma_start(offs_sb[:], offs)
+        nc.scalar.dma_start(out=gate_sb[:, 0:HEAD], in_=gate[0:P, 0:HEAD])
+        nc.sync.dma_start(out=planes[0, 0][:, 0:T], in_=rows[0, 0])
+        nc.sync.dma_start(out=gate_sb[:, HEAD:CHUNK], in_=gate[0:P, HEAD:CHUNK])
+        for a in range(PASSES):
+            for d in range(PACK):
+                if a + d > 0:
+                    nc.sync.dma_start(out=planes[a, d][:, 0:T], in_=rows[a, d])
+        nc.sync.dma_start(out=gate_sb[:, CHUNK:S], in_=gate[0:P, CHUNK:S])
+        nc.sync.dma_start(pos1_sb[:], pos1)
+        nc.sync.dma_start(pos2_sb[:], pos2)
+        nc.vector.memset(ws_sb[:].rearrange("p g k -> p (g k)").bitcast(I32), 0)
+        words = w_words.bitcast(I32).rearrange("e a p n -> p (e a) n")
+        w_i32 = w_sb[:].bitcast(I32)
+        half = E * PASSES // 2
+        nc.sync.dma_start(out=w_i32[:, 0:half, :], in_=words[:, 0:half, :])
+        scale_rows = w_scales.bitcast(I32).rearrange("e a f k -> f (e a) k")
+        ws_i32 = ws_sb[:].bitcast(I32)
+        for q in range(4):
+            nc.sync.dma_start(out=ws_i32[32 * q : 32 * q + 4, :, :], in_=scale_rows[4 * q : 4 * q + 4, :, :])
+        nc.sync.dma_start(out=w_i32[:, half:, :], in_=words[:, half:, :])
+
+        g4, gb, codes, scales = {}, {}, {}, {}
+        for c in range(S // CHUNK):
+            for a in range(PASSES):
+                g4[c, a] = keep.tile([P, PACK, CHUNK], F32, name=f"g4_{c}_{a}")
+                gb[c, a] = keep.tile([P, CHUNK * PACK], BF16, name=f"gb_{c}_{a}", align_bytes=64)
+                codes[c, a] = keep.tile([P, CHUNK], U32, name=f"codes_{c}_{a}", align_bytes=64)
+                scales[c, a] = keep.tile([P, CHUNK], U8, name=f"scales_{c}_{a}", align_bytes=64)
+
+        def gather(c, a, d, lo, hi):
+            first, last = c * CHUNK + lo, c * CHUNK + hi
+            nc.vector.tensor_tensor(
+                g4[c, a][:, d, lo:hi],
+                planes[a, d][:].indirect(offs_sb[:, first // 16 : last // 16]),
+                gate_sb[:, first:last],
+                MULT,
+            )
+
+        def interleave(copy, c, a, lo, hi):
+            copy(
+                gb[c, a][:, PACK * lo : PACK * hi].rearrange("p (n i d) -> p n d i", d=PACK, i=4),
+                g4[c, a][:, :, lo:hi].rearrange("p d (n i) -> p n d i", i=4),
+            )
+
+        def quantise(c, a, lo, hi):
+            while lo < hi:
+                width = max(w for w in (512, 256, 128, 64) if lo + w <= hi)
+                nc.vector.quantize_mx(
+                    out=codes[c, a][:, lo : lo + width].bitcast(FP8X4),
+                    scales=scales[c, a][:, lo : lo + width],
+                    in_=gb[c, a][:, PACK * lo : PACK * (lo + width)],
+                )
+                lo += width
+
+        def multiply(copy, c, lo, hi):
+            bank = psum.tile([P, 512], F32, name=f"bank_{c}_{lo}")
+            for at in range(lo, hi, C):
+                e = (c * CHUNK + at) // C
+                for a in range(PASSES):
+                    nc.tensor.matmul_mx(
+                        out=bank[:, at - lo : at - lo + C],
+                        lhsT=w_sb[:, PASSES * e + a, :].bitcast(FP4X4),
+                        lhsT_scale=ws_sb[:, PASSES * e + a, :],
+                        rhs=codes[c, a][:, at : at + C].bitcast(FP8X4),
+                        rhs_scale=scales[c, a][:, at : at + C],
+                        start=(a == 0),
+                        stop=(a == PASSES - 1),
+                    )
+            copy(dx[:, c * CHUNK + lo : c * CHUNK + hi], bank[:, 0 : hi - lo])
+
+        def finish(c, a, lo, hi):
+            quantise(c, a, lo, hi)
+            if a < PASSES - 1:
+                return
+            first, last = lo // C * C, hi // C * C
+            step = 512 if c == 0 else C
+            for at in range(first, last, step):
+                end = min(at + step, last)
+                multiply(nc.vector.tensor_copy if c * CHUNK + end == S else nc.scalar.copy, c, at, end)
+
+        done = 0
+        for i, (c, a, lo, hi, lag) in enumerate(PIECES):
+            for d in range(PACK):
+                if i + d == 0:
+                    gather(c, a, d, lo, HEAD)
+                    gather(c, a, d, HEAD, hi)
+                else:
+                    gather(c, a, d, lo, hi)
+            interleave(nc.vector.tensor_copy if i == len(PIECES) - 1 else nc.scalar.copy, c, a, lo, hi)
+            while done + PIECES[done][4] <= i:
+                finish(*PIECES[done][:4])
+                done += 1
+                if done == len(PIECES):
+                    break
+
+        one = keep.tile([P, T], F32, name="one")
+        two = keep.tile([P, T], F32, name="two")
+        both = keep.tile([P, T], F32, name="both")
+        nc.vector.tensor_copy(one[:], dx[:].indirect(pos1_sb[:]))
+        for lo, hi in ((0, 512), (512, T)):
+            nc.vector.tensor_copy(two[:, lo:hi], dx[:].indirect(pos2_sb[:, lo // 16 : hi // 16]))
+            nc.vector.tensor_tensor(both[:, lo:hi], one[:, lo:hi], two[:, lo:hi], mybir.AluOpType.add)
+            nc.sync.dma_start(out=out[:, lo:hi], in_=both[:, lo:hi])

@@ -158,10 +158,10 @@ def tile_moe_bdx_lin_none_kernel(tc, dyT, w_words, w_scales, gate, offs, pos1, p
                     break
 
         one = keep.tile([P, T], F32, name="one")
-        two = keep.tile([P, T], F32, name="two")
         both = keep.tile([P, T], F32, name="both")
         nc.vector.tensor_copy(one[:], dx[:].indirect(pos1_sb[:]))
         for lo, hi in ((0, 512), (512, T)):
-            nc.vector.tensor_copy(two[:, lo:hi], dx[:].indirect(pos2_sb[:, lo // 16 : hi // 16]))
-            nc.vector.tensor_tensor(both[:, lo:hi], one[:, lo:hi], two[:, lo:hi], mybir.AluOpType.add)
+            nc.vector.tensor_tensor(
+                both[:, lo:hi], dx[:].indirect(pos2_sb[:, lo // 16 : hi // 16]), one[:, lo:hi], mybir.AluOpType.add
+            )
             nc.sync.dma_start(out=out[:, lo:hi], in_=both[:, lo:hi])

@@ -11,6 +11,7 @@ U8 = mybir.dt.uint8
 FP8X4 = mybir.dt.float8_e4m3fn_x4
 FP4X4 = mybir.dt.float4_e2m1fn_x4
 MULT = mybir.AluOpType.mult
+ADD = mybir.AluOpType.add
 
 P = 128
 K, T, E, C, N = 128, 768, 12, 128, 1024
@@ -21,20 +22,9 @@ PACK = 4
 FLOPS = 2 * N * K * S
 BYTES = 4 * N * T + E * N * K // 2 + E * N * K // 32 + 4 * S + 2 * P * (S + 2 * T) // 16 + 4 * K * T
 
-CHUNK = S // 2
-HEAD = 256
-WIDE = T + 16
-
-PIECES = (
-    (0, 0, 0, 768, 1),
-    (0, 1, 0, 768, 2),
-    (1, 0, 0, 384, 2),
-    (1, 0, 384, 768, 2),
-    (1, 1, 0, 384, 2),
-    (1, 1, 384, 576, 2),
-    (1, 1, 576, 704, 1),
-    (1, 1, 704, 768, 0),
-)
+BIG = 1024
+HEAD = 384
+WIDE = 1040
 
 
 def tile_moe_bdx_lin_none_kernel(tc, dyT, w_words, w_scales, gate, offs, pos1, pos2, out):
@@ -42,6 +32,7 @@ def tile_moe_bdx_lin_none_kernel(tc, dyT, w_words, w_scales, gate, offs, pos1, p
     with ExitStack() as ctx:
         lists = ctx.enter_context(tc.tile_pool(name="lists", bufs=1))
         keep = ctx.enter_context(tc.tile_pool(name="keep", bufs=1))
+        ring = ctx.enter_context(tc.tile_pool(name="ring", bufs=2))
         psum = ctx.enter_context(tc.psum_pool(name="psum", bufs=1))
 
         offs_sb = lists.tile([P, S // 16], U16, name="offs_sb")
@@ -58,18 +49,18 @@ def tile_moe_bdx_lin_none_kernel(tc, dyT, w_words, w_scales, gate, offs, pos1, p
         dx = keep.tile([P, S], F32, name="dx")
 
         for plane in reversed([planes[a, d] for a in range(PASSES) for d in range(PACK)]):
-            nc.gpsimd.memset(plane[:, T:WIDE], 0.0)
+            nc.vector.memset(plane[:, T:WIDE], 0.0)
 
         rows = dyT.rearrange("(a p d) t -> a d p t", a=PASSES, d=PACK)
         nc.sync.dma_start(offs_sb[:], offs)
         nc.scalar.dma_start(out=gate_sb[:, 0:HEAD], in_=gate[0:P, 0:HEAD])
         nc.sync.dma_start(out=planes[0, 0][:, 0:T], in_=rows[0, 0])
-        nc.sync.dma_start(out=gate_sb[:, HEAD:CHUNK], in_=gate[0:P, HEAD:CHUNK])
+        nc.sync.dma_start(out=gate_sb[:, HEAD:BIG], in_=gate[0:P, HEAD:BIG])
         for a in range(PASSES):
             for d in range(PACK):
                 if a + d > 0:
                     nc.sync.dma_start(out=planes[a, d][:, 0:T], in_=rows[a, d])
-        nc.sync.dma_start(out=gate_sb[:, CHUNK:S], in_=gate[0:P, CHUNK:S])
+        nc.sync.dma_start(out=gate_sb[:, BIG:S], in_=gate[0:P, BIG:S])
         nc.sync.dma_start(pos1_sb[:], pos1)
         nc.sync.dma_start(pos2_sb[:], pos2)
         nc.vector.memset(ws_sb[:].rearrange("p g k -> p (g k)").bitcast(I32), 0)
@@ -84,84 +75,100 @@ def tile_moe_bdx_lin_none_kernel(tc, dyT, w_words, w_scales, gate, offs, pos1, p
         nc.sync.dma_start(out=w_i32[:, half:, :], in_=words[:, half:, :])
 
         g4, gb, codes, scales = {}, {}, {}, {}
-        for c in range(S // CHUNK):
-            for a in range(PASSES):
-                g4[c, a] = keep.tile([P, PACK, CHUNK], F32, name=f"g4_{c}_{a}")
-                gb[c, a] = keep.tile([P, CHUNK * PACK], BF16, name=f"gb_{c}_{a}", align_bytes=64)
-                codes[c, a] = keep.tile([P, CHUNK], U32, name=f"codes_{c}_{a}", align_bytes=64)
-                scales[c, a] = keep.tile([P, CHUNK], U8, name=f"scales_{c}_{a}", align_bytes=64)
 
-        def gather(c, a, d, lo, hi):
-            first, last = c * CHUNK + lo, c * CHUNK + hi
+        def gather(a, d, lo, hi, first, last):
+            if (a, first) not in g4:
+                g4[a, first] = ring.tile([P, PACK, last - first], F32, name="g4")
             nc.vector.tensor_tensor(
-                g4[c, a][:, d, lo:hi],
-                planes[a, d][:].indirect(offs_sb[:, first // 16 : last // 16]),
-                gate_sb[:, first:last],
+                g4[a, first][:, d, lo - first : hi - first],
+                planes[a, d][:].indirect(offs_sb[:, lo // 16 : hi // 16]),
+                gate_sb[:, lo:hi],
                 MULT,
             )
 
-        def interleave(copy, c, a, lo, hi):
+        def interleave(copy, a, lo, hi, first, last):
+            if (a, first) not in gb:
+                gb[a, first] = keep.tile([P, PACK * (last - first)], BF16, name=f"gb_{a}_{first}", align_bytes=64)
             copy(
-                gb[c, a][:, PACK * lo : PACK * hi].rearrange("p (n i d) -> p n d i", d=PACK, i=4),
-                g4[c, a][:, :, lo:hi].rearrange("p d (n i) -> p n d i", i=4),
+                gb[a, first][:, PACK * (lo - first) : PACK * (hi - first)].rearrange("p (n i d) -> p n d i", d=PACK, i=4),
+                g4[a, lo][:].rearrange("p d (n i) -> p n d i", i=4),
             )
 
-        def quantise(c, a, lo, hi):
-            while lo < hi:
-                width = max(w for w in (512, 256, 128, 64) if lo + w <= hi)
-                nc.vector.quantize_mx(
-                    out=codes[c, a][:, lo : lo + width].bitcast(FP8X4),
-                    scales=scales[c, a][:, lo : lo + width],
-                    in_=gb[c, a][:, PACK * lo : PACK * (lo + width)],
-                )
-                lo += width
-
-        def multiply(copy, c, lo, hi):
-            bank = psum.tile([P, 512], F32, name=f"bank_{c}_{lo}")
+        def quantise(a, first, lo, hi):
+            words = keep.tile([P, hi - lo], U32, name=f"codes_{a}_{lo}", align_bytes=64)
+            plane = keep.tile([P, hi - lo], U8, name=f"scales_{a}_{lo}", align_bytes=64)
+            nc.vector.quantize_mx(
+                out=words[:].bitcast(FP8X4),
+                scales=plane[:],
+                in_=gb[a, first][:, PACK * (lo - first) : PACK * (hi - first)],
+            )
             for at in range(lo, hi, C):
-                e = (c * CHUNK + at) // C
-                for a in range(PASSES):
+                codes[a, at] = words[:, at - lo : at - lo + C]
+                scales[a, at] = plane[:, at - lo : at - lo + C]
+
+        banks = {}
+
+        def multiply(a, lo, hi, first):
+            if first not in banks:
+                banks[first] = psum.tile([P, 512], F32, name=f"bank_{first}")
+            for at in range(lo, hi, C):
+                e = at // C
+                for b in a:
                     nc.tensor.matmul_mx(
-                        out=bank[:, at - lo : at - lo + C],
-                        lhsT=w_sb[:, PASSES * e + a, :].bitcast(FP4X4),
-                        lhsT_scale=ws_sb[:, PASSES * e + a, :],
-                        rhs=codes[c, a][:, at : at + C].bitcast(FP8X4),
-                        rhs_scale=scales[c, a][:, at : at + C],
-                        start=(a == 0),
-                        stop=(a == PASSES - 1),
+                        out=banks[first][:, at - first : at - first + C],
+                        lhsT=w_sb[:, PASSES * e + b, :].bitcast(FP4X4),
+                        lhsT_scale=ws_sb[:, PASSES * e + b, :],
+                        rhs=codes[b, at].bitcast(FP8X4),
+                        rhs_scale=scales[b, at],
+                        start=(b == 0),
+                        stop=(b == PASSES - 1),
                     )
-            copy(dx[:, c * CHUNK + lo : c * CHUNK + hi], bank[:, 0 : hi - lo])
 
-        def finish(c, a, lo, hi):
-            quantise(c, a, lo, hi)
-            if a < PASSES - 1:
-                return
-            first, last = lo // C * C, hi // C * C
-            step = 512 if c == 0 else C
-            for at in range(first, last, step):
-                end = min(at + step, last)
-                multiply(nc.vector.tensor_copy if c * CHUNK + end == S else nc.scalar.copy, c, at, end)
+        def drain(copy, lo, hi):
+            copy(dx[:, lo:hi], banks[lo][:, 0 : hi - lo])
 
-        done = 0
-        for i, (c, a, lo, hi, lag) in enumerate(PIECES):
+        def gathers(a, lo, hi):
             for d in range(PACK):
-                if i + d == 0:
-                    gather(c, a, d, lo, HEAD)
-                    gather(c, a, d, HEAD, hi)
-                else:
-                    gather(c, a, d, lo, hi)
-            interleave(nc.vector.tensor_copy if i == len(PIECES) - 1 else nc.scalar.copy, c, a, lo, hi)
-            while done + PIECES[done][4] <= i:
-                finish(*PIECES[done][:4])
-                done += 1
-                if done == len(PIECES):
-                    break
+                gather(a, d, lo, hi, lo, hi)
+
+        gather(0, 0, 0, HEAD, 0, BIG)
+        gather(0, 0, HEAD, BIG, 0, BIG)
+        for d in range(1, PACK):
+            gather(0, d, 0, BIG, 0, BIG)
+        interleave(nc.scalar.copy, 0, 0, BIG, 0, BIG)
+        gathers(1, 0, BIG)
+        interleave(nc.scalar.copy, 1, 0, BIG, 0, BIG)
+        quantise(0, 0, 0, BIG)
+        gathers(0, BIG, S)
+        interleave(nc.scalar.copy, 0, BIG, S, BIG, S)
+        quantise(1, 0, 0, BIG)
+        for first in range(0, BIG, 512):
+            multiply((0, 1), first, first + 512, first)
+        gathers(1, BIG, S - 2 * C)
+        interleave(nc.scalar.copy, 1, BIG, S - 2 * C, BIG, S - 2 * C)
+        quantise(0, BIG, BIG, S)
+        for first in range(BIG, S, C):
+            multiply((0,), first, first + C, first)
+        gathers(1, S - 2 * C, S - C)
+        interleave(nc.scalar.copy, 1, S - 2 * C, S - C, S - 2 * C, S)
+        for first in range(0, BIG, 512):
+            drain(nc.scalar.copy, first, first + 512)
+        gathers(1, S - C, S)
+        quantise(1, BIG, BIG, S - 2 * C)
+        for first in range(BIG, S - 2 * C, C):
+            multiply((1,), first, first + C, first)
+            drain(nc.scalar.copy, first, first + C)
+        interleave(nc.vector.tensor_copy, 1, S - C, S, S - 2 * C, S)
+        quantise(1, S - 2 * C, S - 2 * C, S)
+        for first, copy in ((S - 2 * C, nc.scalar.copy), (S - C, nc.vector.tensor_copy)):
+            multiply((1,), first, first + C, first)
+            drain(copy, first, first + C)
 
         one = keep.tile([P, T], F32, name="one")
         both = keep.tile([P, T], F32, name="both")
-        nc.vector.tensor_copy(one[:], dx[:].indirect(pos1_sb[:]))
-        for lo, hi in ((0, 512), (512, T)):
-            nc.vector.tensor_tensor(
-                both[:, lo:hi], dx[:].indirect(pos2_sb[:, lo // 16 : hi // 16]), one[:, lo:hi], mybir.AluOpType.add
-            )
+        cuts = ((0, 512), (512, T))
+        for lo, hi in cuts:
+            nc.vector.tensor_copy(one[:, lo:hi], dx[:].indirect(pos1_sb[:, lo // 16 : hi // 16]))
+        for lo, hi in cuts:
+            nc.vector.tensor_tensor(both[:, lo:hi], dx[:].indirect(pos2_sb[:, lo // 16 : hi // 16]), one[:, lo:hi], ADD)
             nc.sync.dma_start(out=out[:, lo:hi], in_=both[:, lo:hi])

@@ -1,6 +1,7 @@
 from contextlib import ExitStack
 
 import concourse.mybir as mybir
+from concourse.masks import make_identity
 
 F32 = mybir.dt.float32
 BF16 = mybir.dt.bfloat16
@@ -12,6 +13,7 @@ FP8X4 = mybir.dt.float8_e4m3fn_x4
 FP4X4 = mybir.dt.float4_e2m1fn_x4
 MULT = mybir.AluOpType.mult
 ADD = mybir.AluOpType.add
+COPY = mybir.ActivationFunctionType.Copy
 
 P = 128
 K, T, E, C, N = 128, 768, 12, 128, 1024
@@ -23,7 +25,6 @@ FLOPS = 2 * N * K * S
 BYTES = 4 * N * T + E * N * K // 2 + E * N * K // 32 + 4 * S + 2 * P * (S + 2 * T) // 16 + 4 * K * T
 
 BIG = 1024
-HEAD = 384
 WIDE = 1040
 
 
@@ -34,6 +35,7 @@ def tile_moe_bdx_lin_none_kernel(tc, dyT, w_words, w_scales, gate, offs, pos1, p
         keep = ctx.enter_context(tc.tile_pool(name="keep", bufs=1))
         ring = ctx.enter_context(tc.tile_pool(name="ring", bufs=2))
         psum = ctx.enter_context(tc.psum_pool(name="psum", bufs=1))
+        psum2 = ctx.enter_context(tc.psum_pool(name="psum2", bufs=2))
 
         offs_sb = lists.tile([P, S // 16], U16, name="offs_sb")
         pos1_sb = lists.tile([P, T // 16], U16, name="pos1_sb")
@@ -51,15 +53,19 @@ def tile_moe_bdx_lin_none_kernel(tc, dyT, w_words, w_scales, gate, offs, pos1, p
         for plane in reversed([planes[a, d] for a in range(PASSES) for d in range(PACK)]):
             nc.vector.memset(plane[:, T:WIDE], 0.0)
 
+        ident = keep.tile([P, P], F32, name="ident")
+        make_identity(nc, ident[:])
+        gate_rows = keep.tile([P, C], F32, name="gate_rows")
+        nc.gpsimd.memset(gate_rows[:], 0.0)
+
         rows = dyT.rearrange("(a p d) t -> a d p t", a=PASSES, d=PACK)
         nc.sync.dma_start(offs_sb[:], offs)
-        nc.scalar.dma_start(out=gate_sb[:, 0:HEAD], in_=gate[0:P, 0:HEAD])
-        nc.sync.dma_start(out=planes[0, 0][:, 0:T], in_=rows[0, 0])
-        nc.sync.dma_start(out=gate_sb[:, HEAD:BIG], in_=gate[0:P, HEAD:BIG])
-        for a in range(PASSES):
-            for d in range(PACK):
-                if a + d > 0:
-                    nc.sync.dma_start(out=planes[a, d][:, 0:T], in_=rows[a, d])
+        for d in range(PACK):
+            nc.sync.dma_start(out=planes[0, d][:, 0:T], in_=rows[0, d])
+        nc.sync.dma_start(out=gate_rows[0 : BIG // C, :], in_=gate[0, 0:BIG].rearrange("(e s) -> e s", s=C))
+        nc.sync.dma_start(out=gate_sb[:, 0:BIG], in_=gate[0:P, 0:BIG])
+        for d in range(PACK):
+            nc.sync.dma_start(out=planes[1, d][:, 0:T], in_=rows[1, d])
         nc.sync.dma_start(out=gate_sb[:, BIG:S], in_=gate[0:P, BIG:S])
         nc.sync.dma_start(pos1_sb[:], pos1)
         nc.sync.dma_start(pos2_sb[:], pos2)
@@ -110,7 +116,12 @@ def tile_moe_bdx_lin_none_kernel(tc, dyT, w_words, w_scales, gate, offs, pos1, p
 
         def multiply(a, lo, hi, first):
             if first not in banks:
-                banks[first] = psum.tile([P, 512], F32, name=f"bank_{first}")
+                if first < BIG:
+                    banks[first] = psum.tile([P, 512], F32, name=f"bank_{first}")
+                elif first < S - 2 * C:
+                    banks[first] = psum2.tile([P, 512], F32, name="turn")
+                else:
+                    banks[first] = psum2.tile([P, 512], F32, name="back")
             for at in range(lo, hi, C):
                 e = at // C
                 for b in a:
@@ -131,11 +142,43 @@ def tile_moe_bdx_lin_none_kernel(tc, dyT, w_words, w_scales, gate, offs, pos1, p
             for d in range(PACK):
                 gather(a, d, lo, hi, lo, hi)
 
-        gather(0, 0, 0, HEAD, 0, BIG)
-        gather(0, 0, HEAD, BIG, 0, BIG)
-        for d in range(1, PACK):
-            gather(0, d, 0, BIG, 0, BIG)
-        interleave(nc.scalar.copy, 0, 0, BIG, 0, BIG)
+        gate_bank = psum.tile([P, 512], F32, name="gate_bank")
+        nc.tensor.transpose(gate_bank[:, 0:P], gate_rows[:], ident[:])
+        gate_cols = keep.tile([P, BIG // C], F32, name="gate_cols")
+        nc.scalar.copy(gate_cols[:], gate_bank[:, 0 : BIG // C])
+
+        def by_turns(a):
+            x4 = ring.tile([P, PACK, BIG], F32, name="g4")
+            gb[a, 0] = keep.tile([P, PACK * BIG], BF16, name=f"gb_{a}_{BIG}", align_bytes=64)
+            pairs = keep.tile([P, PACK * BIG], BF16, name="gb_1_0", align_bytes=64)
+            for u in range(2):
+                for d in (2 * u, 2 * u + 1):
+                    nc.vector.tensor_copy(x4[:, d, :], planes[a, d][:].indirect(offs_sb[:, 0 : BIG // 16]))
+                for e0 in range(0, BIG // C, 2):
+                    turn = psum2.tile([P, 2, 2, P], F32, name="turn")
+                    for b in range(2):
+                        for j in range(2):
+                            nc.tensor.transpose(turn[:, b, j, :], x4[:, 2 * u + j, (e0 + b) * C : (e0 + b + 1) * C], ident[:])
+                    for b in range(2):
+                        nc.scalar.activation(
+                            pairs[:, (2 * (e0 + b) + u) * 2 * P : (2 * (e0 + b) + u + 1) * 2 * P].rearrange("s (p j) -> s p j", j=2),
+                            turn[:, b, :, :].rearrange("s j p -> s p j"),
+                            COPY,
+                            scale=gate_cols[:, e0 + b : e0 + b + 1],
+                        )
+            gb_words = gb[a, 0][:].bitcast(F32)
+            for e0 in range(0, BIG // C, 2):
+                back = psum2.tile([P, 2, 2, C], F32, name="back")
+                for b in range(2):
+                    pair_words = pairs[:].bitcast(F32)[:, (e0 + b) * 2 * P : (e0 + b + 1) * 2 * P]
+                    for u in range(2):
+                        nc.tensor.transpose(back[:, b, u, :], pair_words[:, u * P : (u + 1) * P], ident[:])
+                nc.scalar.copy(
+                    gb_words[:, 2 * e0 * C : 2 * (e0 + 2) * C].rearrange("p (b s u) -> p b s u", b=2, u=2),
+                    back[:].rearrange("p b u s -> p b s u"),
+                )
+
+        by_turns(0)
         gathers(1, 0, BIG)
         interleave(nc.scalar.copy, 1, 0, BIG, 0, BIG)
         quantise(0, 0, 0, BIG)

@@ -50,17 +50,20 @@ def tile_moe_bdx_lin_none_kernel(tc, dyT, w_words, w_scales, gate, offs, pos1, p
                 planes[a, d] = keep.tile([P, WIDE], F32, name=f"dy_{a}_{d}")
         dx = keep.tile([P, S], F32, name="dx")
 
-        for plane in reversed([planes[a, d] for a in range(PASSES) for d in range(PACK)]):
-            nc.vector.memset(plane[:, T:WIDE], 0.0)
+        for d in reversed(range(PACK)):
+            nc.vector.memset(planes[0, d][:, T:WIDE], 0.0)
 
         ident = keep.tile([P, P], F32, name="ident")
         make_identity(nc, ident[:])
         gate_rows = keep.tile([P, C], F32, name="gate_rows")
         nc.gpsimd.memset(gate_rows[:], 0.0)
+        for d in reversed(range(PACK)):
+            nc.gpsimd.memset(planes[1, d][:, T:WIDE], 0.0)
 
         rows = dyT.rearrange("(a p d) t -> a d p t", a=PASSES, d=PACK)
+        nc.sync.dma_start(out=planes[0, 0][:, 0:T], in_=rows[0, 0])
         nc.sync.dma_start(offs_sb[:], offs)
-        for d in range(PACK):
+        for d in range(1, PACK):
             nc.sync.dma_start(out=planes[0, d][:, 0:T], in_=rows[0, d])
         nc.sync.dma_start(out=gate_rows[0 : BIG // C, :], in_=gate[0, 0:BIG].rearrange("(e s) -> e s", s=C))
         nc.sync.dma_start(out=gate_sb[:, 0:BIG], in_=gate[0:P, 0:BIG])
@@ -193,7 +196,7 @@ def tile_moe_bdx_lin_none_kernel(tc, dyT, w_words, w_scales, gate, offs, pos1, p
         for first in range(BIG, S, C):
             multiply((0,), first, first + C, first)
         gathers(1, S - 2 * C, S - C)
-        interleave(nc.scalar.copy, 1, S - 2 * C, S - C, S - 2 * C, S)
+        interleave(nc.scalar.copy, 1, S - 2 * C, S - C, S - 2 * C, S - C)
         for first in range(0, BIG, 512):
             drain(nc.scalar.copy, first, first + 512)
         gathers(1, S - C, S)
@@ -201,11 +204,13 @@ def tile_moe_bdx_lin_none_kernel(tc, dyT, w_words, w_scales, gate, offs, pos1, p
         for first in range(BIG, S - 2 * C, C):
             multiply((1,), first, first + C, first)
             drain(nc.scalar.copy, first, first + C)
-        interleave(nc.vector.tensor_copy, 1, S - C, S, S - 2 * C, S)
-        quantise(1, S - 2 * C, S - 2 * C, S)
-        for first, copy in ((S - 2 * C, nc.scalar.copy), (S - C, nc.vector.tensor_copy)):
-            multiply((1,), first, first + C, first)
-            drain(copy, first, first + C)
+        quantise(1, S - 2 * C, S - 2 * C, S - C)
+        multiply((1,), S - 2 * C, S - C, S - 2 * C)
+        drain(nc.scalar.copy, S - 2 * C, S - C)
+        interleave(nc.vector.tensor_copy, 1, S - C, S, S - C, S)
+        quantise(1, S - C, S - C, S)
+        multiply((1,), S - C, S, S - C)
+        drain(nc.scalar.copy, S - C, S)
 
         one = keep.tile([P, T], F32, name="one")
         both = keep.tile([P, T], F32, name="both")

@@ -58,7 +58,7 @@ def tile_moe_bdx_lin_none_kernel(tc, dyT, w_words, w_scales, gate, offs, pos1, p
         gate_rows = keep.tile([P, C], F32, name="gate_rows")
         nc.gpsimd.memset(gate_rows[:], 0.0)
         for d in reversed(range(PACK)):
-            nc.gpsimd.memset(planes[1, d][:, T:WIDE], 0.0)
+            nc.scalar.copy(planes[1, d][:, T:WIDE], planes[0, d][:, T:WIDE])
 
         rows = dyT.rearrange("(a p d) t -> a d p t", a=PASSES, d=PACK)
         nc.sync.dma_start(out=planes[0, 0][:, 0:T], in_=rows[0, 0])

@@ -25,7 +25,9 @@ FLOPS = 2 * N * K * S
 BYTES = 4 * N * T + E * N * K // 2 + E * N * K // 32 + 4 * S + 2 * P * (S + 2 * T) // 16 + 4 * K * T
 
 BIG = 1024
-WIDE = 1040
+LAST = S - C
+WIDE0 = 2048
+WIDE1 = 1040
 
 
 def tile_moe_bdx_lin_none_kernel(tc, dyT, w_words, w_scales, gate, offs, pos1, pos2, out):
@@ -33,7 +35,7 @@ def tile_moe_bdx_lin_none_kernel(tc, dyT, w_words, w_scales, gate, offs, pos1, p
     with ExitStack() as ctx:
         lists = ctx.enter_context(tc.tile_pool(name="lists", bufs=1))
         keep = ctx.enter_context(tc.tile_pool(name="keep", bufs=1))
-        ring = ctx.enter_context(tc.tile_pool(name="ring", bufs=2))
+        reuse = ctx.enter_context(tc.tile_pool(name="reuse", bufs=1))
         psum = ctx.enter_context(tc.psum_pool(name="psum", bufs=1))
         psum2 = ctx.enter_context(tc.psum_pool(name="psum2", bufs=2))
 
@@ -44,32 +46,32 @@ def tile_moe_bdx_lin_none_kernel(tc, dyT, w_words, w_scales, gate, offs, pos1, p
         w_sb = keep.tile([P, E * PASSES, 2 * K], U8, name="w_sb", align_bytes=64)
         ws_sb = keep.tile([P, E * PASSES, K], U8, name="ws_sb", align_bytes=64)
         gate_sb = keep.tile([P, S], F32, name="gate_sb")
-        planes = {}
-        for a in range(PASSES):
-            for d in range(PACK):
-                planes[a, d] = keep.tile([P, WIDE], F32, name=f"dy_{a}_{d}")
+        dy0 = keep.tile([P, (PACK - 1) * T + WIDE0], F32, name="dy0")
+        dy1 = [keep.tile([P, WIDE1], F32, name=f"dy1_{d}") for d in range(PACK)]
         dx = keep.tile([P, S], F32, name="dx")
 
-        for d in reversed(range(PACK)):
-            nc.vector.memset(planes[0, d][:, T:WIDE], 0.0)
+        def at0(d):
+            return (PACK - 1 - d) * T
 
+        nc.vector.memset(dy0[:, PACK * T :], 0.0)
         ident = keep.tile([P, P], F32, name="ident")
         make_identity(nc, ident[:])
         gate_rows = keep.tile([P, C], F32, name="gate_rows")
         nc.gpsimd.memset(gate_rows[:], 0.0)
         for d in reversed(range(PACK)):
-            nc.scalar.copy(planes[1, d][:, T:WIDE], planes[0, d][:, T:WIDE])
+            nc.scalar.copy(dy1[d][:, T:WIDE1], dy0[:, PACK * T : PACK * T + WIDE1 - T])
 
         rows = dyT.rearrange("(a p d) t -> a d p t", a=PASSES, d=PACK)
-        nc.sync.dma_start(out=planes[0, 0][:, 0:T], in_=rows[0, 0])
+        nc.sync.dma_start(out=dy0[:, at0(0) : at0(0) + T], in_=rows[0, 0])
         nc.sync.dma_start(offs_sb[:], offs)
         for d in range(1, PACK):
-            nc.sync.dma_start(out=planes[0, d][:, 0:T], in_=rows[0, d])
-        nc.sync.dma_start(out=gate_rows[0 : BIG // C, :], in_=gate[0, 0:BIG].rearrange("(e s) -> e s", s=C))
-        nc.sync.dma_start(out=gate_sb[:, 0:BIG], in_=gate[0:P, 0:BIG])
+            nc.sync.dma_start(out=dy0[:, at0(d) : at0(d) + T], in_=rows[0, d])
+        by_expert = gate[0, :].rearrange("(e s) -> e s", s=C)
+        nc.sync.dma_start(out=gate_rows[0:8, :], in_=by_expert[0:8])
+        nc.sync.dma_start(out=gate_rows[8:E, :], in_=by_expert[8:E])
+        nc.sync.dma_start(out=gate_sb[:], in_=gate[0:P, :])
         for d in range(PACK):
-            nc.sync.dma_start(out=planes[1, d][:, 0:T], in_=rows[1, d])
-        nc.sync.dma_start(out=gate_sb[:, BIG:S], in_=gate[0:P, BIG:S])
+            nc.sync.dma_start(out=dy1[d][:, 0:T], in_=rows[1, d])
         nc.sync.dma_start(pos1_sb[:], pos1)
         nc.sync.dma_start(pos2_sb[:], pos2)
         nc.vector.memset(ws_sb[:].rearrange("p g k -> p (g k)").bitcast(I32), 0)
@@ -83,134 +85,119 @@ def tile_moe_bdx_lin_none_kernel(tc, dyT, w_words, w_scales, gate, offs, pos1, p
             nc.sync.dma_start(out=ws_i32[32 * q : 32 * q + 4, :, :], in_=scale_rows[4 * q : 4 * q + 4, :, :])
         nc.sync.dma_start(out=w_i32[:, half:, :], in_=words[:, half:, :])
 
-        g4, gb, codes, scales = {}, {}, {}, {}
+        codes, scales, banks = {}, {}, {}
 
-        def gather(a, d, lo, hi, first, last):
-            if (a, first) not in g4:
-                g4[a, first] = ring.tile([P, PACK, last - first], F32, name="g4")
-            nc.vector.tensor_tensor(
-                g4[a, first][:, d, lo - first : hi - first],
-                planes[a, d][:].indirect(offs_sb[:, lo // 16 : hi // 16]),
-                gate_sb[:, lo:hi],
-                MULT,
-            )
-
-        def interleave(copy, a, lo, hi, first, last):
-            if (a, first) not in gb:
-                gb[a, first] = keep.tile([P, PACK * (last - first)], BF16, name=f"gb_{a}_{first}", align_bytes=64)
-            copy(
-                gb[a, first][:, PACK * (lo - first) : PACK * (hi - first)].rearrange("p (n i d) -> p n d i", d=PACK, i=4),
-                g4[a, lo][:].rearrange("p d (n i) -> p n d i", i=4),
-            )
-
-        def quantise(a, first, lo, hi):
-            words = keep.tile([P, hi - lo], U32, name=f"codes_{a}_{lo}", align_bytes=64)
-            plane = keep.tile([P, hi - lo], U8, name=f"scales_{a}_{lo}", align_bytes=64)
-            nc.vector.quantize_mx(
-                out=words[:].bitcast(FP8X4),
-                scales=plane[:],
-                in_=gb[a, first][:, PACK * (lo - first) : PACK * (hi - first)],
-            )
-            for at in range(lo, hi, C):
-                codes[a, at] = words[:, at - lo : at - lo + C]
-                scales[a, at] = plane[:, at - lo : at - lo + C]
-
-        banks = {}
-
-        def multiply(a, lo, hi, first):
-            if first not in banks:
-                if first < BIG:
-                    banks[first] = psum.tile([P, 512], F32, name=f"bank_{first}")
-                elif first < S - 2 * C:
-                    banks[first] = psum2.tile([P, 512], F32, name="turn")
-                else:
-                    banks[first] = psum2.tile([P, 512], F32, name="back")
-            for at in range(lo, hi, C):
-                e = at // C
-                for b in a:
-                    nc.tensor.matmul_mx(
-                        out=banks[first][:, at - first : at - first + C],
-                        lhsT=w_sb[:, PASSES * e + b, :].bitcast(FP4X4),
-                        lhsT_scale=ws_sb[:, PASSES * e + b, :],
-                        rhs=codes[b, at].bitcast(FP8X4),
-                        rhs_scale=scales[b, at],
-                        start=(b == 0),
-                        stop=(b == PASSES - 1),
-                    )
-
-        def drain(copy, lo, hi):
-            copy(dx[:, lo:hi], banks[lo][:, 0 : hi - lo])
-
-        def gathers(a, lo, hi):
+        def gathers(g4, lo, hi):
             for d in range(PACK):
-                gather(a, d, lo, hi, lo, hi)
+                nc.vector.tensor_tensor(
+                    g4[:, d, :], dy1[d][:].indirect(offs_sb[:, lo // 16 : hi // 16]), gate_sb[:, lo:hi], MULT
+                )
+
+        def interleave(copy, gb, g4):
+            copy(
+                gb.rearrange("p (n i d) -> p n d i", d=PACK, i=4),
+                g4.rearrange("p d (n i) -> p n d i", i=4),
+            )
+
+        def quantise(a, lo, hi, gb, made=None):
+            if made is None:
+                made = keep.tile([P, hi - lo], U32, name=f"codes_{a}_{lo}", align_bytes=64)
+            plane = keep.tile([P, hi - lo], U8, name=f"scales_{a}_{lo}", align_bytes=64)
+            nc.vector.quantize_mx(out=made[:].bitcast(FP8X4), scales=plane[:], in_=gb)
+            for at in range(lo, hi, C):
+                codes[a, at // C] = made[:, at - lo : at - lo + C]
+                scales[a, at // C] = plane[:, at - lo : at - lo + C]
+
+        def multiply(e, a, into):
+            nc.tensor.matmul_mx(
+                out=into,
+                lhsT=w_sb[:, PASSES * e + a, :].bitcast(FP4X4),
+                lhsT_scale=ws_sb[:, PASSES * e + a, :],
+                rhs=codes[a, e].bitcast(FP8X4),
+                rhs_scale=scales[a, e],
+                start=(a == 0),
+                stop=(a == PASSES - 1),
+            )
 
         gate_bank = psum.tile([P, 512], F32, name="gate_bank")
         nc.tensor.transpose(gate_bank[:, 0:P], gate_rows[:], ident[:])
-        gate_cols = keep.tile([P, BIG // C], F32, name="gate_cols")
-        nc.scalar.copy(gate_cols[:], gate_bank[:, 0 : BIG // C])
+        gate_cols = keep.tile([P, E], F32, name="gate_cols")
+        nc.scalar.copy(gate_cols[:], gate_bank[:, 0:E])
 
-        def by_turns(a):
-            x4 = ring.tile([P, PACK, BIG], F32, name="g4")
-            gb[a, 0] = keep.tile([P, PACK * BIG], BF16, name=f"gb_{a}_{BIG}", align_bytes=64)
-            pairs = keep.tile([P, PACK * BIG], BF16, name="gb_1_0", align_bytes=64)
-            for u in range(2):
-                for d in (2 * u, 2 * u + 1):
-                    nc.vector.tensor_copy(x4[:, d, :], planes[a, d][:].indirect(offs_sb[:, 0 : BIG // 16]))
-                for e0 in range(0, BIG // C, 2):
-                    turn = psum2.tile([P, 2, 2, P], F32, name="turn")
-                    for b in range(2):
-                        for j in range(2):
-                            nc.tensor.transpose(turn[:, b, j, :], x4[:, 2 * u + j, (e0 + b) * C : (e0 + b + 1) * C], ident[:])
-                    for b in range(2):
-                        nc.scalar.activation(
-                            pairs[:, (2 * (e0 + b) + u) * 2 * P : (2 * (e0 + b) + u + 1) * 2 * P].rearrange("s (p j) -> s p j", j=2),
-                            turn[:, b, :, :].rearrange("s j p -> s p j"),
-                            COPY,
-                            scale=gate_cols[:, e0 + b : e0 + b + 1],
-                        )
-            gb_words = gb[a, 0][:].bitcast(F32)
-            for e0 in range(0, BIG // C, 2):
-                back = psum2.tile([P, 2, 2, C], F32, name="back")
+        x4 = keep.tile([P, PACK, S], F32, name="x4")
+        gb0_big = keep.tile([P, PACK * BIG], BF16, name="gb0_big", align_bytes=64)
+        gb0_rest = keep.tile([P, PACK * (S - BIG)], BF16, name="gb0_rest", align_bytes=64)
+        pairs = keep.tile([P, PACK * S], BF16, name="pairs", align_bytes=64)
+        for u in range(2):
+            for d in (2 * u, 2 * u + 1):
+                nc.vector.tensor_copy(x4[:, d, :], dy0[:, at0(d) : at0(d) + WIDE0].indirect(offs_sb[:]))
+            for e0 in range(0, E, 2):
+                turn = psum2.tile([P, 2, 2, P], F32, name="turn")
                 for b in range(2):
-                    pair_words = pairs[:].bitcast(F32)[:, (e0 + b) * 2 * P : (e0 + b + 1) * 2 * P]
-                    for u in range(2):
-                        nc.tensor.transpose(back[:, b, u, :], pair_words[:, u * P : (u + 1) * P], ident[:])
-                nc.scalar.copy(
-                    gb_words[:, 2 * e0 * C : 2 * (e0 + 2) * C].rearrange("p (b s u) -> p b s u", b=2, u=2),
-                    back[:].rearrange("p b u s -> p b s u"),
-                )
+                    for j in range(2):
+                        nc.tensor.transpose(turn[:, b, j, :], x4[:, 2 * u + j, (e0 + b) * C : (e0 + b + 1) * C], ident[:])
+                for b in range(2):
+                    nc.scalar.activation(
+                        pairs[:, (2 * (e0 + b) + u) * 2 * P : (2 * (e0 + b) + u + 1) * 2 * P].rearrange("s (p j) -> s p j", j=2),
+                        turn[:, b, :, :].rearrange("s j p -> s p j"),
+                        COPY,
+                        scale=gate_cols[:, e0 + b : e0 + b + 1],
+                    )
+        for e0 in range(0, E, 2):
+            back = psum2.tile([P, 2, 2, C], F32, name="back")
+            for b in range(2):
+                pair_words = pairs[:].bitcast(F32)[:, (e0 + b) * 2 * P : (e0 + b + 1) * 2 * P]
+                for u in range(2):
+                    nc.tensor.transpose(back[:, b, u, :], pair_words[:, u * P : (u + 1) * P], ident[:])
+            if e0 * C < BIG:
+                into = gb0_big[:].bitcast(F32)[:, 2 * e0 * C : 2 * (e0 + 2) * C]
+            else:
+                into = gb0_rest[:].bitcast(F32)[:, 2 * (e0 * C - BIG) : 2 * ((e0 + 2) * C - BIG)]
+            nc.scalar.copy(into.rearrange("p (b s u) -> p b s u", b=2, u=2), back[:].rearrange("p b u s -> p b s u"))
 
-        by_turns(0)
-        gathers(1, 0, BIG)
-        interleave(nc.scalar.copy, 1, 0, BIG, 0, BIG)
-        quantise(0, 0, 0, BIG)
-        gathers(0, BIG, S)
-        interleave(nc.scalar.copy, 0, BIG, S, BIG, S)
-        quantise(1, 0, 0, BIG)
-        for first in range(0, BIG, 512):
-            multiply((0, 1), first, first + 512, first)
-        gathers(1, BIG, S - 2 * C)
-        interleave(nc.scalar.copy, 1, BIG, S - 2 * C, BIG, S - 2 * C)
-        quantise(0, BIG, BIG, S)
-        for first in range(BIG, S, C):
-            multiply((0,), first, first + C, first)
-        gathers(1, S - 2 * C, S - C)
-        interleave(nc.scalar.copy, 1, S - 2 * C, S - C, S - 2 * C, S - C)
-        for first in range(0, BIG, 512):
-            drain(nc.scalar.copy, first, first + 512)
-        gathers(1, S - C, S)
-        quantise(1, BIG, BIG, S - 2 * C)
-        for first in range(BIG, S - 2 * C, C):
-            multiply((1,), first, first + C, first)
-            drain(nc.scalar.copy, first, first + C)
-        quantise(1, S - 2 * C, S - 2 * C, S - C)
-        multiply((1,), S - 2 * C, S - C, S - 2 * C)
-        drain(nc.scalar.copy, S - 2 * C, S - C)
-        interleave(nc.vector.tensor_copy, 1, S - C, S, S - C, S)
-        quantise(1, S - C, S - C, S)
-        multiply((1,), S - C, S, S - C)
-        drain(nc.scalar.copy, S - C, S)
+        g_big = reuse.tile([P, PACK, BIG], F32, name="g_big", offset=0, align_bytes=64)
+        gathers(g_big, 0, BIG)
+        gb1_big = keep.tile([P, PACK * BIG], BF16, name="pairs", align_bytes=64)
+        for lo in (0, 512):
+            interleave(nc.scalar.copy, gb1_big[:, PACK * lo : PACK * (lo + 512)], g_big[:, :, lo : lo + 512])
+        g_mid = keep.tile([P, PACK, LAST - BIG], F32, name="g_mid", align_bytes=64)
+        gathers(g_mid, BIG, LAST)
+        quantise(0, 0, BIG, gb0_big[:])
+        gb1_mid = keep.tile([P, PACK * (LAST - BIG)], BF16, name="gb0_big", align_bytes=64)
+        interleave(nc.scalar.copy, gb1_mid[:, 0 : PACK * 2 * C], g_mid[:, :, 0 : 2 * C])
+        interleave(nc.scalar.copy, gb1_mid[:, PACK * 2 * C :], g_mid[:, :, 2 * C :])
+        for lo in (0, 512):
+            quantise(1, lo, lo + 512, gb1_big[:, PACK * lo : PACK * (lo + 512)])
+            banks[lo] = psum2.tile([P, 512], F32, name="back")
+            for e in range(lo // C, lo // C + 4):
+                for a in range(PASSES):
+                    multiply(e, a, banks[lo][:, e * C - lo : (e + 1) * C - lo])
+        codes_rest = reuse.tile([P, S - BIG], U32, name="codes_rest", offset=4 * PACK * C, align_bytes=64)
+        quantise(0, BIG, S, gb0_rest[:], codes_rest)
+        for e in range(BIG // C, E):
+            if e < BIG // C + 2:
+                banks[e * C] = psum2.tile([P, 512], F32, name="turn")
+            else:
+                banks[e * C] = psum.tile([P, 512], F32, name=f"bank_{e}")
+            multiply(e, 0, banks[e * C][:, 0:C])
+        g_last = reuse.tile([P, PACK, C], F32, name="g_last", offset=0, align_bytes=64)
+        gathers(g_last, LAST, S)
+        for lo in (0, 512):
+            nc.scalar.copy(dx[:, lo : lo + 512], banks[lo][:])
+
+        def finish(e):
+            multiply(e, 1, banks[e * C][:, 0:C])
+            nc.scalar.copy(dx[:, e * C : (e + 1) * C], banks[e * C][:, 0:C])
+
+        quantise(1, BIG, BIG + 2 * C, gb1_mid[:, 0 : PACK * 2 * C])
+        finish(8)
+        finish(9)
+        gb1_last = keep.tile([P, PACK * C], BF16, name="g_mid", align_bytes=64)
+        interleave(nc.vector.tensor_copy, gb1_last[:], g_last[:])
+        quantise(1, BIG + 2 * C, LAST, gb1_mid[:, PACK * 2 * C :])
+        finish(10)
+        quantise(1, LAST, S, gb1_last[:])
+        finish(11)
 
         one = keep.tile([P, T], F32, name="one")
         both = keep.tile([P, T], F32, name="both")

@@ -101,22 +101,22 @@ def tile_moe_bdx_lin_none_kernel(tc, dyT, w_words, w_scales, gate, offs, pos1, p
 
         def quantise(a, lo, hi, gb, made=None):
             if made is None:
-                made = keep.tile([P, hi - lo], U32, name=f"codes_{a}_{lo}", align_bytes=64)
+                made = keep.tile([P, hi - lo], U32, name=f"codes_{a}_{lo}", align_bytes=64)[:]
             plane = keep.tile([P, hi - lo], U8, name=f"scales_{a}_{lo}", align_bytes=64)
-            nc.vector.quantize_mx(out=made[:].bitcast(FP8X4), scales=plane[:], in_=gb)
+            nc.vector.quantize_mx(out=made.bitcast(FP8X4), scales=plane[:], in_=gb)
             for at in range(lo, hi, C):
                 codes[a, at // C] = made[:, at - lo : at - lo + C]
                 scales[a, at // C] = plane[:, at - lo : at - lo + C]
 
-        def multiply(e, a, into):
+        def multiply(e, a, into, first):
             nc.tensor.matmul_mx(
                 out=into,
                 lhsT=w_sb[:, PASSES * e + a, :].bitcast(FP4X4),
                 lhsT_scale=ws_sb[:, PASSES * e + a, :],
                 rhs=codes[a, e].bitcast(FP8X4),
                 rhs_scale=scales[a, e],
-                start=(a == 0),
-                stop=(a == PASSES - 1),
+                start=first,
+                stop=not first,
             )
 
         gate_bank = psum.tile([P, 512], F32, name="gate_bank")
@@ -171,33 +171,36 @@ def tile_moe_bdx_lin_none_kernel(tc, dyT, w_words, w_scales, gate, offs, pos1, p
             banks[lo] = psum2.tile([P, 512], F32, name="back")
             for e in range(lo // C, lo // C + 4):
                 for a in range(PASSES):
-                    multiply(e, a, banks[lo][:, e * C - lo : (e + 1) * C - lo])
-        codes_rest = reuse.tile([P, S - BIG], U32, name="codes_rest", offset=4 * PACK * C, align_bytes=64)
-        quantise(0, BIG, S, gb0_rest[:], codes_rest)
-        for e in range(BIG // C, E):
-            if e < BIG // C + 2:
-                banks[e * C] = psum2.tile([P, 512], F32, name="turn")
-            else:
-                banks[e * C] = psum.tile([P, 512], F32, name=f"bank_{e}")
-            multiply(e, 0, banks[e * C][:, 0:C])
+                    multiply(e, a, banks[lo][:, e * C - lo : (e + 1) * C - lo], a == 0)
         g_last = reuse.tile([P, PACK, C], F32, name="g_last", offset=0, align_bytes=64)
         gathers(g_last, LAST, S)
-        for lo in (0, 512):
-            nc.scalar.copy(dx[:, lo : lo + 512], banks[lo][:])
+        gb1_last = keep.tile([P, PACK * C], BF16, name="gb1_last", align_bytes=64)
+        nc.scalar.copy(dx[:, 0:512], banks[0][:])
+        interleave(nc.scalar.copy, gb1_last[:], g_last[:])
+        nc.scalar.copy(dx[:, 512:BIG], banks[512][:])
 
-        def finish(e):
-            multiply(e, 1, banks[e * C][:, 0:C])
+        def begin(e, a, pool, name):
+            banks[e * C] = pool.tile([P, 512], F32, name=name)
+            multiply(e, a, banks[e * C][:, 0:C], True)
+
+        def finish(e, a):
+            multiply(e, a, banks[e * C][:, 0:C], False)
             nc.scalar.copy(dx[:, e * C : (e + 1) * C], banks[e * C][:, 0:C])
 
         quantise(1, BIG, BIG + 2 * C, gb1_mid[:, 0 : PACK * 2 * C])
-        finish(8)
-        finish(9)
-        gb1_last = keep.tile([P, PACK * C], BF16, name="g_mid", align_bytes=64)
-        interleave(nc.vector.tensor_copy, gb1_last[:], g_last[:])
+        begin(8, 1, psum2, "turn")
+        begin(9, 1, psum2, "turn")
+        codes_late = keep.tile([P, S - BIG], U32, name="g_mid", align_bytes=64)
+        quantise(0, BIG, BIG + 2 * C, gb0_rest[:, 0 : PACK * 2 * C], codes_late[:, 0 : 2 * C])
+        finish(8, 0)
+        finish(9, 0)
+        quantise(0, BIG + 2 * C, S, gb0_rest[:, PACK * 2 * C :], codes_late[:, 2 * C :])
+        begin(10, 0, psum, "bank_10")
+        begin(11, 0, psum, "bank_11")
         quantise(1, BIG + 2 * C, LAST, gb1_mid[:, PACK * 2 * C :])
-        finish(10)
+        finish(10, 1)
         quantise(1, LAST, S, gb1_last[:])
-        finish(11)
+        finish(11, 1)
 
         one = keep.tile([P, T], F32, name="one")
         both = keep.tile([P, T], F32, name="both")

@@ -26,6 +26,7 @@ BYTES = 4 * N * T + E * N * K // 2 + E * N * K // 32 + 4 * S + 2 * P * (S + 2 * 
 
 BIG = 1024
 LAST = S - C
+WORDS = PACK * C
 WIDE0 = 2048
 WIDE1 = 1040
 
@@ -48,13 +49,12 @@ def tile_moe_bdx_lin_none_kernel(tc, dyT, w_words, w_scales, gate, offs, pos1, p
         gate_sb = keep.tile([P, S], F32, name="gate_sb")
         dy0 = keep.tile([P, (PACK - 1) * T + WIDE0], F32, name="dy0")
         dy1 = [keep.tile([P, WIDE1], F32, name=f"dy1_{d}") for d in range(PACK)]
-        dx = keep.tile([P, S], F32, name="dx")
 
         def at0(d):
             return (PACK - 1 - d) * T
 
         nc.vector.memset(dy0[:, PACK * T :], 0.0)
-        ident = keep.tile([P, P], F32, name="ident")
+        ident = keep.tile([P, P], F32, name="ident", align_bytes=64)
         make_identity(nc, ident[:])
         gate_rows = keep.tile([P, C], F32, name="gate_rows")
         nc.gpsimd.memset(gate_rows[:], 0.0)
@@ -87,26 +87,23 @@ def tile_moe_bdx_lin_none_kernel(tc, dyT, w_words, w_scales, gate, offs, pos1, p
 
         codes, scales, banks = {}, {}, {}
 
+        def gather(into, d, lo, hi):
+            nc.vector.tensor_tensor(into, dy1[d][:].indirect(offs_sb[:, lo // 16 : hi // 16]), gate_sb[:, lo:hi], MULT)
+
         def gathers(g4, lo, hi):
             for d in range(PACK):
-                nc.vector.tensor_tensor(
-                    g4[:, d, :], dy1[d][:].indirect(offs_sb[:, lo // 16 : hi // 16]), gate_sb[:, lo:hi], MULT
-                )
+                gather(g4[:, d, :], d, lo, hi)
 
-        def interleave(copy, gb, g4):
-            copy(
-                gb.rearrange("p (n i d) -> p n d i", d=PACK, i=4),
-                g4.rearrange("p d (n i) -> p n d i", i=4),
-            )
 
-        def quantise(a, lo, hi, gb, made=None):
+        def quantise(parts, values, made=None):
+            a0, e0 = parts[0]
             if made is None:
-                made = keep.tile([P, hi - lo], U32, name=f"codes_{a}_{lo}", align_bytes=64)[:]
-            plane = keep.tile([P, hi - lo], U8, name=f"scales_{a}_{lo}", align_bytes=64)
-            nc.vector.quantize_mx(out=made.bitcast(FP8X4), scales=plane[:], in_=gb)
-            for at in range(lo, hi, C):
-                codes[a, at // C] = made[:, at - lo : at - lo + C]
-                scales[a, at // C] = plane[:, at - lo : at - lo + C]
+                made = keep.tile([P, len(parts) * C], U32, name=f"codes_{a0}_{e0}", align_bytes=64)[:]
+            plane = keep.tile([P, len(parts) * C], U8, name=f"scales_{a0}_{e0}", align_bytes=64)
+            nc.vector.quantize_mx(out=made.bitcast(FP8X4), scales=plane[:], in_=values)
+            for i, part in enumerate(parts):
+                codes[part] = made[:, i * C : (i + 1) * C]
+                scales[part] = plane[:, i * C : (i + 1) * C]
 
         def multiply(e, a, into, first):
             nc.tensor.matmul_mx(
@@ -125,9 +122,18 @@ def tile_moe_bdx_lin_none_kernel(tc, dyT, w_words, w_scales, gate, offs, pos1, p
         nc.scalar.copy(gate_cols[:], gate_bank[:, 0:E])
 
         x4 = keep.tile([P, PACK, S], F32, name="x4")
-        gb0_big = keep.tile([P, PACK * BIG], BF16, name="gb0_big", align_bytes=64)
-        gb0_rest = keep.tile([P, PACK * (S - BIG)], BF16, name="gb0_rest", align_bytes=64)
-        pairs = keep.tile([P, PACK * S], BF16, name="pairs", align_bytes=64)
+        gb = keep.tile([P, E * PASSES * WORDS], BF16, name="gb", align_bytes=64)
+        by_part = gb[:].rearrange("p (e a c) -> p e a c", e=E, a=PASSES)
+        early_pairs = keep.tile([P, 4 * WORDS], BF16, name="early_pairs", align_bytes=64)
+
+        def pairs(e, u):
+            if e < 4:
+                return early_pairs[:, (2 * e + u) * 2 * P : (2 * e + u + 1) * 2 * P]
+            if e < 8:
+                return by_part[:, 2 * (e - 2), 1, u * 2 * P : (u + 1) * 2 * P]
+            half, place = divmod(2 * (e - 8) + u, 4)
+            return by_part[:, 3 + 2 * place, 1, half * 2 * P : (half + 1) * 2 * P]
+
         for u in range(2):
             for d in (2 * u, 2 * u + 1):
                 nc.vector.tensor_copy(x4[:, d, :], dy0[:, at0(d) : at0(d) + WIDE0].indirect(offs_sb[:]))
@@ -138,69 +144,78 @@ def tile_moe_bdx_lin_none_kernel(tc, dyT, w_words, w_scales, gate, offs, pos1, p
                         nc.tensor.transpose(turn[:, b, j, :], x4[:, 2 * u + j, (e0 + b) * C : (e0 + b + 1) * C], ident[:])
                 for b in range(2):
                     nc.scalar.activation(
-                        pairs[:, (2 * (e0 + b) + u) * 2 * P : (2 * (e0 + b) + u + 1) * 2 * P].rearrange("s (p j) -> s p j", j=2),
+                        pairs(e0 + b, u).rearrange("s (p j) -> s p j", j=2),
                         turn[:, b, :, :].rearrange("s j p -> s p j"),
                         COPY,
                         scale=gate_cols[:, e0 + b : e0 + b + 1],
                     )
         for e0 in range(0, E, 2):
-            back = psum2.tile([P, 2, 2, C], F32, name="back")
+            back = psum2.tile([P, 2, 2, C], F32, name="turn" if e0 // 4 == 1 else "back")
             for b in range(2):
-                pair_words = pairs[:].bitcast(F32)[:, (e0 + b) * 2 * P : (e0 + b + 1) * 2 * P]
                 for u in range(2):
-                    nc.tensor.transpose(back[:, b, u, :], pair_words[:, u * P : (u + 1) * P], ident[:])
-            if e0 * C < BIG:
-                into = gb0_big[:].bitcast(F32)[:, 2 * e0 * C : 2 * (e0 + 2) * C]
-            else:
-                into = gb0_rest[:].bitcast(F32)[:, 2 * (e0 * C - BIG) : 2 * ((e0 + 2) * C - BIG)]
-            nc.scalar.copy(into.rearrange("p (b s u) -> p b s u", b=2, u=2), back[:].rearrange("p b u s -> p b s u"))
+                    nc.tensor.transpose(back[:, b, u, :], pairs(e0 + b, u).bitcast(F32), ident[:])
+            into = gb[:].bitcast(F32).rearrange("p (e a s u) -> p e a s u", e=E, a=PASSES, u=2)[:, e0 : e0 + 2, 0]
+            nc.scalar.copy(into, back[:].rearrange("p b u s -> p b s u"))
 
-        g_big = reuse.tile([P, PACK, BIG], F32, name="g_big", offset=0, align_bytes=64)
-        gathers(g_big, 0, BIG)
-        gb1_big = keep.tile([P, PACK * BIG], BF16, name="pairs", align_bytes=64)
-        for lo in (0, 512):
-            interleave(nc.scalar.copy, gb1_big[:, PACK * lo : PACK * (lo + 512)], g_big[:, :, lo : lo + 512])
+        g_big = reuse.tile([P, PACK, BIG], F32, name="g_big")
+        for d in range(PACK - 1):
+            gather(g_big[:, d, :], d, 0, BIG)
+        for h in range(2):
+            gather(g_big[:, PACK - 1, 512 * h : 512 * (h + 1)], PACK - 1, 512 * h, 512 * (h + 1))
+
+        def interleave(first, last, g4):
+            nc.scalar.copy(
+                by_part[:, first:last, 1, :].rearrange("p e (n i d) -> p e n d i", d=PACK, i=4),
+                g4.rearrange("p d (e n i) -> p e n d i", e=last - first, i=4),
+            )
+
+        def both_passes(first, last):
+            quantise(
+                [(a, e) for e in range(first, last) for a in range(PASSES)],
+                gb[:, first * PASSES * WORDS : last * PASSES * WORDS],
+            )
+
+        def products(bank, at, first, last):
+            for e in range(first, last):
+                for a in range(PASSES):
+                    multiply(e, a, bank[:, (e - at) * C : (e - at + 1) * C], a == 0)
+
+        for h in range(2):
+            interleave(4 * h, 4 * h + 4, g_big[:, :, 512 * h : 512 * (h + 1)])
         g_mid = keep.tile([P, PACK, LAST - BIG], F32, name="g_mid", align_bytes=64)
         gathers(g_mid, BIG, LAST)
-        quantise(0, 0, BIG, gb0_big[:])
-        gb1_mid = keep.tile([P, PACK * (LAST - BIG)], BF16, name="gb0_big", align_bytes=64)
-        interleave(nc.scalar.copy, gb1_mid[:, 0 : PACK * 2 * C], g_mid[:, :, 0 : 2 * C])
-        interleave(nc.scalar.copy, gb1_mid[:, PACK * 2 * C :], g_mid[:, :, 2 * C :])
-        for lo in (0, 512):
-            quantise(1, lo, lo + 512, gb1_big[:, PACK * lo : PACK * (lo + 512)])
-            banks[lo] = psum2.tile([P, 512], F32, name="back")
-            for e in range(lo // C, lo // C + 4):
-                for a in range(PASSES):
-                    multiply(e, a, banks[lo][:, e * C - lo : (e + 1) * C - lo], a == 0)
-        g_last = reuse.tile([P, PACK, C], F32, name="g_last", offset=0, align_bytes=64)
+        interleave(8, 11, g_mid[:])
+        for first, last in ((0, 4), (4, 6)):
+            both_passes(first, last)
+            banks[first] = psum2.tile([P, 512], F32, name="back")
+            products(banks[first], first, first, last)
+        dx = reuse.tile([P, S], F32, name="g_big")
+        g_last = dx[:, BIG:S].rearrange("p (d s) -> p d s", d=PACK)
         gathers(g_last, LAST, S)
-        gb1_last = keep.tile([P, PACK * C], BF16, name="gb1_last", align_bytes=64)
-        nc.scalar.copy(dx[:, 0:512], banks[0][:])
-        interleave(nc.scalar.copy, gb1_last[:], g_last[:])
-        nc.scalar.copy(dx[:, 512:BIG], banks[512][:])
 
-        def begin(e, a, pool, name):
-            banks[e * C] = pool.tile([P, 512], F32, name=name)
-            multiply(e, a, banks[e * C][:, 0:C], True)
+        def drain(first, last):
+            nc.scalar.copy(dx[:, first * C : last * C], banks[first][:, 0 : (last - first) * C])
 
-        def finish(e, a):
-            multiply(e, a, banks[e * C][:, 0:C], False)
-            nc.scalar.copy(dx[:, e * C : (e + 1) * C], banks[e * C][:, 0:C])
-
-        quantise(1, BIG, BIG + 2 * C, gb1_mid[:, 0 : PACK * 2 * C])
-        begin(8, 1, psum2, "turn")
-        begin(9, 1, psum2, "turn")
-        codes_late = keep.tile([P, S - BIG], U32, name="g_mid", align_bytes=64)
-        quantise(0, BIG, BIG + 2 * C, gb0_rest[:, 0 : PACK * 2 * C], codes_late[:, 0 : 2 * C])
-        finish(8, 0)
-        finish(9, 0)
-        quantise(0, BIG + 2 * C, S, gb0_rest[:, PACK * 2 * C :], codes_late[:, 2 * C :])
-        begin(10, 0, psum, "bank_10")
-        begin(11, 0, psum, "bank_11")
-        quantise(1, BIG + 2 * C, LAST, gb1_mid[:, PACK * 2 * C :])
-        finish(10, 1)
-        quantise(1, LAST, S, gb1_last[:])
-        finish(11, 1)
+        drain(0, 4)
+        drain(4, 6)
+        interleave(11, 12, g_last)
+        for first in (6, 8):
+            banks[first] = psum2.tile([P, 512], F32, name="turn")
+            for e in (first, first + 1):
+                both_passes(e, e + 1)
+                products(banks[first], first, e, e + 1)
+            drain(first, first + 2)
+        banks[10] = psum.tile([P, 512], F32, name="bank_10")
+        both_passes(10, 11)
+        products(banks[10], 10, 10, 11)
+        drain(10, 11)
+        banks[11] = psum.tile([P, 512], F32, name="gate_bank")
+        codes_late = keep.tile([P, C], U32, name="g_mid", align_bytes=64)
+        quantise([(0, 11)], by_part[:, 11, 0, :], codes_late[:])
+        multiply(11, 0, banks[11][:, 0:C], True)
+        quantise([(1, 11)], by_part[:, 11, 1, :])
+        multiply(11, 1, banks[11][:, 0:C], False)
+        drain(11, 12)
 
         one = keep.tile([P, T], F32, name="one")
         both = keep.tile([P, T], F32, name="both")

@@ -36,7 +36,6 @@ def tile_moe_bdx_lin_none_kernel(tc, dyT, w_words, w_scales, gate, offs, pos1, p
     with ExitStack() as ctx:
         lists = ctx.enter_context(tc.tile_pool(name="lists", bufs=1))
         keep = ctx.enter_context(tc.tile_pool(name="keep", bufs=1))
-        reuse = ctx.enter_context(tc.tile_pool(name="reuse", bufs=1))
         psum = ctx.enter_context(tc.psum_pool(name="psum", bufs=1))
         psum2 = ctx.enter_context(tc.psum_pool(name="psum2", bufs=2))
 
@@ -85,7 +84,7 @@ def tile_moe_bdx_lin_none_kernel(tc, dyT, w_words, w_scales, gate, offs, pos1, p
             nc.sync.dma_start(out=ws_i32[32 * q : 32 * q + 4, :, :], in_=scale_rows[4 * q : 4 * q + 4, :, :])
         nc.sync.dma_start(out=w_i32[:, half:, :], in_=words[:, half:, :])
 
-        codes, scales, banks = {}, {}, {}
+        codes, scales, banks, whole = {}, {}, {}, {}
 
         def gather(into, d, lo, hi):
             nc.vector.tensor_tensor(into, dy1[d][:].indirect(offs_sb[:, lo // 16 : hi // 16]), gate_sb[:, lo:hi], MULT)
@@ -101,6 +100,7 @@ def tile_moe_bdx_lin_none_kernel(tc, dyT, w_words, w_scales, gate, offs, pos1, p
                 made = keep.tile([P, len(parts) * C], U32, name=f"codes_{a0}_{e0}", align_bytes=64)[:]
             plane = keep.tile([P, len(parts) * C], U8, name=f"scales_{a0}_{e0}", align_bytes=64)
             nc.vector.quantize_mx(out=made.bitcast(FP8X4), scales=plane[:], in_=values)
+            whole[a0, e0] = (made, plane[:])
             for i, part in enumerate(parts):
                 codes[part] = made[:, i * C : (i + 1) * C]
                 scales[part] = plane[:, i * C : (i + 1) * C]
@@ -124,19 +124,17 @@ def tile_moe_bdx_lin_none_kernel(tc, dyT, w_words, w_scales, gate, offs, pos1, p
         x4 = keep.tile([P, PACK, S], F32, name="x4")
         gb = keep.tile([P, E * PASSES * WORDS], BF16, name="gb", align_bytes=64)
         by_part = gb[:].rearrange("p (e a c) -> p e a c", e=E, a=PASSES)
-        early_pairs = keep.tile([P, 4 * WORDS], BF16, name="early_pairs", align_bytes=64)
+        pair_tile = keep.tile([P, E * WORDS], BF16, name="pair_tile", align_bytes=64)
 
         def pairs(e, u):
-            if e < 4:
-                return early_pairs[:, (2 * e + u) * 2 * P : (2 * e + u + 1) * 2 * P]
-            if e < 8:
-                return by_part[:, 2 * (e - 2), 1, u * 2 * P : (u + 1) * 2 * P]
-            half, place = divmod(2 * (e - 8) + u, 4)
-            return by_part[:, 3 + 2 * place, 1, half * 2 * P : (half + 1) * 2 * P]
+            return pair_tile[:, (2 * e + u) * 2 * P : (2 * e + u + 1) * 2 * P]
 
         for u in range(2):
             for d in (2 * u, 2 * u + 1):
-                nc.vector.tensor_copy(x4[:, d, :], dy0[:, at0(d) : at0(d) + WIDE0].indirect(offs_sb[:]))
+                for lo, hi in ((0, S),) if d < PACK - 1 else ((0, S // 2), (S // 2, S)):
+                    nc.vector.tensor_copy(
+                        x4[:, d, lo:hi], dy0[:, at0(d) : at0(d) + WIDE0].indirect(offs_sb[:, lo // 16 : hi // 16])
+                    )
             for e0 in range(0, E, 2):
                 turn = psum2.tile([P, 2, 2, P], F32, name="turn")
                 for b in range(2):
@@ -149,19 +147,20 @@ def tile_moe_bdx_lin_none_kernel(tc, dyT, w_words, w_scales, gate, offs, pos1, p
                         COPY,
                         scale=gate_cols[:, e0 + b : e0 + b + 1],
                     )
-        for e0 in range(0, E, 2):
-            back = psum2.tile([P, 2, 2, C], F32, name="turn" if e0 // 4 == 1 else "back")
+        pass0_words = gb[:].bitcast(F32).rearrange("p (b e a s u) -> p e a b s u", b=2, e=E // 2, a=PASSES, u=2)
+        for step in range(E // 2):
+            e0 = (step + 4) % (E // 2)
+            back = psum2.tile([P, 2, 2, C], F32, name="turn" if step // 2 == 1 else "back")
             for b in range(2):
                 for u in range(2):
-                    nc.tensor.transpose(back[:, b, u, :], pairs(e0 + b, u).bitcast(F32), ident[:])
-            into = gb[:].bitcast(F32).rearrange("p (e a s u) -> p e a s u", e=E, a=PASSES, u=2)[:, e0 : e0 + 2, 0]
-            nc.scalar.copy(into, back[:].rearrange("p b u s -> p b s u"))
+                    nc.tensor.transpose(back[:, b, u, :], pairs(e0 + b * E // 2, u).bitcast(F32), ident[:])
+            nc.scalar.copy(pass0_words[:, e0, 0], back[:].rearrange("p b u s -> p b s u"))
 
-        g_big = reuse.tile([P, PACK, BIG], F32, name="g_big")
-        for d in range(PACK - 1):
-            gather(g_big[:, d, :], d, 0, BIG)
-        for h in range(2):
-            gather(g_big[:, PACK - 1, 512 * h : 512 * (h + 1)], PACK - 1, 512 * h, 512 * (h + 1))
+        g = keep.tile([P, 3 * 512 + PACK * BIG], F32, name="g")
+        g_big = g[:, 3 * 512 :].rearrange("p (d s) -> p d s", d=PACK)
+        g_mid = g[:, 0 : PACK * 512].rearrange("p (d s) -> p d s", d=PACK)[:, :, 0 : LAST - BIG]
+        g_last = g[:, 2 * 512 + PACK * BIG :].rearrange("p (d s) -> p d s", d=PACK)
+        dx = keep.tile([P, S], F32, name="dx")
 
         def interleave(first, last, g4):
             nc.scalar.copy(
@@ -180,27 +179,52 @@ def tile_moe_bdx_lin_none_kernel(tc, dyT, w_words, w_scales, gate, offs, pos1, p
                 for a in range(PASSES):
                     multiply(e, a, bank[:, (e - at) * C : (e - at + 1) * C], a == 0)
 
-        for h in range(2):
-            interleave(4 * h, 4 * h + 4, g_big[:, :, 512 * h : 512 * (h + 1)])
-        g_mid = keep.tile([P, PACK, LAST - BIG], F32, name="g_mid", align_bytes=64)
-        gathers(g_mid, BIG, LAST)
-        interleave(8, 11, g_mid[:])
-        for first, last in ((0, 4), (4, 6)):
-            both_passes(first, last)
-            banks[first] = psum2.tile([P, 512], F32, name="back")
-            products(banks[first], first, first, last)
-        dx = reuse.tile([P, S], F32, name="g_big")
-        g_last = dx[:, BIG:S].rearrange("p (d s) -> p d s", d=PACK)
-        gathers(g_last, LAST, S)
+        def two_experts(first, pool, name):
+            banks[first] = pool.tile([P, 512], F32, name=name)
+            products(banks[first], first, first, first + 2)
+
+        warm = psum.tile([P, 512], F32, name="warm")
+
+        def warm_up(e, width):
+            nc.tensor.matmul_mx(
+                out=warm[:, 0:width],
+                lhsT=w_sb[:, 0, :].bitcast(FP4X4),
+                lhsT_scale=ws_sb[:, 0, :],
+                rhs=whole[0, e][0][:, 0:width].bitcast(FP8X4),
+                rhs_scale=whole[0, e][1][:, 0:width],
+                start=True,
+                stop=True,
+            )
 
         def drain(first, last):
             nc.scalar.copy(dx[:, first * C : last * C], banks[first][:, 0 : (last - first) * C])
 
-        drain(0, 4)
-        drain(4, 6)
+        quantise([(0, 11)], by_part[:, 11, 0, :])
+        banks[11] = psum.tile([P, 512], F32, name="gate_bank")
+        multiply(11, 0, banks[11][:, 0:C], True)
+        for d in range(PACK - 1):
+            gather(g_big[:, d, :], d, 0, BIG)
+        for h in range(2):
+            gather(g_big[:, PACK - 1, 512 * h : 512 * (h + 1)], PACK - 1, 512 * h, 512 * (h + 1))
+        for h in range(2):
+            interleave(4 * h, 4 * h + 4, g_big[:, :, 512 * h : 512 * (h + 1)])
+        for d in range(PACK - 1):
+            gather(g_mid[:, d, :], d, BIG, LAST)
+        both_passes(0, 2)
+        two_experts(0, psum2, "back")
+        drain(0, 2)
+        warm_up(0, 4 * C)
+        gather(g_mid[:, PACK - 1, :], PACK - 1, BIG, LAST)
+        interleave(8, 11, g_mid)
+        for first, name in ((2, "back"), (4, "turn")):
+            both_passes(first, first + 2)
+            two_experts(first, psum2, name)
+            drain(first, first + 2)
+        warm_up(4, 2 * C)
+        gathers(g_last, LAST, S)
         interleave(11, 12, g_last)
-        for first in (6, 8):
-            banks[first] = psum2.tile([P, 512], F32, name="turn")
+        for first, pool, name in ((6, psum2, "turn"), (8, psum, "bank_8")):
+            banks[first] = pool.tile([P, 512], F32, name=name)
             for e in (first, first + 1):
                 both_passes(e, e + 1)
                 products(banks[first], first, e, e + 1)
@@ -209,10 +233,6 @@ def tile_moe_bdx_lin_none_kernel(tc, dyT, w_words, w_scales, gate, offs, pos1, p
         both_passes(10, 11)
         products(banks[10], 10, 10, 11)
         drain(10, 11)
-        banks[11] = psum.tile([P, 512], F32, name="gate_bank")
-        codes_late = keep.tile([P, C], U32, name="g_mid", align_bytes=64)
-        quantise([(0, 11)], by_part[:, 11, 0, :], codes_late[:])
-        multiply(11, 0, banks[11][:, 0:C], True)
         quantise([(1, 11)], by_part[:, 11, 1, :])
         multiply(11, 1, banks[11][:, 0:C], False)
         drain(11, 12)

@@ -61,8 +61,9 @@ def tile_moe_bdx_lin_none_kernel(tc, dyT, w_words, w_scales, gate, offs, pos1, p
             nc.scalar.copy(dy1[d][:, T:WIDE1], dy0[:, PACK * T : PACK * T + WIDE1 - T])
 
         rows = dyT.rearrange("(a p d) t -> a d p t", a=PASSES, d=PACK)
-        nc.sync.dma_start(out=dy0[:, at0(0) : at0(0) + T], in_=rows[0, 0])
         nc.sync.dma_start(offs_sb[:], offs)
+        nc.sync.dma_start(out=dy0[:, at0(0) : at0(0) + T // 2], in_=rows[0, 0][:, 0 : T // 2])
+        nc.scalar.dma_start(out=dy0[:, at0(0) + T // 2 : at0(0) + T], in_=rows[0, 0][:, T // 2 :])
         for d in range(1, PACK):
             nc.sync.dma_start(out=dy0[:, at0(d) : at0(d) + T], in_=rows[0, d])
         by_expert = gate[0, :].rearrange("(e s) -> e s", s=C)
@@ -88,11 +89,6 @@ def tile_moe_bdx_lin_none_kernel(tc, dyT, w_words, w_scales, gate, offs, pos1, p
 
         def gather(into, d, lo, hi):
             nc.vector.tensor_tensor(into, dy1[d][:].indirect(offs_sb[:, lo // 16 : hi // 16]), gate_sb[:, lo:hi], MULT)
-
-        def gathers(g4, lo, hi):
-            for d in range(PACK):
-                gather(g4[:, d, :], d, lo, hi)
-
 
         def quantise(parts, values, made=None):
             a0, e0 = parts[0]
@@ -216,19 +212,26 @@ def tile_moe_bdx_lin_none_kernel(tc, dyT, w_words, w_scales, gate, offs, pos1, p
         warm_up(0, 4 * C)
         gather(g_mid[:, PACK - 1, :], PACK - 1, BIG, LAST)
         interleave(8, 11, g_mid)
-        for first, name in ((2, "back"), (4, "turn")):
-            both_passes(first, first + 2)
-            two_experts(first, psum2, name)
-            drain(first, first + 2)
+        both_passes(2, 4)
+        two_experts(2, psum2, "back")
+        drain(2, 4)
+        both_passes(4, 6)
+        two_experts(4, psum2, "turn")
+        both_passes(6, 7)
+        products(banks[4], 4, 6, 7)
         warm_up(4, 2 * C)
-        gathers(g_last, LAST, S)
-        interleave(11, 12, g_last)
-        for first, pool, name in ((6, psum2, "turn"), (8, psum, "bank_8")):
+        last_words = by_part[:, E - 1, 1, :].rearrange("p (s u j) -> p u s j", u=2, j=2)
+        for u in range(2):
+            for d in (2 * u, 2 * u + 1):
+                gather(g_last[:, d, :], d, LAST, S)
+            nc.scalar.copy(last_words[:, u], g_last[:, 2 * u : 2 * u + 2, :].rearrange("p j s -> p s j"))
+        drain(4, 7)
+        for first, last, pool, name in ((7, 8, psum2, "turn"), (8, 10, psum, "bank_8")):
             banks[first] = pool.tile([P, 512], F32, name=name)
-            for e in (first, first + 1):
+            for e in range(first, last):
                 both_passes(e, e + 1)
                 products(banks[first], first, e, e + 1)
-            drain(first, first + 2)
+            drain(first, last)
         banks[10] = psum.tile([P, 512], F32, name="bank_10")
         both_passes(10, 11)
         products(banks[10], 10, 10, 11)

@@ -61,9 +61,8 @@ def tile_moe_bdx_lin_none_kernel(tc, dyT, w_words, w_scales, gate, offs, pos1, p
             nc.scalar.copy(dy1[d][:, T:WIDE1], dy0[:, PACK * T : PACK * T + WIDE1 - T])
 
         rows = dyT.rearrange("(a p d) t -> a d p t", a=PASSES, d=PACK)
+        nc.sync.dma_start(out=dy0[:, at0(0) : at0(0) + T], in_=rows[0, 0])
         nc.sync.dma_start(offs_sb[:], offs)
-        nc.sync.dma_start(out=dy0[:, at0(0) : at0(0) + T // 2], in_=rows[0, 0][:, 0 : T // 2])
-        nc.scalar.dma_start(out=dy0[:, at0(0) + T // 2 : at0(0) + T], in_=rows[0, 0][:, T // 2 :])
         for d in range(1, PACK):
             nc.sync.dma_start(out=dy0[:, at0(d) : at0(d) + T], in_=rows[0, d])
         by_expert = gate[0, :].rearrange("(e s) -> e s", s=C)
@@ -132,7 +131,7 @@ def tile_moe_bdx_lin_none_kernel(tc, dyT, w_words, w_scales, gate, offs, pos1, p
                         x4[:, d, lo:hi], dy0[:, at0(d) : at0(d) + WIDE0].indirect(offs_sb[:, lo // 16 : hi // 16])
                     )
             for e0 in range(0, E, 2):
-                turn = psum2.tile([P, 2, 2, P], F32, name="turn")
+                turn = psum2.tile([P, 2, 2, P], F32, name="turn" if (u * E + e0) % 8 < 4 else "back")
                 for b in range(2):
                     for j in range(2):
                         nc.tensor.transpose(turn[:, b, j, :], x4[:, 2 * u + j, (e0 + b) * C : (e0 + b + 1) * C], ident[:])
@@ -146,7 +145,7 @@ def tile_moe_bdx_lin_none_kernel(tc, dyT, w_words, w_scales, gate, offs, pos1, p
         pass0_words = gb[:].bitcast(F32).rearrange("p (b e a s u) -> p e a b s u", b=2, e=E // 2, a=PASSES, u=2)
         for step in range(E // 2):
             e0 = (step + 4) % (E // 2)
-            back = psum2.tile([P, 2, 2, C], F32, name="turn" if step // 2 == 1 else "back")
+            back = psum2.tile([P, 2, 2, C], F32, name="back" if step // 2 == 1 else "turn")
             for b in range(2):
                 for u in range(2):
                     nc.tensor.transpose(back[:, b, u, :], pairs(e0 + b * E // 2, u).bitcast(F32), ident[:])
@@ -195,9 +194,6 @@ def tile_moe_bdx_lin_none_kernel(tc, dyT, w_words, w_scales, gate, offs, pos1, p
         def drain(first, last):
             nc.scalar.copy(dx[:, first * C : last * C], banks[first][:, 0 : (last - first) * C])
 
-        quantise([(0, 11)], by_part[:, 11, 0, :])
-        banks[11] = psum.tile([P, 512], F32, name="gate_bank")
-        multiply(11, 0, banks[11][:, 0:C], True)
         for d in range(PACK - 1):
             gather(g_big[:, d, :], d, 0, BIG)
         for h in range(2):
@@ -217,21 +213,24 @@ def tile_moe_bdx_lin_none_kernel(tc, dyT, w_words, w_scales, gate, offs, pos1, p
         drain(2, 4)
         both_passes(4, 6)
         two_experts(4, psum2, "turn")
-        both_passes(6, 7)
-        products(banks[4], 4, 6, 7)
-        warm_up(4, 2 * C)
+        drain(4, 6)
+        both_passes(6, 8)
+        two_experts(6, psum2, "turn")
+        warm_up(6, 2 * C)
         last_words = by_part[:, E - 1, 1, :].rearrange("p (s u j) -> p u s j", u=2, j=2)
         for u in range(2):
             for d in (2 * u, 2 * u + 1):
                 gather(g_last[:, d, :], d, LAST, S)
             nc.scalar.copy(last_words[:, u], g_last[:, 2 * u : 2 * u + 2, :].rearrange("p j s -> p s j"))
-        drain(4, 7)
-        for first, last, pool, name in ((7, 8, psum2, "turn"), (8, 10, psum, "bank_8")):
-            banks[first] = pool.tile([P, 512], F32, name=name)
-            for e in range(first, last):
-                both_passes(e, e + 1)
-                products(banks[first], first, e, e + 1)
-            drain(first, last)
+        quantise([(0, 11)], by_part[:, 11, 0, :], keep.tile([P, C], U32, name="codes_0_4", align_bytes=64)[:])
+        banks[11] = psum.tile([P, 512], F32, name="gate_bank")
+        multiply(11, 0, banks[11][:, 0:C], True)
+        drain(6, 8)
+        banks[8] = psum.tile([P, 512], F32, name="bank_8")
+        for e in (8, 9):
+            both_passes(e, e + 1)
+            products(banks[8], 8, e, e + 1)
+        drain(8, 10)
         banks[10] = psum.tile([P, 512], F32, name="bank_10")
         both_passes(10, 11)
         products(banks[10], 10, 10, 11)

@@ -25,6 +25,7 @@ FLOPS = 2 * N * K * S
 BYTES = 4 * N * T + E * N * K // 2 + E * N * K // 32 + 4 * S + 2 * P * (S + 2 * T) // 16 + 4 * K * T
 
 BIG = 1024
+MID = BIG // C
 LAST = S - C
 WORDS = PACK * C
 WIDE0 = 2048
@@ -117,8 +118,17 @@ def tile_moe_bdx_lin_none_kernel(tc, dyT, w_words, w_scales, gate, offs, pos1, p
         nc.scalar.copy(gate_cols[:], gate_bank[:, 0:E])
 
         x4 = keep.tile([P, PACK, S], F32, name="x4")
-        gb = keep.tile([P, E * PASSES * WORDS], BF16, name="gb", align_bytes=64)
-        by_part = gb[:].rearrange("p (e a c) -> p e a c", e=E, a=PASSES)
+        gb = keep.tile([P, (E * PASSES + 1) * WORDS], BF16, name="gb", align_bytes=64)
+        blocks = gb[:].rearrange("p (b c) -> p b c", c=WORDS)
+
+        def block(e, a):
+            if e == E - 1:
+                return E * PASSES if a else PASSES * (MID + 1)
+            return PASSES * e + a + max(e - MID, 0)
+
+        def couple(view, first, second):
+            return view[:, first : second + 1 : second - first]
+
         pair_tile = keep.tile([P, E * WORDS], BF16, name="pair_tile", align_bytes=64)
 
         def pairs(e, u):
@@ -142,14 +152,16 @@ def tile_moe_bdx_lin_none_kernel(tc, dyT, w_words, w_scales, gate, offs, pos1, p
                         COPY,
                         scale=gate_cols[:, e0 + b : e0 + b + 1],
                     )
-        pass0_words = gb[:].bitcast(F32).rearrange("p (b e a s u) -> p e a b s u", b=2, e=E // 2, a=PASSES, u=2)
+        block_words = gb[:].bitcast(F32).rearrange("p (b s u) -> p b s u", s=C, u=2)
         for step in range(E // 2):
             e0 = (step + 4) % (E // 2)
             back = psum2.tile([P, 2, 2, C], F32, name="back" if step // 2 == 1 else "turn")
             for b in range(2):
                 for u in range(2):
                     nc.tensor.transpose(back[:, b, u, :], pairs(e0 + b * E // 2, u).bitcast(F32), ident[:])
-            nc.scalar.copy(pass0_words[:, e0, 0], back[:].rearrange("p b u s -> p b s u"))
+            nc.scalar.copy(
+                couple(block_words, block(e0, 0), block(e0 + E // 2, 0)), back[:].rearrange("p b u s -> p b s u")
+            )
 
         g = keep.tile([P, 3 * 512 + PACK * BIG], F32, name="g")
         g_big = g[:, 3 * 512 :].rearrange("p (d s) -> p d s", d=PACK)
@@ -158,15 +170,16 @@ def tile_moe_bdx_lin_none_kernel(tc, dyT, w_words, w_scales, gate, offs, pos1, p
         dx = keep.tile([P, S], F32, name="dx")
 
         def interleave(first, last, g4):
+            step = PASSES if first < MID else PASSES + 1
             nc.scalar.copy(
-                by_part[:, first:last, 1, :].rearrange("p e (n i d) -> p e n d i", d=PACK, i=4),
+                blocks[:, block(first, 1) : block(last - 1, 1) + 1 : step, :].rearrange("p e (n i d) -> p e n d i", d=PACK, i=4),
                 g4.rearrange("p d (e n i) -> p e n d i", e=last - first, i=4),
             )
 
         def both_passes(first, last):
             quantise(
                 [(a, e) for e in range(first, last) for a in range(PASSES)],
-                gb[:, first * PASSES * WORDS : last * PASSES * WORDS],
+                gb[:, block(first, 0) * WORDS : (block(last - 1, 1) + 1) * WORDS],
             )
 
         def products(bank, at, first, last):
@@ -174,9 +187,10 @@ def tile_moe_bdx_lin_none_kernel(tc, dyT, w_words, w_scales, gate, offs, pos1, p
                 for a in range(PASSES):
                     multiply(e, a, bank[:, (e - at) * C : (e - at + 1) * C], a == 0)
 
-        def two_experts(first, pool, name):
-            banks[first] = pool.tile([P, 512], F32, name=name)
-            products(banks[first], first, first, first + 2)
+        def four_experts(first, name):
+            both_passes(first, first + 4)
+            banks[first] = psum2.tile([P, 512], F32, name=name)
+            products(banks[first], first, first, first + 4)
 
         warm = psum.tile([P, 512], F32, name="warm")
 
@@ -202,30 +216,19 @@ def tile_moe_bdx_lin_none_kernel(tc, dyT, w_words, w_scales, gate, offs, pos1, p
             interleave(4 * h, 4 * h + 4, g_big[:, :, 512 * h : 512 * (h + 1)])
         for d in range(PACK - 1):
             gather(g_mid[:, d, :], d, BIG, LAST)
-        both_passes(0, 2)
-        two_experts(0, psum2, "back")
-        drain(0, 2)
-        warm_up(0, 4 * C)
+        four_experts(0, "back")
+        warm_up(0, 2 * C)
         gather(g_mid[:, PACK - 1, :], PACK - 1, BIG, LAST)
         interleave(8, 11, g_mid)
-        both_passes(2, 4)
-        two_experts(2, psum2, "back")
-        drain(2, 4)
-        both_passes(4, 6)
-        two_experts(4, psum2, "turn")
-        drain(4, 6)
-        both_passes(6, 8)
-        two_experts(6, psum2, "turn")
-        warm_up(6, 2 * C)
-        last_words = by_part[:, E - 1, 1, :].rearrange("p (s u j) -> p u s j", u=2, j=2)
-        for u in range(2):
-            for d in (2 * u, 2 * u + 1):
-                gather(g_last[:, d, :], d, LAST, S)
-            nc.scalar.copy(last_words[:, u], g_last[:, 2 * u : 2 * u + 2, :].rearrange("p j s -> p s j"))
-        quantise([(0, 11)], by_part[:, 11, 0, :], keep.tile([P, C], U32, name="codes_0_4", align_bytes=64)[:])
+        drain(0, 4)
+        four_experts(4, "back")
+        for d in range(PACK):
+            gather(g_last[:, d, :], d, LAST, S)
+        interleave(11, 12, g_last)
+        quantise([(0, 11)], blocks[:, block(11, 0), :])
         banks[11] = psum.tile([P, 512], F32, name="gate_bank")
         multiply(11, 0, banks[11][:, 0:C], True)
-        drain(6, 8)
+        drain(4, 8)
         banks[8] = psum.tile([P, 512], F32, name="bank_8")
         for e in (8, 9):
             both_passes(e, e + 1)
@@ -235,7 +238,7 @@ def tile_moe_bdx_lin_none_kernel(tc, dyT, w_words, w_scales, gate, offs, pos1, p
         both_passes(10, 11)
         products(banks[10], 10, 10, 11)
         drain(10, 11)
-        quantise([(1, 11)], by_part[:, 11, 1, :])
+        quantise([(1, 11)], blocks[:, block(11, 1), :])
         multiply(11, 1, banks[11][:, 0:C], False)
         drain(11, 12)
 

@@ -85,7 +85,7 @@ def tile_moe_bdx_lin_none_kernel(tc, dyT, w_words, w_scales, gate, offs, pos1, p
             nc.sync.dma_start(out=ws_i32[32 * q : 32 * q + 4, :, :], in_=scale_rows[4 * q : 4 * q + 4, :, :])
         nc.sync.dma_start(out=w_i32[:, half:, :], in_=words[:, half:, :])
 
-        codes, scales, banks, whole = {}, {}, {}, {}
+        codes, scales, banks = {}, {}, {}
 
         def gather(into, d, lo, hi):
             nc.vector.tensor_tensor(into, dy1[d][:].indirect(offs_sb[:, lo // 16 : hi // 16]), gate_sb[:, lo:hi], MULT)
@@ -96,7 +96,6 @@ def tile_moe_bdx_lin_none_kernel(tc, dyT, w_words, w_scales, gate, offs, pos1, p
                 made = keep.tile([P, len(parts) * C], U32, name=f"codes_{a0}_{e0}", align_bytes=64)[:]
             plane = keep.tile([P, len(parts) * C], U8, name=f"scales_{a0}_{e0}", align_bytes=64)
             nc.vector.quantize_mx(out=made.bitcast(FP8X4), scales=plane[:], in_=values)
-            whole[a0, e0] = (made, plane[:])
             for i, part in enumerate(parts):
                 codes[part] = made[:, i * C : (i + 1) * C]
                 scales[part] = plane[:, i * C : (i + 1) * C]
@@ -192,19 +191,6 @@ def tile_moe_bdx_lin_none_kernel(tc, dyT, w_words, w_scales, gate, offs, pos1, p
             banks[first] = psum2.tile([P, 512], F32, name=name)
             products(banks[first], first, first, first + 4)
 
-        warm = psum.tile([P, 512], F32, name="warm")
-
-        def warm_up(e, width):
-            nc.tensor.matmul_mx(
-                out=warm[:, 0:width],
-                lhsT=w_sb[:, 0, :].bitcast(FP4X4),
-                lhsT_scale=ws_sb[:, 0, :],
-                rhs=whole[0, e][0][:, 0:width].bitcast(FP8X4),
-                rhs_scale=whole[0, e][1][:, 0:width],
-                start=True,
-                stop=True,
-            )
-
         def drain(first, last):
             nc.scalar.copy(dx[:, first * C : last * C], banks[first][:, 0 : (last - first) * C])
 
@@ -217,7 +203,6 @@ def tile_moe_bdx_lin_none_kernel(tc, dyT, w_words, w_scales, gate, offs, pos1, p
         for d in range(PACK - 1):
             gather(g_mid[:, d, :], d, BIG, LAST)
         four_experts(0, "back")
-        warm_up(0, 2 * C)
         gather(g_mid[:, PACK - 1, :], PACK - 1, BIG, LAST)
         interleave(8, 11, g_mid)
         drain(0, 4)

@@ -66,24 +66,27 @@ def tile_moe_bdx_lin_none_kernel(tc, dyT, w_words, w_scales, gate, offs, pos1, p
         nc.sync.dma_start(offs_sb[:], offs)
         for d in range(1, PACK):
             nc.sync.dma_start(out=dy0[:, at0(d) : at0(d) + T], in_=rows[0, d])
+            if d == 1:
+                nc.sync.dma_start(pos1_sb[:], pos1)
+                nc.sync.dma_start(pos2_sb[:], pos2)
         by_expert = gate[0, :].rearrange("(e s) -> e s", s=C)
         nc.sync.dma_start(out=gate_rows[0:8, :], in_=by_expert[0:8])
         nc.sync.dma_start(out=gate_rows[8:E, :], in_=by_expert[8:E])
         nc.sync.dma_start(out=gate_sb[:], in_=gate[0:P, :])
         for d in range(PACK):
             nc.sync.dma_start(out=dy1[d][:, 0:T], in_=rows[1, d])
-        nc.sync.dma_start(pos1_sb[:], pos1)
-        nc.sync.dma_start(pos2_sb[:], pos2)
         nc.vector.memset(ws_sb[:].rearrange("p g k -> p (g k)").bitcast(I32), 0)
         words = w_words.bitcast(I32).rearrange("e a p n -> p (e a) n")
         w_i32 = w_sb[:].bitcast(I32)
-        half = E * PASSES // 2
-        nc.sync.dma_start(out=w_i32[:, 0:half, :], in_=words[:, 0:half, :])
+        half = E * PASSES // 3
+        for q in range(1):
+            nc.sync.dma_start(out=w_i32[:, q * half : (q + 1) * half, :], in_=words[:, q * half : (q + 1) * half, :])
         scale_rows = w_scales.bitcast(I32).rearrange("e a f k -> f (e a) k")
         ws_i32 = ws_sb[:].bitcast(I32)
         for q in range(4):
             nc.sync.dma_start(out=ws_i32[32 * q : 32 * q + 4, :, :], in_=scale_rows[4 * q : 4 * q + 4, :, :])
-        nc.sync.dma_start(out=w_i32[:, half:, :], in_=words[:, half:, :])
+        for q in range(1, 3):
+            nc.sync.dma_start(out=w_i32[:, q * half : (q + 1) * half, :], in_=words[:, q * half : (q + 1) * half, :])
 
         codes, scales, banks = {}, {}, {}
 
@@ -229,8 +232,8 @@ def tile_moe_bdx_lin_none_kernel(tc, dyT, w_words, w_scales, gate, offs, pos1, p
 
         one = keep.tile([P, T], F32, name="one")
         both = keep.tile([P, T], F32, name="both")
-        cuts = ((0, 512), (512, T))
-        for lo, hi in cuts:
+        cuts = ((0, 384), (384, 640), (640, T))
+        for lo, hi in ((0, 384), (384, T)):
             nc.vector.tensor_copy(one[:, lo:hi], dx[:].indirect(pos1_sb[:, lo // 16 : hi // 16]))
         for lo, hi in cuts:
             nc.vector.tensor_tensor(both[:, lo:hi], dx[:].indirect(pos2_sb[:, lo // 16 : hi // 16]), one[:, lo:hi], ADD)

@@ -138,7 +138,7 @@ def tile_moe_bdx_lin_none_kernel(tc, dyT, w_words, w_scales, gate, offs, pos1, p
 
         for u in range(2):
             for d in (2 * u, 2 * u + 1):
-                for lo, hi in ((0, S),) if d < PACK - 1 else ((0, S // 2), (S // 2, S)):
+                for lo, hi in ((0, S),):
                     nc.vector.tensor_copy(
                         x4[:, d, lo:hi], dy0[:, at0(d) : at0(d) + WIDE0].indirect(offs_sb[:, lo // 16 : hi // 16])
                     )

@@ -72,20 +72,19 @@ def tile_moe_bdx_lin_none_kernel(tc, dyT, w_words, w_scales, gate, offs, pos1, p
         by_expert = gate[0, :].rearrange("(e s) -> e s", s=C)
         nc.sync.dma_start(out=gate_rows[0:8, :], in_=by_expert[0:8])
         nc.sync.dma_start(out=gate_rows[8:E, :], in_=by_expert[8:E])
-        nc.sync.dma_start(out=gate_sb[:], in_=gate[0:P, :])
         for d in range(PACK):
             nc.sync.dma_start(out=dy1[d][:, 0:T], in_=rows[1, d])
         nc.vector.memset(ws_sb[:].rearrange("p g k -> p (g k)").bitcast(I32), 0)
         words = w_words.bitcast(I32).rearrange("e a p n -> p (e a) n")
         w_i32 = w_sb[:].bitcast(I32)
-        half = E * PASSES // 3
+        half = E * PASSES // 4
         for q in range(1):
             nc.sync.dma_start(out=w_i32[:, q * half : (q + 1) * half, :], in_=words[:, q * half : (q + 1) * half, :])
         scale_rows = w_scales.bitcast(I32).rearrange("e a f k -> f (e a) k")
         ws_i32 = ws_sb[:].bitcast(I32)
         for q in range(4):
             nc.sync.dma_start(out=ws_i32[32 * q : 32 * q + 4, :, :], in_=scale_rows[4 * q : 4 * q + 4, :, :])
-        for q in range(1, 3):
+        for q in range(1, 4):
             nc.sync.dma_start(out=w_i32[:, q * half : (q + 1) * half, :], in_=words[:, q * half : (q + 1) * half, :])
 
         codes, scales, banks = {}, {}, {}
@@ -118,6 +117,11 @@ def tile_moe_bdx_lin_none_kernel(tc, dyT, w_words, w_scales, gate, offs, pos1, p
         nc.tensor.transpose(gate_bank[:, 0:P], gate_rows[:], ident[:])
         gate_cols = keep.tile([P, E], F32, name="gate_cols")
         nc.scalar.copy(gate_cols[:], gate_bank[:, 0:E])
+        for e0 in range(0, E, 4):
+            spread = psum.tile([P, 4, C], F32, name=("gate_bank", "bank_8", "bank_10")[e0 // 4])
+            for b in range(4):
+                nc.tensor.transpose(spread[:, b, :], gate_cols[:, e0 + b : e0 + b + 1].to_broadcast([P, P]), ident[:])
+            nc.scalar.copy(gate_sb[:, e0 * C : (e0 + 4) * C], spread[:].rearrange("p b s -> p (b s)"))
 
         x4 = keep.tile([P, PACK, S], F32, name="x4")
         gb = keep.tile([P, (E * PASSES + 1) * WORDS], BF16, name="gb", align_bytes=64)

@@ -1,7 +1,6 @@
 from contextlib import ExitStack
 
 import concourse.mybir as mybir
-from concourse.masks import make_identity
 
 F32 = mybir.dt.float32
 BF16 = mybir.dt.bfloat16
@@ -24,12 +23,8 @@ PACK = 4
 FLOPS = 2 * N * K * S
 BYTES = 4 * N * T + E * N * K // 2 + E * N * K // 32 + 4 * S + 2 * P * (S + 2 * T) // 16 + 4 * K * T
 
-BIG = 1024
-MID = BIG // C
-LAST = S - C
-WORDS = PACK * C
-WIDE0 = 2048
-WIDE1 = 1040
+BANKS = ((0, 3), (3, 6), (6, 8), (8, 9), (9, 12))
+RUN = 2
 
 
 def tile_moe_bdx_lin_none_kernel(tc, dyT, w_words, w_scales, gate, offs, pos1, pos2, out):
@@ -38,7 +33,6 @@ def tile_moe_bdx_lin_none_kernel(tc, dyT, w_words, w_scales, gate, offs, pos1, p
         lists = ctx.enter_context(tc.tile_pool(name="lists", bufs=1))
         keep = ctx.enter_context(tc.tile_pool(name="keep", bufs=1))
         psum = ctx.enter_context(tc.psum_pool(name="psum", bufs=1))
-        psum2 = ctx.enter_context(tc.psum_pool(name="psum2", bufs=2))
 
         offs_sb = lists.tile([P, S // 16], U16, name="offs_sb")
         pos1_sb = lists.tile([P, T // 16], U16, name="pos1_sb")
@@ -47,198 +41,172 @@ def tile_moe_bdx_lin_none_kernel(tc, dyT, w_words, w_scales, gate, offs, pos1, p
         w_sb = keep.tile([P, E * PASSES, 2 * K], U8, name="w_sb", align_bytes=64)
         ws_sb = keep.tile([P, E * PASSES, K], U8, name="ws_sb", align_bytes=64)
         gate_sb = keep.tile([P, S], F32, name="gate_sb")
-        dy0 = keep.tile([P, (PACK - 1) * T + WIDE0], F32, name="dy0")
-        dy1 = [keep.tile([P, WIDE1], F32, name=f"dy1_{d}") for d in range(PACK)]
-
-        def at0(d):
-            return (PACK - 1 - d) * T
-
-        nc.vector.memset(dy0[:, PACK * T :], 0.0)
-        ident = keep.tile([P, P], F32, name="ident", align_bytes=64)
-        make_identity(nc, ident[:])
-        gate_rows = keep.tile([P, C], F32, name="gate_rows")
-        nc.gpsimd.memset(gate_rows[:], 0.0)
-        for d in reversed(range(PACK)):
-            nc.scalar.copy(dy1[d][:, T:WIDE1], dy0[:, PACK * T : PACK * T + WIDE1 - T])
+        planes = {(a, d): keep.tile([P, T], F32, name=f"plane_{a}_{d}") for a in range(PASSES) for d in range(PACK)}
 
         rows = dyT.rearrange("(a p d) t -> a d p t", a=PASSES, d=PACK)
-        nc.sync.dma_start(out=dy0[:, at0(0) : at0(0) + T], in_=rows[0, 0])
-        nc.sync.dma_start(offs_sb[:], offs)
-        for d in range(1, PACK):
-            nc.sync.dma_start(out=dy0[:, at0(d) : at0(d) + T], in_=rows[0, d])
-            if d == 1:
-                nc.sync.dma_start(pos1_sb[:], pos1)
-                nc.sync.dma_start(pos2_sb[:], pos2)
-        by_expert = gate[0, :].rearrange("(e s) -> e s", s=C)
-        nc.sync.dma_start(out=gate_rows[0:8, :], in_=by_expert[0:8])
-        nc.sync.dma_start(out=gate_rows[8:E, :], in_=by_expert[8:E])
-        for d in range(PACK):
-            nc.sync.dma_start(out=dy1[d][:, 0:T], in_=rows[1, d])
-        nc.vector.memset(ws_sb[:].rearrange("p g k -> p (g k)").bitcast(I32), 0)
         words = w_words.bitcast(I32).rearrange("e a p n -> p (e a) n")
         w_i32 = w_sb[:].bitcast(I32)
-        half = E * PASSES // 4
-        for q in range(1):
-            nc.sync.dma_start(out=w_i32[:, q * half : (q + 1) * half, :], in_=words[:, q * half : (q + 1) * half, :])
         scale_rows = w_scales.bitcast(I32).rearrange("e a f k -> f (e a) k")
         ws_i32 = ws_sb[:].bitcast(I32)
-        for q in range(4):
-            nc.sync.dma_start(out=ws_i32[32 * q : 32 * q + 4, :, :], in_=scale_rows[4 * q : 4 * q + 4, :, :])
-        for q in range(1, 4):
-            nc.sync.dma_start(out=w_i32[:, q * half : (q + 1) * half, :], in_=words[:, q * half : (q + 1) * half, :])
 
-        codes, scales, banks = {}, {}, {}
+        def load_plane(a, d):
+            nc.sync.dma_start(out=planes[a, d][:], in_=rows[a, d])
 
-        def gather(into, d, lo, hi):
-            nc.vector.tensor_tensor(into, dy1[d][:].indirect(offs_sb[:, lo // 16 : hi // 16]), gate_sb[:, lo:hi], MULT)
+        def load_gate(lo, hi):
+            nc.sync.dma_start(out=gate_sb[:, lo:hi], in_=gate[0:P, lo:hi])
 
-        def quantise(parts, values, made=None):
-            a0, e0 = parts[0]
-            if made is None:
-                made = keep.tile([P, len(parts) * C], U32, name=f"codes_{a0}_{e0}", align_bytes=64)[:]
-            plane = keep.tile([P, len(parts) * C], U8, name=f"scales_{a0}_{e0}", align_bytes=64)
-            nc.vector.quantize_mx(out=made.bitcast(FP8X4), scales=plane[:], in_=values)
-            for i, part in enumerate(parts):
-                codes[part] = made[:, i * C : (i + 1) * C]
-                scales[part] = plane[:, i * C : (i + 1) * C]
+        def load_words(first, last):
+            nc.sync.dma_start(out=w_i32[:, PASSES * first : PASSES * last, :], in_=words[:, PASSES * first : PASSES * last, :])
 
-        def multiply(e, a, into, first):
-            nc.tensor.matmul_mx(
-                out=into,
-                lhsT=w_sb[:, PASSES * e + a, :].bitcast(FP4X4),
-                lhsT_scale=ws_sb[:, PASSES * e + a, :],
-                rhs=codes[a, e].bitcast(FP8X4),
-                rhs_scale=scales[a, e],
-                start=first,
-                stop=not first,
-            )
+        def load_scales():
+            for q in range(4):
+                nc.sync.dma_start(out=ws_i32[32 * q : 32 * q + 4, :, :], in_=scale_rows[4 * q : 4 * q + 4, :, :])
 
-        gate_bank = psum.tile([P, 512], F32, name="gate_bank")
-        nc.tensor.transpose(gate_bank[:, 0:P], gate_rows[:], ident[:])
-        gate_cols = keep.tile([P, E], F32, name="gate_cols")
-        nc.scalar.copy(gate_cols[:], gate_bank[:, 0:E])
-        for e0 in range(0, E, 4):
-            spread = psum.tile([P, 4, C], F32, name=("gate_bank", "bank_8", "bank_10")[e0 // 4])
-            for b in range(4):
-                nc.tensor.transpose(spread[:, b, :], gate_cols[:, e0 + b : e0 + b + 1].to_broadcast([P, P]), ident[:])
-            nc.scalar.copy(gate_sb[:, e0 * C : (e0 + 4) * C], spread[:].rearrange("p b s -> p (b s)"))
+        nc.vector.memset(ws_sb[:].rearrange("p g k -> p (g k)").bitcast(I32), 0)
+        load_plane(0, 0)
+        nc.sync.dma_start(offs_sb[:], offs)
+        load_gate(1152, S)
+        for d in range(1, PACK):
+            load_plane(0, d)
+        load_gate(0, 384)
+        for d in range(PACK):
+            load_plane(1, d)
+        load_gate(384, 1152)
+        load_words(0, E)
+        load_scales()
+        nc.sync.dma_start(pos1_sb[:], pos1)
+        nc.sync.dma_start(pos2_sb[:], pos2)
 
-        x4 = keep.tile([P, PACK, S], F32, name="x4")
-        gb = keep.tile([P, (E * PASSES + 1) * WORDS], BF16, name="gb", align_bytes=64)
-        blocks = gb[:].rearrange("p (b c) -> p b c", c=WORDS)
-
-        def block(e, a):
-            if e == E - 1:
-                return E * PASSES if a else PASSES * (MID + 1)
-            return PASSES * e + a + max(e - MID, 0)
-
-        def couple(view, first, second):
-            return view[:, first : second + 1 : second - first]
-
-        pair_tile = keep.tile([P, E * WORDS], BF16, name="pair_tile", align_bytes=64)
-
-        def pairs(e, u):
-            return pair_tile[:, (2 * e + u) * 2 * P : (2 * e + u + 1) * 2 * P]
-
-        for u in range(2):
-            for d in (2 * u, 2 * u + 1):
-                for lo, hi in ((0, S),):
-                    nc.vector.tensor_copy(
-                        x4[:, d, lo:hi], dy0[:, at0(d) : at0(d) + WIDE0].indirect(offs_sb[:, lo // 16 : hi // 16])
-                    )
-            for e0 in range(0, E, 2):
-                turn = psum2.tile([P, 2, 2, P], F32, name="turn" if (u * E + e0) % 8 < 4 else "back")
-                for b in range(2):
-                    for j in range(2):
-                        nc.tensor.transpose(turn[:, b, j, :], x4[:, 2 * u + j, (e0 + b) * C : (e0 + b + 1) * C], ident[:])
-                for b in range(2):
-                    nc.scalar.activation(
-                        pairs(e0 + b, u).rearrange("s (p j) -> s p j", j=2),
-                        turn[:, b, :, :].rearrange("s j p -> s p j"),
-                        COPY,
-                        scale=gate_cols[:, e0 + b : e0 + b + 1],
-                    )
-        block_words = gb[:].bitcast(F32).rearrange("p (b s u) -> p b s u", s=C, u=2)
-        for step in range(E // 2):
-            e0 = (step + 4) % (E // 2)
-            back = psum2.tile([P, 2, 2, C], F32, name="back" if step // 2 == 1 else "turn")
-            for b in range(2):
-                for u in range(2):
-                    nc.tensor.transpose(back[:, b, u, :], pairs(e0 + b * E // 2, u).bitcast(F32), ident[:])
-            nc.scalar.copy(
-                couple(block_words, block(e0, 0), block(e0 + E // 2, 0)), back[:].rearrange("p b u s -> p b s u")
-            )
-
-        g = keep.tile([P, 3 * 512 + PACK * BIG], F32, name="g")
-        g_big = g[:, 3 * 512 :].rearrange("p (d s) -> p d s", d=PACK)
-        g_mid = g[:, 0 : PACK * 512].rearrange("p (d s) -> p d s", d=PACK)[:, :, 0 : LAST - BIG]
-        g_last = g[:, 2 * 512 + PACK * BIG :].rearrange("p (d s) -> p d s", d=PACK)
+        gathered, rounded, codes, scales, banks = {}, {}, {}, {}, {}
         dx = keep.tile([P, S], F32, name="dx")
 
-        def interleave(first, last, g4):
-            step = PASSES if first < MID else PASSES + 1
-            nc.scalar.copy(
-                blocks[:, block(first, 1) : block(last - 1, 1) + 1 : step, :].rearrange("p e (n i d) -> p e n d i", d=PACK, i=4),
-                g4.rearrange("p d (e n i) -> p e n d i", e=last - first, i=4),
+        def find(table, a, lo):
+            return [(tile, at) for (b, at, end), tile in table.items() if b == a and at <= lo < end][0]
+
+        def window(a, d, lo, hi):
+            return planes[a, d][:].indirect(offs_sb[:, lo // 16 : hi // 16])
+
+        def piece(a, lo, hi):
+            gathered[a, lo, hi] = keep.tile([P, PACK, hi - lo], F32, name=f"x_{a}_{lo}")
+
+        def block(a, lo, hi):
+            rounded[a, lo, hi] = keep.tile([P, (hi - lo) * PACK], BF16, name=f"g_{a}_{lo}", align_bytes=64)
+
+        def into(a, d, lo, hi):
+            x, at = find(gathered, a, lo)
+            return x[:, d, lo - at : hi - at]
+
+        def gather_scalar(a, d, lo, hi):
+            nc.scalar.activation(into(a, d, lo, hi), window(a, d, lo, hi), COPY)
+
+        def gather_vector(a, d, lo, hi):
+            nc.vector.tensor_copy(into(a, d, lo, hi), window(a, d, lo, hi))
+
+        def gather_gated(a, d, lo, hi):
+            nc.vector.tensor_tensor(into(a, d, lo, hi), window(a, d, lo, hi), gate_sb[:, lo:hi], MULT)
+
+        def views(a, lo, hi):
+            x, at = find(gathered, a, lo)
+            g, start = find(rounded, a, lo)
+            src = x[:, :, lo - at : hi - at].rearrange("p d (n i) -> p n d i", i=RUN)
+            dst = g[:, (lo - start) * PACK : (hi - start) * PACK].rearrange("p (n i d) -> p n d i", i=RUN, d=PACK)
+            return dst, src
+
+        def weave_gated(a, lo, hi):
+            dst, src = views(a, lo, hi)
+            gates = gate_sb[:, lo:hi].rearrange("p (n i) -> p n i", i=RUN)
+            nc.vector.tensor_tensor(dst, src, gates.unsqueeze(2).to_broadcast([P, (hi - lo) // RUN, PACK, RUN]), MULT)
+
+        def weave(a, lo, hi):
+            dst, src = views(a, lo, hi)
+            nc.vector.tensor_copy(dst, src)
+
+        def quantise(a, lo, hi):
+            g, start = find(rounded, a, lo)
+            codes[a, lo, hi] = keep.tile([P, hi - lo], U32, name=f"codes_{a}_{lo}", align_bytes=64)
+            scales[a, lo, hi] = keep.tile([P, hi - lo], U8, name=f"scales_{a}_{lo}", align_bytes=64)
+            nc.vector.quantize_mx(
+                out=codes[a, lo, hi][:].bitcast(FP8X4),
+                scales=scales[a, lo, hi][:],
+                in_=g[:, (lo - start) * PACK : (hi - start) * PACK],
             )
 
-        def both_passes(first, last):
-            quantise(
-                [(a, e) for e in range(first, last) for a in range(PASSES)],
-                gb[:, block(first, 0) * WORDS : (block(last - 1, 1) + 1) * WORDS],
-            )
-
-        def products(bank, at, first, last):
+        def products(a, first, last):
             for e in range(first, last):
-                for a in range(PASSES):
-                    multiply(e, a, bank[:, (e - at) * C : (e - at + 1) * C], a == 0)
+                low, high = [group for group in BANKS if group[0] <= e < group[1]][0]
+                if low not in banks:
+                    banks[low] = [psum.tile([P, 512], F32, name=f"bank_{low}"), 0]
+                made, at = find(codes, a, e * C)
+                plane, at = find(scales, a, e * C)
+                nc.tensor.matmul_mx(
+                    out=banks[low][0][:, (e - low) * C : (e - low + 1) * C],
+                    lhsT=w_sb[:, PASSES * e + a, :].bitcast(FP4X4),
+                    lhsT_scale=ws_sb[:, PASSES * e + a, :],
+                    rhs=made[:, e * C - at : (e + 1) * C - at].bitcast(FP8X4),
+                    rhs_scale=plane[:, e * C - at : (e + 1) * C - at],
+                    start=banks[low][1] == 0,
+                    stop=banks[low][1] == PASSES * (high - low) - 1,
+                )
+                banks[low][1] = banks[low][1] + 1
 
-        def four_experts(first, name):
-            both_passes(first, first + 4)
-            banks[first] = psum2.tile([P, 512], F32, name=name)
-            products(banks[first], first, first, first + 4)
+        def drain(first, last, engine):
+            if engine == "scalar":
+                nc.scalar.copy(dx[:, first * C : last * C], banks[first][0][:, 0 : (last - first) * C])
+            else:
+                nc.vector.tensor_copy(dx[:, first * C : last * C], banks[first][0][:, 0 : (last - first) * C])
 
-        def drain(first, last):
-            nc.scalar.copy(dx[:, first * C : last * C], banks[first][:, 0 : (last - first) * C])
+        for a, lo, hi in ((0, 0, 384), (0, 384, 768), (0, 768, 1152), (1, 0, 384), (1, 384, 768), (1, 768, 1024), (1, 1024, 1152)):
+            piece(a, lo, hi)
+            block(a, lo, hi)
+            for d in range(PACK):
+                gather_scalar(a, d, lo, hi)
+        for a in range(PASSES):
+            piece(a, 1152, S)
+            block(a, 1152, S)
 
-        for d in range(PACK - 1):
-            gather(g_big[:, d, :], d, 0, BIG)
-        for h in range(2):
-            gather(g_big[:, PACK - 1, 512 * h : 512 * (h + 1)], PACK - 1, 512 * h, 512 * (h + 1))
-        for h in range(2):
-            interleave(4 * h, 4 * h + 4, g_big[:, :, 512 * h : 512 * (h + 1)])
-        for d in range(PACK - 1):
-            gather(g_mid[:, d, :], d, BIG, LAST)
-        four_experts(0, "back")
-        gather(g_mid[:, PACK - 1, :], PACK - 1, BIG, LAST)
-        interleave(8, 11, g_mid)
-        drain(0, 4)
-        four_experts(4, "back")
         for d in range(PACK):
-            gather(g_last[:, d, :], d, LAST, S)
-        interleave(11, 12, g_last)
-        quantise([(0, 11)], blocks[:, block(11, 0), :])
-        banks[11] = psum.tile([P, 512], F32, name="gate_bank")
-        multiply(11, 0, banks[11][:, 0:C], True)
-        drain(4, 8)
-        banks[8] = psum.tile([P, 512], F32, name="bank_8")
-        for e in (8, 9):
-            both_passes(e, e + 1)
-            products(banks[8], 8, e, e + 1)
-        drain(8, 10)
-        banks[10] = psum.tile([P, 512], F32, name="bank_10")
-        both_passes(10, 11)
-        products(banks[10], 10, 10, 11)
-        drain(10, 11)
-        quantise([(1, 11)], blocks[:, block(11, 1), :])
-        multiply(11, 1, banks[11][:, 0:C], False)
-        drain(11, 12)
+            gather_gated(0, d, 1152, S)
+        weave(0, 1152, S)
+        weave_gated(0, 0, 384)
+        quantise(0, 1152, S)
+        quantise(0, 0, 384)
+        products(0, 9, 12)
+        products(0, 0, 3)
+        for d in range(PACK):
+            gather_gated(1, d, 1152, S)
+        weave_gated(0, 384, 768)
+        weave(1, 1152, S)
+        quantise(0, 384, 768)
+        products(0, 3, 6)
+        weave_gated(0, 768, 1152)
+        quantise(1, 1152, S)
+        products(1, 9, 12)
+        quantise(0, 768, 1152)
+        products(0, 6, 9)
+        weave_gated(1, 0, 256)
+        weave_gated(1, 256, 384)
+        quantise(1, 0, 256)
+        quantise(1, 256, 384)
+        products(1, 0, 3)
+        weave_gated(1, 384, 640)
+        weave_gated(1, 640, 768)
+        quantise(1, 384, 640)
+        quantise(1, 640, 768)
+        products(1, 3, 6)
+        weave_gated(1, 768, 1024)
+        weave_gated(1, 1024, 1152)
+        quantise(1, 768, 1024)
+        products(1, 6, 8)
+        quantise(1, 1024, 1152)
+        products(1, 8, 9)
+        for first, last in ((9, 12), (0, 3), (3, 6), (6, 8), (8, 9)):
+            drain(first, last, "scalar")
 
         one = keep.tile([P, T], F32, name="one")
         both = keep.tile([P, T], F32, name="both")
-        cuts = ((0, 384), (384, 640), (640, T))
-        for lo, hi in ((0, 384), (384, T)):
-            nc.vector.tensor_copy(one[:, lo:hi], dx[:].indirect(pos1_sb[:, lo // 16 : hi // 16]))
-        for lo, hi in cuts:
+        for lo, hi in ((0, 128), (128, 384), (384, 640), (640, T)):
+            nc.scalar.activation(one[:, lo:hi], dx[:].indirect(pos1_sb[:, lo // 16 : hi // 16]), COPY)
             nc.vector.tensor_tensor(both[:, lo:hi], dx[:].indirect(pos2_sb[:, lo // 16 : hi // 16]), one[:, lo:hi], ADD)
-            nc.sync.dma_start(out=out[:, lo:hi], in_=both[:, lo:hi])
+            if lo:
+                at = 0 if lo == 128 else lo
+                nc.sync.dma_start(out=out[:, at:hi], in_=both[:, at:hi])

@@ -23,7 +23,8 @@ PACK = 4
 FLOPS = 2 * N * K * S
 BYTES = 4 * N * T + E * N * K // 2 + E * N * K // 32 + 4 * S + 2 * P * (S + 2 * T) // 16 + 4 * K * T
 
-BANKS = ((0, 3), (3, 6), (6, 8), (8, 9), (9, 12))
+BANKS = ((0, 4), (4, 8), (8, 10), (10, 11), (11, 12))
+WIDTHS = (880, T)
 RUN = 2
 
 
@@ -41,7 +42,7 @@ def tile_moe_bdx_lin_none_kernel(tc, dyT, w_words, w_scales, gate, offs, pos1, p
         w_sb = keep.tile([P, E * PASSES, 2 * K], U8, name="w_sb", align_bytes=64)
         ws_sb = keep.tile([P, E * PASSES, K], U8, name="ws_sb", align_bytes=64)
         gate_sb = keep.tile([P, S], F32, name="gate_sb")
-        planes = {(a, d): keep.tile([P, T], F32, name=f"plane_{a}_{d}") for a in range(PASSES) for d in range(PACK)}
+        planes = {(a, d): keep.tile([P, WIDTHS[a] if d else T], F32, name=f"plane_{a}_{d}") for a in range(PASSES) for d in range(PACK)}
 
         rows = dyT.rearrange("(a p d) t -> a d p t", a=PASSES, d=PACK)
         words = w_words.bitcast(I32).rearrange("e a p n -> p (e a) n")
@@ -50,7 +51,7 @@ def tile_moe_bdx_lin_none_kernel(tc, dyT, w_words, w_scales, gate, offs, pos1, p
         ws_i32 = ws_sb[:].bitcast(I32)
 
         def load_plane(a, d):
-            nc.sync.dma_start(out=planes[a, d][:], in_=rows[a, d])
+            nc.sync.dma_start(out=planes[a, d][:, 0:T], in_=rows[a, d])
 
         def load_gate(lo, hi):
             nc.sync.dma_start(out=gate_sb[:, lo:hi], in_=gate[0:P, lo:hi])
@@ -63,15 +64,20 @@ def tile_moe_bdx_lin_none_kernel(tc, dyT, w_words, w_scales, gate, offs, pos1, p
                 nc.sync.dma_start(out=ws_i32[32 * q : 32 * q + 4, :, :], in_=scale_rows[4 * q : 4 * q + 4, :, :])
 
         nc.vector.memset(ws_sb[:].rearrange("p g k -> p (g k)").bitcast(I32), 0)
+        zeros = keep.tile([P, 112], F32, name="zeros")
+        nc.gpsimd.memset(zeros[:], 0.0)
+        nc.scalar.activation(planes[0, 1][:, T:], zeros[:], COPY)
+        for d in (2, 3):
+            nc.gpsimd.memset(planes[0, d][:, T:], 0.0)
         load_plane(0, 0)
         nc.sync.dma_start(offs_sb[:], offs)
+        load_gate(864, 1152)
         load_gate(1152, S)
         for d in range(1, PACK):
             load_plane(0, d)
-        load_gate(0, 384)
         for d in range(PACK):
             load_plane(1, d)
-        load_gate(384, 1152)
+        load_gate(0, 864)
         load_words(0, E)
         load_scales()
         nc.sync.dma_start(pos1_sb[:], pos1)
@@ -155,58 +161,71 @@ def tile_moe_bdx_lin_none_kernel(tc, dyT, w_words, w_scales, gate, offs, pos1, p
             else:
                 nc.vector.tensor_copy(dx[:, first * C : last * C], banks[first][0][:, 0 : (last - first) * C])
 
-        for a, lo, hi in ((0, 0, 384), (0, 384, 768), (0, 768, 1152), (1, 0, 384), (1, 384, 768), (1, 768, 1024), (1, 1024, 1152)):
-            piece(a, lo, hi)
-            block(a, lo, hi)
-            for d in range(PACK):
-                gather_scalar(a, d, lo, hi)
-        for a in range(PASSES):
-            piece(a, 1152, S)
-            block(a, 1152, S)
+        woven = keep.tile([P, S * PACK], BF16, name="woven", align_bytes=64)
 
+
+        def place(a, lo, hi, at):
+            rounded[a, lo, hi] = woven[:, at * PACK : (at + hi - lo) * PACK]
+
+
+        def reuse(tile, pieces):
+            flat, at = tile[:].rearrange("p d s -> p (d s)"), 0
+            for lo, hi in pieces:
+                gathered[1, lo, hi] = flat[:, at : at + PACK * (hi - lo)].rearrange("p (d s) -> p d s", d=PACK)
+                at = at + PACK * (hi - lo)
+
+        place(0, 0, S, 0)
+        piece(0, 0, 864)
+        piece(0, 864, S)
+        piece(1, 0, 640)
+        gather_vector(0, 0, 0, 160)
         for d in range(PACK):
-            gather_gated(0, d, 1152, S)
-        weave(0, 1152, S)
-        weave_gated(0, 0, 384)
-        quantise(0, 1152, S)
-        quantise(0, 0, 384)
-        products(0, 9, 12)
-        products(0, 0, 3)
-        for d in range(PACK):
-            gather_gated(1, d, 1152, S)
-        weave_gated(0, 384, 768)
-        weave(1, 1152, S)
-        quantise(0, 384, 768)
-        products(0, 3, 6)
-        weave_gated(0, 768, 1152)
-        quantise(1, 1152, S)
-        products(1, 9, 12)
-        quantise(0, 768, 1152)
-        products(0, 6, 9)
-        weave_gated(1, 0, 256)
-        weave_gated(1, 256, 384)
-        quantise(1, 0, 256)
-        quantise(1, 256, 384)
-        products(1, 0, 3)
-        weave_gated(1, 384, 640)
-        weave_gated(1, 640, 768)
-        quantise(1, 384, 640)
-        quantise(1, 640, 768)
-        products(1, 3, 6)
-        weave_gated(1, 768, 1024)
-        weave_gated(1, 1024, 1152)
-        quantise(1, 768, 1024)
-        products(1, 6, 8)
-        quantise(1, 1024, 1152)
-        products(1, 8, 9)
-        for first, last in ((9, 12), (0, 3), (3, 6), (6, 8), (8, 9)):
-            drain(first, last, "scalar")
+            gather_scalar(0, d, 0 if d else 160, 864)
+        gather_gated(0, 0, 864, 1152)
+        gather_gated(0, 0, 1152, S)
+        for d in range(1, PACK):
+            gather_gated(0, d, 864, S)
+        weave(0, 864, S)
+        weave_gated(0, 0, 864)
+        reuse(gathered[0, 0, 864], ((640, 1024), (1024, 1280)))
+        for lo, hi in ((0, 640), (640, 1024), (1024, 1280)):
+            for d in range(PACK):
+                gather_scalar(1, d, lo, hi)
+        quantise(0, 0, 1024)
+        quantise(0, 1024, S)
+        products(0, 0, E)
+        place(1, 0, 1280, 0)
+        place(1, 1280, 1408, 0)
+        place(1, 1408, S, 512)
+        weave_gated(1, 0, 640)
+        reuse(gathered[1, 0, 640], ((1280, 1408), (1408, S)))
+        for lo, hi in ((1280, 1408), (1408, S)):
+            for d in range(PACK):
+                gather_scalar(1, d, lo, hi)
+        weave_gated(1, 640, 1024)
+        quantise(1, 0, 512)
+        products(1, 0, 4)
+        weave_gated(1, 1024, 1280)
+        quantise(1, 512, 1024)
+        products(1, 4, 8)
+        weave_gated(1, 1280, 1408)
+        quantise(1, 1024, 1280)
+        products(1, 8, 10)
+        weave_gated(1, 1408, S)
+        quantise(1, 1280, 1408)
+        products(1, 10, 11)
+        quantise(1, 1408, S)
+        products(1, 11, 12)
+        for first, last in BANKS:
+            drain(first, last, "scalar" if first < 10 else "vector")
 
         one = keep.tile([P, T], F32, name="one")
         both = keep.tile([P, T], F32, name="both")
-        for lo, hi in ((0, 128), (128, 384), (384, 640), (640, T)):
+        nc.vector.tensor_copy(one[:, 0:128], dx[:].indirect(pos1_sb[:, 0:8]))
+        for lo, hi in ((128, 256), (256, 512), (512, T)):
             nc.scalar.activation(one[:, lo:hi], dx[:].indirect(pos1_sb[:, lo // 16 : hi // 16]), COPY)
+        for lo, hi in ((0, 256), (256, 512), (512, 640), (640, T)):
             nc.vector.tensor_tensor(both[:, lo:hi], dx[:].indirect(pos2_sb[:, lo // 16 : hi // 16]), one[:, lo:hi], ADD)
             if lo:
-                at = 0 if lo == 128 else lo
+                at = 0 if lo == 256 else lo
                 nc.sync.dma_start(out=out[:, at:hi], in_=both[:, at:hi])

@@ -1,6 +1,7 @@
 from contextlib import ExitStack
 
 import concourse.mybir as mybir
+from concourse.masks import make_identity
 
 F32 = mybir.dt.float32
 BF16 = mybir.dt.bfloat16
@@ -24,8 +25,8 @@ FLOPS = 2 * N * K * S
 BYTES = 4 * N * T + E * N * K // 2 + E * N * K // 32 + 4 * S + 2 * P * (S + 2 * T) // 16 + 4 * K * T
 
 BANKS = ((0, 4), (4, 8), (8, 10), (10, 11), (11, 12))
-WIDTHS = (880, T)
-RUN = 2
+WIDTHS = (784, T)
+RUN = 4
 
 
 def tile_moe_bdx_lin_none_kernel(tc, dyT, w_words, w_scales, gate, offs, pos1, pos2, out):
@@ -64,24 +65,34 @@ def tile_moe_bdx_lin_none_kernel(tc, dyT, w_words, w_scales, gate, offs, pos1, p
                 nc.sync.dma_start(out=ws_i32[32 * q : 32 * q + 4, :, :], in_=scale_rows[4 * q : 4 * q + 4, :, :])
 
         nc.vector.memset(ws_sb[:].rearrange("p g k -> p (g k)").bitcast(I32), 0)
-        zeros = keep.tile([P, 112], F32, name="zeros")
-        nc.gpsimd.memset(zeros[:], 0.0)
+        ident = keep.tile([P, P], F32, name="ident", align_bytes=64)
+        make_identity(nc, ident[:])
+        gate_cols = keep.tile([P, S // 512, 8], F32, name="gate_cols")
+        zeros = keep.tile([P, WIDTHS[0] - T], F32, name="zeros")
+        nc.vector.memset(zeros[:], 0.0)
         nc.scalar.activation(planes[0, 1][:, T:], zeros[:], COPY)
         for d in (2, 3):
-            nc.gpsimd.memset(planes[0, d][:, T:], 0.0)
+            nc.vector.memset(planes[0, d][:, T:], 0.0)
         load_plane(0, 0)
         nc.sync.dma_start(offs_sb[:], offs)
-        load_gate(864, 1152)
+        load_gate(768, 1152)
         load_gate(1152, S)
-        for d in range(1, PACK):
+        load_plane(0, 1)
+        nc.sync.dma_start(out=gate_cols[:, :, 0:RUN], in_=gate[0, :].rearrange("(b p i) -> p b i", p=P, i=RUN))
+        for d in range(2, PACK):
             load_plane(0, d)
         for d in range(PACK):
             load_plane(1, d)
-        load_gate(0, 864)
         load_words(0, E)
         load_scales()
         nc.sync.dma_start(pos1_sb[:], pos1)
         nc.sync.dma_start(pos2_sb[:], pos2)
+
+        gate_banks = [psum.tile([P, 512], F32, name=f"gate_bank_{b}") for b in range(S // 512)]
+        for b in range(S // 512):
+            for i in range(RUN):
+                nc.tensor.transpose(gate_banks[b][:, i * P : (i + 1) * P], gate_cols[:, b, i : i + 1].to_broadcast([P, P]), ident[:])
+
 
         gathered, rounded, codes, scales, banks = {}, {}, {}, {}, {}
         dx = keep.tile([P, S], F32, name="dx")
@@ -120,12 +131,24 @@ def tile_moe_bdx_lin_none_kernel(tc, dyT, w_words, w_scales, gate, offs, pos1, p
 
         def weave_gated(a, lo, hi):
             dst, src = views(a, lo, hi)
-            gates = gate_sb[:, lo:hi].rearrange("p (n i) -> p n i", i=RUN)
+            gates = gate_banks[lo // 512][:].rearrange("p (i n) -> p n i", i=RUN)[:, lo % 512 // RUN : (lo % 512 + hi - lo) // RUN, :]
             nc.vector.tensor_tensor(dst, src, gates.unsqueeze(2).to_broadcast([P, (hi - lo) // RUN, PACK, RUN]), MULT)
 
         def weave(a, lo, hi):
             dst, src = views(a, lo, hi)
             nc.vector.tensor_copy(dst, src)
+
+        def weave_gpsimd(a, lo, hi):
+            x, at = find(gathered, a, lo)
+            g, start = find(rounded, a, lo)
+            nc.gpsimd.tensor_scalar(
+                g[:, (lo - start) * PACK : (hi - start) * PACK].rearrange("p (s d) -> p s d", d=PACK),
+                x[:, :, lo - at : hi - at].rearrange("p d s -> p s d"),
+                1.0,
+                0.0,
+                MULT,
+                ADD,
+            )
 
         def quantise(a, lo, hi):
             g, start = find(rounded, a, lo)
@@ -174,37 +197,42 @@ def tile_moe_bdx_lin_none_kernel(tc, dyT, w_words, w_scales, gate, offs, pos1, p
                 gathered[1, lo, hi] = flat[:, at : at + PACK * (hi - lo)].rearrange("p (d s) -> p d s", d=PACK)
                 at = at + PACK * (hi - lo)
 
+
         place(0, 0, S, 0)
-        piece(0, 0, 864)
-        piece(0, 864, S)
-        piece(1, 0, 640)
-        gather_vector(0, 0, 0, 160)
+        piece(0, 0, 768)
+        piece(0, 768, S)
+        piece(1, 0, 512)
+        gather_vector(0, 0, 0, 128)
         for d in range(PACK):
-            gather_scalar(0, d, 0 if d else 160, 864)
-        gather_gated(0, 0, 864, 1152)
+            gather_scalar(0, d, 0 if d else 128, 768)
+        gather_gated(0, 0, 768, 1152)
         gather_gated(0, 0, 1152, S)
         for d in range(1, PACK):
-            gather_gated(0, d, 864, S)
-        weave(0, 864, S)
-        weave_gated(0, 0, 864)
-        reuse(gathered[0, 0, 864], ((640, 1024), (1024, 1280)))
-        for lo, hi in ((0, 640), (640, 1024), (1024, 1280)):
+            gather_gated(0, d, 768, S)
+        weave_gpsimd(0, 768, S)
+        weave_gated(0, 0, 512)
+        weave_gated(0, 512, 768)
+        reuse(gathered[0, 0, 768], ((512, 1024),))
+        reuse(gathered[0, 768, S], ((1024, 1280),))
+        for lo, hi in ((0, 512), (512, 1024), (1024, 1280)):
+            for d in range(PACK):
+                gather_scalar(1, d, lo, hi)
+        first = keep.tile([P, 512 * PACK], BF16, name="first", align_bytes=64)
+        rounded[1, 0, 512] = first
+        weave_gated(1, 0, 512)
+        reuse(gathered[1, 0, 512], ((1280, 1408), (1408, S)))
+        for lo, hi in ((1280, 1408), (1408, S)):
             for d in range(PACK):
                 gather_scalar(1, d, lo, hi)
         quantise(0, 0, 1024)
         quantise(0, 1024, S)
         products(0, 0, E)
-        place(1, 0, 1280, 0)
-        place(1, 1280, 1408, 0)
+        place(1, 512, 1280, 512)
+        rounded[1, 1280, 1408] = first[:, 0 : C * PACK]
         place(1, 1408, S, 512)
-        weave_gated(1, 0, 640)
-        reuse(gathered[1, 0, 640], ((1280, 1408), (1408, S)))
-        for lo, hi in ((1280, 1408), (1408, S)):
-            for d in range(PACK):
-                gather_scalar(1, d, lo, hi)
-        weave_gated(1, 640, 1024)
         quantise(1, 0, 512)
         products(1, 0, 4)
+        weave_gated(1, 512, 1024)
         weave_gated(1, 1024, 1280)
         quantise(1, 512, 1024)
         products(1, 4, 8)
@@ -216,8 +244,8 @@ def tile_moe_bdx_lin_none_kernel(tc, dyT, w_words, w_scales, gate, offs, pos1, p
         products(1, 10, 11)
         quantise(1, 1408, S)
         products(1, 11, 12)
-        for first, last in BANKS:
-            drain(first, last, "scalar" if first < 10 else "vector")
+        for low, high in BANKS:
+            drain(low, high, "scalar" if low < 10 else "vector")
 
         one = keep.tile([P, T], F32, name="one")
         both = keep.tile([P, T], F32, name="both")

@@ -25,7 +25,7 @@ FLOPS = 2 * N * K * S
 BYTES = 4 * N * T + E * N * K // 2 + E * N * K // 32 + 4 * S + 2 * P * (S + 2 * T) // 16 + 4 * K * T
 
 BANKS = ((0, 4), (4, 8), (8, 10), (10, 11), (11, 12))
-WIDTHS = (784, T)
+WIDTHS = (848, T)
 RUN = 4
 
 
@@ -67,32 +67,33 @@ def tile_moe_bdx_lin_none_kernel(tc, dyT, w_words, w_scales, gate, offs, pos1, p
         nc.vector.memset(ws_sb[:].rearrange("p g k -> p (g k)").bitcast(I32), 0)
         ident = keep.tile([P, P], F32, name="ident", align_bytes=64)
         make_identity(nc, ident[:])
-        gate_cols = keep.tile([P, S // 512, 8], F32, name="gate_cols")
         zeros = keep.tile([P, WIDTHS[0] - T], F32, name="zeros")
         nc.vector.memset(zeros[:], 0.0)
         nc.scalar.activation(planes[0, 1][:, T:], zeros[:], COPY)
         for d in (2, 3):
             nc.vector.memset(planes[0, d][:, T:], 0.0)
+        second = keep.tile([P, PACK, 512], F32, name="second")
         load_plane(0, 0)
         nc.sync.dma_start(offs_sb[:], offs)
-        load_gate(768, 1152)
-        load_gate(1152, S)
+        load_gate(0, 256)
         load_plane(0, 1)
-        nc.sync.dma_start(out=gate_cols[:, :, 0:RUN], in_=gate[0, :].rearrange("(b p i) -> p b i", p=P, i=RUN))
+        load_gate(256, 832)
         for d in range(2, PACK):
             load_plane(0, d)
         for d in range(PACK):
             load_plane(1, d)
-        load_words(0, E)
+        nc.sync.dma_start(out=second[:, 0 : S // 512, 0:RUN], in_=gate[0, :].rearrange("(b p i) -> p b i", p=P, i=RUN))
+        for first in range(0, E, 4):
+            load_words(first, first + 4)
         load_scales()
         nc.sync.dma_start(pos1_sb[:], pos1)
         nc.sync.dma_start(pos2_sb[:], pos2)
 
-        gate_banks = [psum.tile([P, 512], F32, name=f"gate_bank_{b}") for b in range(S // 512)]
-        for b in range(S // 512):
+        gate_banks = {}
+        for b in (1, 2, 0):
+            gate_banks[b] = psum.tile([P, 512], F32, name=f"gate_bank_{b}")
             for i in range(RUN):
-                nc.tensor.transpose(gate_banks[b][:, i * P : (i + 1) * P], gate_cols[:, b, i : i + 1].to_broadcast([P, P]), ident[:])
-
+                nc.tensor.transpose(gate_banks[b][:, i * P : (i + 1) * P], second[:, b, i : i + 1].to_broadcast([P, P]), ident[:])
 
         gathered, rounded, codes, scales, banks = {}, {}, {}, {}, {}
         dx = keep.tile([P, S], F32, name="dx")
@@ -150,6 +151,16 @@ def tile_moe_bdx_lin_none_kernel(tc, dyT, w_words, w_scales, gate, offs, pos1, p
                 ADD,
             )
 
+        def gate_gpsimd(a, lo, hi):
+            x, at = find(gathered, a, lo)
+            g, start = find(rounded, a, lo)
+            nc.gpsimd.tensor_tensor(
+                g[:, (lo - start) * PACK : (hi - start) * PACK].rearrange("p (s d) -> p s d", d=PACK),
+                x[:, :, lo - at : hi - at].rearrange("p d s -> p s d"),
+                gate_sb[:, lo:hi].unsqueeze(2).to_broadcast([P, hi - lo, PACK]),
+                MULT,
+            )
+
         def quantise(a, lo, hi):
             g, start = find(rounded, a, lo)
             codes[a, lo, hi] = keep.tile([P, hi - lo], U32, name=f"codes_{a}_{lo}", align_bytes=64)
@@ -199,43 +210,44 @@ def tile_moe_bdx_lin_none_kernel(tc, dyT, w_words, w_scales, gate, offs, pos1, p
 
 
         place(0, 0, S, 0)
-        piece(0, 0, 768)
-        piece(0, 768, S)
+        piece(0, 0, 832)
+        piece(0, 832, S)
         piece(1, 0, 512)
-        gather_vector(0, 0, 0, 128)
+        gather_vector(0, 0, 832, 1024)
         for d in range(PACK):
-            gather_scalar(0, d, 0 if d else 128, 768)
-        gather_gated(0, 0, 768, 1152)
-        gather_gated(0, 0, 1152, S)
-        for d in range(1, PACK):
-            gather_gated(0, d, 768, S)
-        weave_gpsimd(0, 768, S)
-        weave_gated(0, 0, 512)
-        weave_gated(0, 512, 768)
-        reuse(gathered[0, 0, 768], ((512, 1024),))
-        reuse(gathered[0, 768, S], ((1024, 1280),))
-        for lo, hi in ((0, 512), (512, 1024), (1024, 1280)):
+            gather_scalar(0, d, 832 if d else 1024, S)
+        for lo, hi in ((0, 256), (256, 832)):
+            for d in range(2):
+                gather_gated(0, d, lo, hi)
+        for d in range(2, PACK):
+            gather_gated(0, d, 0, 832)
+        weave_gpsimd(0, 0, 832)
+        weave_gated(0, 832, 1024)
+        weave_gated(0, 1024, S)
+        gathered[1, 512, 1024] = second
+        reuse(gathered[0, 832, S], ((1024, 1280), (1280, 1408), (1408, S)))
+        for lo, hi in ((0, 512), (512, 1024), (1024, 1280), (1280, 1408), (1408, S)):
             for d in range(PACK):
                 gather_scalar(1, d, lo, hi)
         first = keep.tile([P, 512 * PACK], BF16, name="first", align_bytes=64)
         rounded[1, 0, 512] = first
-        weave_gated(1, 0, 512)
-        reuse(gathered[1, 0, 512], ((1280, 1408), (1408, S)))
-        for lo, hi in ((1280, 1408), (1408, S)):
-            for d in range(PACK):
-                gather_scalar(1, d, lo, hi)
-        quantise(0, 0, 1024)
+        gate_gpsimd(1, 0, 128)
+        weave_gated(1, 128, 512)
         quantise(0, 1024, S)
-        products(0, 0, E)
-        place(1, 512, 1280, 512)
-        rounded[1, 1280, 1408] = first[:, 0 : C * PACK]
-        place(1, 1408, S, 512)
+        products(0, 8, E)
         quantise(1, 0, 512)
         products(1, 0, 4)
-        weave_gated(1, 512, 1024)
+        quantise(0, 0, 1024)
+        products(0, 0, 8)
+        place(1, 512, 1024, 896)
+        gate_gpsimd(1, 512, 640)
+        weave_gated(1, 640, 1024)
+        place(1, 1024, 1280, 512)
         weave_gated(1, 1024, 1280)
         quantise(1, 512, 1024)
         products(1, 4, 8)
+        rounded[1, 1280, 1408] = first[:, 0 : C * PACK]
+        place(1, 1408, S, 896)
         weave_gated(1, 1280, 1408)
         quantise(1, 1024, 1280)
         products(1, 8, 10)
@@ -245,7 +257,7 @@ def tile_moe_bdx_lin_none_kernel(tc, dyT, w_words, w_scales, gate, offs, pos1, p
         quantise(1, 1408, S)
         products(1, 11, 12)
         for low, high in BANKS:
-            drain(low, high, "scalar" if low < 10 else "vector")
+            drain(low, high, "scalar" if low < 11 else "vector")
 
         one = keep.tile([P, T], F32, name="one")
         both = keep.tile([P, T], F32, name="both")

@@ -257,7 +257,7 @@ def tile_moe_bdx_lin_none_kernel(tc, dyT, w_words, w_scales, gate, offs, pos1, p
         quantise(1, 1408, S)
         products(1, 11, 12)
         for low, high in BANKS:
-            drain(low, high, "scalar" if low < 11 else "vector")
+            drain(low, high, "scalar")
 
         one = keep.tile([P, T], F32, name="one")
         both = keep.tile([P, T], F32, name="both")

@@ -64,7 +64,6 @@ def tile_moe_bdx_lin_none_kernel(tc, dyT, w_words, w_scales, gate, offs, pos1, p
             for q in range(4):
                 nc.sync.dma_start(out=ws_i32[32 * q : 32 * q + 4, :, :], in_=scale_rows[4 * q : 4 * q + 4, :, :])
 
-        nc.vector.memset(ws_sb[:].rearrange("p g k -> p (g k)").bitcast(I32), 0)
         ident = keep.tile([P, P], F32, name="ident", align_bytes=64)
         make_identity(nc, ident[:])
         zeros = keep.tile([P, WIDTHS[0] - T], F32, name="zeros")
@@ -72,7 +71,8 @@ def tile_moe_bdx_lin_none_kernel(tc, dyT, w_words, w_scales, gate, offs, pos1, p
         nc.scalar.activation(planes[0, 1][:, T:], zeros[:], COPY)
         for d in (2, 3):
             nc.vector.memset(planes[0, d][:, T:], 0.0)
-        second = keep.tile([P, PACK, 512], F32, name="second")
+        nc.vector.memset(ws_sb[:].rearrange("p g k -> p (g k)").bitcast(I32), 0)
+        second = keep.tile([P, PACK, 384], F32, name="second")
         load_plane(0, 0)
         nc.sync.dma_start(offs_sb[:], offs)
         load_gate(0, 256)
@@ -83,8 +83,9 @@ def tile_moe_bdx_lin_none_kernel(tc, dyT, w_words, w_scales, gate, offs, pos1, p
         for d in range(PACK):
             load_plane(1, d)
         nc.sync.dma_start(out=second[:, 0 : S // 512, 0:RUN], in_=gate[0, :].rearrange("(b p i) -> p b i", p=P, i=RUN))
-        for first in range(0, E, 4):
-            load_words(first, first + 4)
+        load_gate(1280, 1408)
+        for first in range(0, E, 6):
+            load_words(first, first + 6)
         load_scales()
         nc.sync.dma_start(pos1_sb[:], pos1)
         nc.sync.dma_start(pos2_sb[:], pos2)
@@ -195,7 +196,7 @@ def tile_moe_bdx_lin_none_kernel(tc, dyT, w_words, w_scales, gate, offs, pos1, p
             else:
                 nc.vector.tensor_copy(dx[:, first * C : last * C], banks[first][0][:, 0 : (last - first) * C])
 
-        woven = keep.tile([P, S * PACK], BF16, name="woven", align_bytes=64)
+        woven = keep.tile([P, (C + S) * PACK], BF16, name="woven", align_bytes=64)
 
 
         def place(a, lo, hi, at):
@@ -209,10 +210,10 @@ def tile_moe_bdx_lin_none_kernel(tc, dyT, w_words, w_scales, gate, offs, pos1, p
                 at = at + PACK * (hi - lo)
 
 
-        place(0, 0, S, 0)
+        place(0, 0, S, C)
         piece(0, 0, 832)
         piece(0, 832, S)
-        piece(1, 0, 512)
+        piece(1, 0, 640)
         gather_vector(0, 0, 832, 1024)
         for d in range(PACK):
             gather_scalar(0, d, 832 if d else 1024, S)
@@ -224,40 +225,37 @@ def tile_moe_bdx_lin_none_kernel(tc, dyT, w_words, w_scales, gate, offs, pos1, p
         weave_gpsimd(0, 0, 832)
         weave_gated(0, 832, 1024)
         weave_gated(0, 1024, S)
-        gathered[1, 512, 1024] = second
-        reuse(gathered[0, 832, S], ((1024, 1280), (1280, 1408), (1408, S)))
-        for lo, hi in ((0, 512), (512, 1024), (1024, 1280), (1280, 1408), (1408, S)):
+        gathered[1, 640, 1024] = second
+        reuse(gathered[0, 832, S], ((1024, 1408), (1408, S)))
+        for lo, hi in ((0, 640), (640, 1024), (1024, 1408), (1408, S)):
             for d in range(PACK):
                 gather_scalar(1, d, lo, hi)
         first = keep.tile([P, 512 * PACK], BF16, name="first", align_bytes=64)
         rounded[1, 0, 512] = first
-        gate_gpsimd(1, 0, 128)
-        weave_gated(1, 128, 512)
-        quantise(0, 1024, S)
-        products(0, 8, E)
-        quantise(1, 0, 512)
-        products(1, 0, 4)
+        place(1, 512, 1024, 0)
+        gate_gpsimd(1, 512, 640)
+        weave_gated(1, 0, 512)
+
         quantise(0, 0, 1024)
         products(0, 0, 8)
-        place(1, 512, 1024, 896)
-        gate_gpsimd(1, 512, 640)
-        weave_gated(1, 640, 1024)
-        place(1, 1024, 1280, 512)
-        weave_gated(1, 1024, 1280)
+        quantise(0, 1024, S)
+        products(0, 8, E)
+        gate_gpsimd(1, 640, 720)
+        weave_gated(1, 720, 1024)
+        quantise(1, 0, 512)
+        products(1, 0, 4)
         quantise(1, 512, 1024)
         products(1, 4, 8)
-        rounded[1, 1280, 1408] = first[:, 0 : C * PACK]
-        place(1, 1408, S, 896)
-        weave_gated(1, 1280, 1408)
-        quantise(1, 1024, 1280)
-        products(1, 8, 10)
+        rounded[1, 1024, S] = first
+        gate_gpsimd(1, 1280, 1408)
+        weave_gated(1, 1024, 1280)
         weave_gated(1, 1408, S)
-        quantise(1, 1280, 1408)
-        products(1, 10, 11)
+        quantise(1, 1024, 1408)
+        products(1, 8, 11)
         quantise(1, 1408, S)
         products(1, 11, 12)
         for low, high in BANKS:
-            drain(low, high, "scalar")
+            drain(low, high, "vector" if low == 8 else "scalar")
 
         one = keep.tile([P, T], F32, name="one")
         both = keep.tile([P, T], F32, name="both")

@@ -66,26 +66,30 @@ def tile_moe_bdx_lin_none_kernel(tc, dyT, w_words, w_scales, gate, offs, pos1, p
 
         ident = keep.tile([P, P], F32, name="ident", align_bytes=64)
         make_identity(nc, ident[:])
-        zeros = keep.tile([P, WIDTHS[0] - T], F32, name="zeros")
-        nc.vector.memset(zeros[:], 0.0)
-        nc.scalar.activation(planes[0, 1][:, T:], zeros[:], COPY)
+        nc.any.memset(planes[0, 1][:, T:], 0.0)
         for d in (2, 3):
             nc.vector.memset(planes[0, d][:, T:], 0.0)
         nc.vector.memset(ws_sb[:].rearrange("p g k -> p (g k)").bitcast(I32), 0)
         second = keep.tile([P, PACK, 384], F32, name="second")
+        by_bank = gate[0, :].rearrange("(b p i) -> p b i", p=P, i=RUN)
+        middle = keep.tile([P, 8], F32, name="middle")
+        outer = second[:].rearrange("p d s -> p (d s)")[:, 0 : 2 * 766].rearrange("p (b s) -> p b s", b=2)[:, :, 0:RUN]
+        columns = {0: outer[:, 0, :], 1: middle, 2: outer[:, 1, :]}
         load_plane(0, 0)
         nc.sync.dma_start(offs_sb[:], offs)
-        load_gate(0, 256)
+        load_gate(0, 384)
         load_plane(0, 1)
-        load_gate(256, 832)
-        for d in range(2, PACK):
-            load_plane(0, d)
-        for d in range(PACK):
-            load_plane(1, d)
-        nc.sync.dma_start(out=second[:, 0 : S // 512, 0:RUN], in_=gate[0, :].rearrange("(b p i) -> p b i", p=P, i=RUN))
+        load_plane(0, 2)
+        load_gate(384, 832)
+        load_plane(0, 3)
+        nc.sync.dma_start(out=middle[:, 0:RUN], in_=by_bank[:, 1, :])
+        load_plane(1, 0)
+        load_plane(1, 1)
+        load_plane(1, 2)
+        load_plane(1, 3)
+        nc.sync.dma_start(out=outer, in_=by_bank[:, 0:3:2, :])
         load_gate(1280, 1408)
-        for first in range(0, E, 6):
-            load_words(first, first + 6)
+        load_words(0, E)
         load_scales()
         nc.sync.dma_start(pos1_sb[:], pos1)
         nc.sync.dma_start(pos2_sb[:], pos2)
@@ -94,7 +98,7 @@ def tile_moe_bdx_lin_none_kernel(tc, dyT, w_words, w_scales, gate, offs, pos1, p
         for b in (1, 2, 0):
             gate_banks[b] = psum.tile([P, 512], F32, name=f"gate_bank_{b}")
             for i in range(RUN):
-                nc.tensor.transpose(gate_banks[b][:, i * P : (i + 1) * P], second[:, b, i : i + 1].to_broadcast([P, P]), ident[:])
+                nc.tensor.transpose(gate_banks[b][:, i * P : (i + 1) * P], columns[b][:, i : i + 1].to_broadcast([P, P]), ident[:])
 
         gathered, rounded, codes, scales, banks = {}, {}, {}, {}, {}
         dx = keep.tile([P, S], F32, name="dx")
@@ -172,6 +176,17 @@ def tile_moe_bdx_lin_none_kernel(tc, dyT, w_words, w_scales, gate, offs, pos1, p
                 in_=g[:, (lo - start) * PACK : (hi - start) * PACK],
             )
 
+        def quantise_parts(parts, values):
+            width = sum(hi - lo for a, lo, hi in parts)
+            made = keep.tile([P, width], U32, name=f"codes_{parts[0][0]}_{parts[0][1]}", align_bytes=64)
+            plane = keep.tile([P, width], U8, name=f"scales_{parts[0][0]}_{parts[0][1]}", align_bytes=64)
+            nc.vector.quantize_mx(out=made[:].bitcast(FP8X4), scales=plane[:], in_=values)
+            at = 0
+            for a, lo, hi in parts:
+                codes[a, lo, hi] = made[:, at : at + hi - lo]
+                scales[a, lo, hi] = plane[:, at : at + hi - lo]
+                at = at + hi - lo
+
         def products(a, first, last):
             for e in range(first, last):
                 low, high = [group for group in BANKS if group[0] <= e < group[1]][0]
@@ -196,7 +211,7 @@ def tile_moe_bdx_lin_none_kernel(tc, dyT, w_words, w_scales, gate, offs, pos1, p
             else:
                 nc.vector.tensor_copy(dx[:, first * C : last * C], banks[first][0][:, 0 : (last - first) * C])
 
-        woven = keep.tile([P, (C + S) * PACK], BF16, name="woven", align_bytes=64)
+        woven = keep.tile([P, (512 + S + 512 - 80) * PACK], BF16, name="woven", align_bytes=64)
 
 
         def place(a, lo, hi, at):
@@ -210,18 +225,17 @@ def tile_moe_bdx_lin_none_kernel(tc, dyT, w_words, w_scales, gate, offs, pos1, p
                 at = at + PACK * (hi - lo)
 
 
-        place(0, 0, S, C)
+        place(0, 0, S, 512)
         piece(0, 0, 832)
         piece(0, 832, S)
         piece(1, 0, 640)
-        gather_vector(0, 0, 832, 1024)
+        gather_vector(0, 0, 832, 960)
         for d in range(PACK):
-            gather_scalar(0, d, 832 if d else 1024, S)
-        for lo, hi in ((0, 256), (256, 832)):
-            for d in range(2):
+            gather_scalar(0, d, 832 if d else 960, S)
+        for lo, hi in ((0, 384), (384, 832)):
+            for d in range(PACK - 1):
                 gather_gated(0, d, lo, hi)
-        for d in range(2, PACK):
-            gather_gated(0, d, 0, 832)
+        gather_gated(0, PACK - 1, 0, 832)
         weave_gpsimd(0, 0, 832)
         weave_gated(0, 832, 1024)
         weave_gated(0, 1024, S)
@@ -230,23 +244,22 @@ def tile_moe_bdx_lin_none_kernel(tc, dyT, w_words, w_scales, gate, offs, pos1, p
         for lo, hi in ((0, 640), (640, 1024), (1024, 1408), (1408, S)):
             for d in range(PACK):
                 gather_scalar(1, d, lo, hi)
-        first = keep.tile([P, 512 * PACK], BF16, name="first", align_bytes=64)
-        rounded[1, 0, 512] = first
-        place(1, 512, 1024, 0)
+        place(1, 0, 512, 0)
+        tail = 512 + S - 80
+        place(1, 640, 1024, tail)
+        place(1, 512, 640, tail + 384)
         gate_gpsimd(1, 512, 640)
         weave_gated(1, 0, 512)
-
-        quantise(0, 0, 1024)
-        products(0, 0, 8)
-        quantise(0, 1024, S)
-        products(0, 8, E)
+        quantise(0, 512, S)
+        products(0, 4, E)
         gate_gpsimd(1, 640, 720)
         weave_gated(1, 720, 1024)
-        quantise(1, 0, 512)
+        quantise_parts(((1, 0, 512), (0, 0, 512)), woven[:, 0 : 1024 * PACK])
         products(1, 0, 4)
-        quantise(1, 512, 1024)
+        products(0, 0, 4)
+        quantise_parts(((1, 640, 1024), (1, 512, 640)), woven[:, tail * PACK :])
         products(1, 4, 8)
-        rounded[1, 1024, S] = first
+        rounded[1, 1024, S] = woven[:, 0 : 512 * PACK]
         gate_gpsimd(1, 1280, 1408)
         weave_gated(1, 1024, 1280)
         weave_gated(1, 1408, S)
@@ -262,8 +275,8 @@ def tile_moe_bdx_lin_none_kernel(tc, dyT, w_words, w_scales, gate, offs, pos1, p
         nc.vector.tensor_copy(one[:, 0:128], dx[:].indirect(pos1_sb[:, 0:8]))
         for lo, hi in ((128, 256), (256, 512), (512, T)):
             nc.scalar.activation(one[:, lo:hi], dx[:].indirect(pos1_sb[:, lo // 16 : hi // 16]), COPY)
-        for lo, hi in ((0, 256), (256, 512), (512, 640), (640, T)):
+        for lo, hi in ((128, 256), (0, 128), (256, 512), (512, 640), (640, T)):
             nc.vector.tensor_tensor(both[:, lo:hi], dx[:].indirect(pos2_sb[:, lo // 16 : hi // 16]), one[:, lo:hi], ADD)
-            if lo:
+            if lo >= 256:
                 at = 0 if lo == 256 else lo
                 nc.sync.dma_start(out=out[:, at:hi], in_=both[:, at:hi])

@@ -25,7 +25,7 @@ FLOPS = 2 * N * K * S
 BYTES = 4 * N * T + E * N * K // 2 + E * N * K // 32 + 4 * S + 2 * P * (S + 2 * T) // 16 + 4 * K * T
 
 BANKS = ((0, 4), (4, 8), (8, 10), (10, 11), (11, 12))
-WIDTHS = (848, T)
+WIDTHS = (912, T)
 RUN = 4
 
 
@@ -80,7 +80,7 @@ def tile_moe_bdx_lin_none_kernel(tc, dyT, w_words, w_scales, gate, offs, pos1, p
         load_gate(0, 384)
         load_plane(0, 1)
         load_plane(0, 2)
-        load_gate(384, 832)
+        load_gate(384, 896)
         load_plane(0, 3)
         nc.sync.dma_start(out=middle[:, 0:RUN], in_=by_bank[:, 1, :])
         load_plane(1, 0)
@@ -226,21 +226,21 @@ def tile_moe_bdx_lin_none_kernel(tc, dyT, w_words, w_scales, gate, offs, pos1, p
 
 
         place(0, 0, S, 512)
-        piece(0, 0, 832)
-        piece(0, 832, S)
+        piece(0, 0, 896)
+        piece(0, 896, S)
         piece(1, 0, 640)
-        gather_vector(0, 0, 832, 960)
+        gather_vector(0, 0, 896, 1024)
         for d in range(PACK):
-            gather_scalar(0, d, 832 if d else 960, S)
-        for lo, hi in ((0, 384), (384, 832)):
+            gather_scalar(0, d, 896 if d else 1024, S)
+        for lo, hi in ((0, 384), (384, 896)):
             for d in range(PACK - 1):
                 gather_gated(0, d, lo, hi)
-        gather_gated(0, PACK - 1, 0, 832)
-        weave_gpsimd(0, 0, 832)
-        weave_gated(0, 832, 1024)
+        gather_gated(0, PACK - 1, 0, 896)
+        weave_gpsimd(0, 0, 896)
+        weave_gated(0, 896, 1024)
         weave_gated(0, 1024, S)
         gathered[1, 640, 1024] = second
-        reuse(gathered[0, 832, S], ((1024, 1408), (1408, S)))
+        reuse(gathered[0, 896, S], ((1024, 1408), (1408, S)))
         for lo, hi in ((0, 640), (640, 1024), (1024, 1408), (1408, S)):
             for d in range(PACK):
                 gather_scalar(1, d, lo, hi)

@@ -20,13 +20,19 @@ K, T, E, C, N = 128, 768, 12, 128, 1024
 S = E * C
 PASSES = N // 512
 PACK = 4
+BANK = 512
 
 FLOPS = 2 * N * K * S
 BYTES = 4 * N * T + E * N * K // 2 + E * N * K // 32 + 4 * S + 2 * P * (S + 2 * T) // 16 + 4 * K * T
 
-BANKS = ((0, 4), (4, 8), (8, 10), (10, 11), (11, 12))
-WIDTHS = (912, T)
-RUN = 4
+SPLIT = 576
+HELP = 128
+EARLY = 384
+SHARES = (32, 96, 128)
+WIDE = S - SPLIT + 16
+FOUR = 4
+RUN = 2
+GROUPS = ((0, 4), (4, 8), (8, 10), (10, 11), (11, 12))
 
 
 def tile_moe_bdx_lin_none_kernel(tc, dyT, w_words, w_scales, gate, offs, pos1, pos2, out):
@@ -43,13 +49,22 @@ def tile_moe_bdx_lin_none_kernel(tc, dyT, w_words, w_scales, gate, offs, pos1, p
         w_sb = keep.tile([P, E * PASSES, 2 * K], U8, name="w_sb", align_bytes=64)
         ws_sb = keep.tile([P, E * PASSES, K], U8, name="ws_sb", align_bytes=64)
         gate_sb = keep.tile([P, S], F32, name="gate_sb")
-        planes = {(a, d): keep.tile([P, WIDTHS[a] if d else T], F32, name=f"plane_{a}_{d}") for a in range(PASSES) for d in range(PACK)}
+        planes = {
+            (a, d): keep.tile([P, WIDE if a == 0 and d else T], F32, name=f"plane_{a}_{d}")
+            for a in range(PASSES)
+            for d in range(PACK)
+        }
+        cuts = (0, BANK + SHARES[0], 2 * BANK, S - C, S)
+        second = keep.tile([P, PACK * (cuts[2] - cuts[1])], F32, name="second")
+
+        ident = keep.tile([P, P], F32, name="ident", align_bytes=64)
+        make_identity(nc, ident[:])
+        for d in (3, 2):
+            nc.vector.memset(planes[0, d][:, T:], 0.0)
+        nc.scalar.activation(planes[0, 1][:, T:], planes[0, 3][:, T:], COPY)
+        nc.vector.memset(ws_sb[:].rearrange("p g k -> p (g k)").bitcast(I32), 0)
 
         rows = dyT.rearrange("(a p d) t -> a d p t", a=PASSES, d=PACK)
-        words = w_words.bitcast(I32).rearrange("e a p n -> p (e a) n")
-        w_i32 = w_sb[:].bitcast(I32)
-        scale_rows = w_scales.bitcast(I32).rearrange("e a f k -> f (e a) k")
-        ws_i32 = ws_sb[:].bitcast(I32)
 
         def load_plane(a, d):
             nc.sync.dma_start(out=planes[a, d][:, 0:T], in_=rows[a, d])
@@ -57,126 +72,79 @@ def tile_moe_bdx_lin_none_kernel(tc, dyT, w_words, w_scales, gate, offs, pos1, p
         def load_gate(lo, hi):
             nc.sync.dma_start(out=gate_sb[:, lo:hi], in_=gate[0:P, lo:hi])
 
-        def load_words(first, last):
-            nc.sync.dma_start(out=w_i32[:, PASSES * first : PASSES * last, :], in_=words[:, PASSES * first : PASSES * last, :])
+        by_bank = gate[0, :].rearrange("(b p i) -> p b i", p=P, i=FOUR)
+        early = keep.tile([P, 2, 8], F32, name="early")
+        astride = 2 * (cuts[2] - cuts[1]) - FOUR // 2
+        late = second[:, astride : astride + FOUR]
+        columns = {0: early[:, 0, :], 1: early[:, 1, :], 2: late}
+        nc.scalar.dma_start(out=early[:, :, 0:FOUR], in_=by_bank[:, 0:2, :])
 
-        def load_scales():
-            for q in range(4):
-                nc.sync.dma_start(out=ws_i32[32 * q : 32 * q + 4, :, :], in_=scale_rows[4 * q : 4 * q + 4, :, :])
-
-        ident = keep.tile([P, P], F32, name="ident", align_bytes=64)
-        make_identity(nc, ident[:])
-        nc.any.memset(planes[0, 1][:, T:], 0.0)
-        for d in (2, 3):
-            nc.vector.memset(planes[0, d][:, T:], 0.0)
-        nc.vector.memset(ws_sb[:].rearrange("p g k -> p (g k)").bitcast(I32), 0)
-        second = keep.tile([P, PACK, 384], F32, name="second")
-        by_bank = gate[0, :].rearrange("(b p i) -> p b i", p=P, i=RUN)
-        middle = keep.tile([P, 8], F32, name="middle")
-        outer = second[:].rearrange("p d s -> p (d s)")[:, 0 : 2 * 766].rearrange("p (b s) -> p b s", b=2)[:, :, 0:RUN]
-        columns = {0: outer[:, 0, :], 1: middle, 2: outer[:, 1, :]}
         load_plane(0, 0)
         nc.sync.dma_start(offs_sb[:], offs)
-        load_gate(0, 384)
+        load_gate(SPLIT, SPLIT + EARLY)
         load_plane(0, 1)
         load_plane(0, 2)
-        load_gate(384, 896)
+        load_gate(SPLIT + EARLY, S)
         load_plane(0, 3)
-        nc.sync.dma_start(out=middle[:, 0:RUN], in_=by_bank[:, 1, :])
-        load_plane(1, 0)
-        load_plane(1, 1)
-        load_plane(1, 2)
-        load_plane(1, 3)
-        nc.sync.dma_start(out=outer, in_=by_bank[:, 0:3:2, :])
-        load_gate(1280, 1408)
-        load_words(0, E)
-        load_scales()
+        for d in range(PACK):
+            load_plane(1, d)
+        nc.sync.dma_start(out=late, in_=by_bank[:, 2, :])
+        load_gate(BANK, cuts[1])
+        nc.sync.dma_start(out=w_sb[:].bitcast(I32), in_=w_words.bitcast(I32).rearrange("e a p n -> p (e a) n"))
+        scale_rows = w_scales.bitcast(I32).rearrange("e a f k -> f (e a) k")
+        for q in range(4):
+            nc.sync.dma_start(out=ws_sb[:].bitcast(I32)[32 * q : 32 * q + 4], in_=scale_rows[4 * q : 4 * q + 4])
         nc.sync.dma_start(pos1_sb[:], pos1)
         nc.sync.dma_start(pos2_sb[:], pos2)
 
         gate_banks = {}
-        for b in (1, 2, 0):
-            gate_banks[b] = psum.tile([P, 512], F32, name=f"gate_bank_{b}")
-            for i in range(RUN):
-                nc.tensor.transpose(gate_banks[b][:, i * P : (i + 1) * P], columns[b][:, i : i + 1].to_broadcast([P, P]), ident[:])
+        for b in (1, 0, 2):
+            gate_banks[b] = psum.tile([P, BANK], F32, name=f"gate_bank_{b}")
+            for i in range(FOUR):
+                nc.tensor.transpose(
+                    gate_banks[b][:, i::FOUR], columns[b][:, i : i + 1].to_broadcast([P, P]), ident[:]
+                )
 
         gathered, rounded, codes, scales, banks = {}, {}, {}, {}, {}
         dx = keep.tile([P, S], F32, name="dx")
 
-        def find(table, a, lo):
-            return [(tile, at) for (b, at, end), tile in table.items() if b == a and at <= lo < end][0]
+        def part(table, a, lo, hi, each=1):
+            first = [at for b, at, end in table if b == a and at <= lo < end][0]
+            whole = [ap for (b, at, end), ap in table.items() if b == a and at == first][0]
+            cut = slice((lo - first) * each, (hi - first) * each)
+            return whole[:, cut] if whole.ndim == 2 else whole[:, :, cut]
+
+        def by_plane(flat):
+            return flat.rearrange("p (d s) -> p d s", d=PACK)
 
         def window(a, d, lo, hi):
             return planes[a, d][:].indirect(offs_sb[:, lo // 16 : hi // 16])
 
-        def piece(a, lo, hi):
-            gathered[a, lo, hi] = keep.tile([P, PACK, hi - lo], F32, name=f"x_{a}_{lo}")
-
-        def block(a, lo, hi):
-            rounded[a, lo, hi] = keep.tile([P, (hi - lo) * PACK], BF16, name=f"g_{a}_{lo}", align_bytes=64)
-
-        def into(a, d, lo, hi):
-            x, at = find(gathered, a, lo)
-            return x[:, d, lo - at : hi - at]
-
         def gather_scalar(a, d, lo, hi):
-            nc.scalar.activation(into(a, d, lo, hi), window(a, d, lo, hi), COPY)
+            nc.scalar.activation(part(gathered, a, lo, hi)[:, d, :], window(a, d, lo, hi), COPY)
 
-        def gather_vector(a, d, lo, hi):
-            nc.vector.tensor_copy(into(a, d, lo, hi), window(a, d, lo, hi))
+        def gather_gated(d, lo, hi):
+            nc.vector.tensor_tensor(part(gathered, 0, lo, hi)[:, d, :], window(0, d, lo, hi), gate_sb[:, lo:hi], MULT)
 
-        def gather_gated(a, d, lo, hi):
-            nc.vector.tensor_tensor(into(a, d, lo, hi), window(a, d, lo, hi), gate_sb[:, lo:hi], MULT)
-
-        def views(a, lo, hi):
-            x, at = find(gathered, a, lo)
-            g, start = find(rounded, a, lo)
-            src = x[:, :, lo - at : hi - at].rearrange("p d (n i) -> p n d i", i=RUN)
-            dst = g[:, (lo - start) * PACK : (hi - start) * PACK].rearrange("p (n i d) -> p n d i", i=RUN, d=PACK)
-            return dst, src
-
-        def weave_gated(a, lo, hi):
-            dst, src = views(a, lo, hi)
-            gates = gate_banks[lo // 512][:].rearrange("p (i n) -> p n i", i=RUN)[:, lo % 512 // RUN : (lo % 512 + hi - lo) // RUN, :]
-            nc.vector.tensor_tensor(dst, src, gates.unsqueeze(2).to_broadcast([P, (hi - lo) // RUN, PACK, RUN]), MULT)
-
-        def weave(a, lo, hi):
-            dst, src = views(a, lo, hi)
-            nc.vector.tensor_copy(dst, src)
-
-        def weave_gpsimd(a, lo, hi):
-            x, at = find(gathered, a, lo)
-            g, start = find(rounded, a, lo)
-            nc.gpsimd.tensor_scalar(
-                g[:, (lo - start) * PACK : (hi - start) * PACK].rearrange("p (s d) -> p s d", d=PACK),
-                x[:, :, lo - at : hi - at].rearrange("p d s -> p s d"),
-                1.0,
-                0.0,
-                MULT,
-                ADD,
-            )
-
-        def gate_gpsimd(a, lo, hi):
-            x, at = find(gathered, a, lo)
-            g, start = find(rounded, a, lo)
-            nc.gpsimd.tensor_tensor(
-                g[:, (lo - start) * PACK : (hi - start) * PACK].rearrange("p (s d) -> p s d", d=PACK),
-                x[:, :, lo - at : hi - at].rearrange("p d s -> p s d"),
-                gate_sb[:, lo:hi].unsqueeze(2).to_broadcast([P, hi - lo, PACK]),
+        def weave_vector(a, lo, hi):
+            runs = slice(lo % BANK // RUN, (lo % BANK + hi - lo) // RUN)
+            gates = gate_banks[lo // BANK][:].rearrange("p (n i) -> p n i", i=RUN)[:, runs, :]
+            nc.vector.tensor_tensor(
+                part(rounded, a, lo, hi, PACK).rearrange("p (n i d) -> p n d i", i=RUN, d=PACK),
+                part(gathered, a, lo, hi).rearrange("p d (n i) -> p n d i", i=RUN),
+                gates.unsqueeze(2).to_broadcast([P, (hi - lo) // RUN, PACK, RUN]),
                 MULT,
             )
 
-        def quantise(a, lo, hi):
-            g, start = find(rounded, a, lo)
-            codes[a, lo, hi] = keep.tile([P, hi - lo], U32, name=f"codes_{a}_{lo}", align_bytes=64)
-            scales[a, lo, hi] = keep.tile([P, hi - lo], U8, name=f"scales_{a}_{lo}", align_bytes=64)
-            nc.vector.quantize_mx(
-                out=codes[a, lo, hi][:].bitcast(FP8X4),
-                scales=scales[a, lo, hi][:],
-                in_=g[:, (lo - start) * PACK : (hi - start) * PACK],
-            )
+        def weave_gpsimd(a, lo, hi, gated):
+            into = part(rounded, a, lo, hi, PACK).rearrange("p (s d) -> p s d", d=PACK)
+            values = part(gathered, a, lo, hi).rearrange("p d s -> p s d")
+            if gated:
+                nc.gpsimd.tensor_scalar(into, values, 1.0, 0.0, MULT, ADD)
+            else:
+                nc.gpsimd.tensor_tensor(into, values, gate_sb[:, lo:hi].unsqueeze(2).to_broadcast([P, hi - lo, PACK]), MULT)
 
-        def quantise_parts(parts, values):
+        def quantise(values, *parts):
             width = sum(hi - lo for a, lo, hi in parts)
             made = keep.tile([P, width], U32, name=f"codes_{parts[0][0]}_{parts[0][1]}", align_bytes=64)
             plane = keep.tile([P, width], U8, name=f"scales_{parts[0][0]}_{parts[0][1]}", align_bytes=64)
@@ -186,89 +154,78 @@ def tile_moe_bdx_lin_none_kernel(tc, dyT, w_words, w_scales, gate, offs, pos1, p
                 codes[a, lo, hi] = made[:, at : at + hi - lo]
                 scales[a, lo, hi] = plane[:, at : at + hi - lo]
                 at = at + hi - lo
+                for e in range(lo // C, hi // C):
+                    multiply(a, e)
 
-        def products(a, first, last):
-            for e in range(first, last):
-                low, high = [group for group in BANKS if group[0] <= e < group[1]][0]
-                if low not in banks:
-                    banks[low] = [psum.tile([P, 512], F32, name=f"bank_{low}"), 0]
-                made, at = find(codes, a, e * C)
-                plane, at = find(scales, a, e * C)
-                nc.tensor.matmul_mx(
-                    out=banks[low][0][:, (e - low) * C : (e - low + 1) * C],
-                    lhsT=w_sb[:, PASSES * e + a, :].bitcast(FP4X4),
-                    lhsT_scale=ws_sb[:, PASSES * e + a, :],
-                    rhs=made[:, e * C - at : (e + 1) * C - at].bitcast(FP8X4),
-                    rhs_scale=plane[:, e * C - at : (e + 1) * C - at],
-                    start=banks[low][1] == 0,
-                    stop=banks[low][1] == PASSES * (high - low) - 1,
-                )
-                banks[low][1] = banks[low][1] + 1
+        done = []
 
-        def drain(first, last, engine):
-            if engine == "scalar":
-                nc.scalar.copy(dx[:, first * C : last * C], banks[first][0][:, 0 : (last - first) * C])
-            else:
-                nc.vector.tensor_copy(dx[:, first * C : last * C], banks[first][0][:, 0 : (last - first) * C])
+        def multiply(a, e):
+            low, high = [group for group in GROUPS if group[0] <= e < group[1]][0]
+            before = len([other for other in done if low <= other < high])
+            if before == 0:
+                banks[low] = psum.tile([P, BANK], F32, name=f"bank_{low}")
+            nc.tensor.matmul_mx(
+                out=banks[low][:, (e - low) * C : (e - low + 1) * C],
+                lhsT=w_sb[:, PASSES * e + a, :].bitcast(FP4X4),
+                lhsT_scale=ws_sb[:, PASSES * e + a, :],
+                rhs=part(codes, a, e * C, (e + 1) * C).bitcast(FP8X4),
+                rhs_scale=part(scales, a, e * C, (e + 1) * C),
+                start=before == 0,
+                stop=before == PASSES * (high - low) - 1,
+            )
+            done.append(e)
 
-        woven = keep.tile([P, (512 + S + 512 - 80) * PACK], BF16, name="woven", align_bytes=64)
+        lead = BANK - SHARES[1]
+        woven = keep.tile([P, (lead + S + BANK) * PACK], BF16, name="woven", align_bytes=64)
 
+        def woven_at(at, width):
+            return woven[:, at * PACK : (at + width) * PACK]
 
-        def place(a, lo, hi, at):
-            rounded[a, lo, hi] = woven[:, at * PACK : (at + hi - lo) * PACK]
+        rounded[0, 0, S] = woven_at(lead, S)
+        rounded[1, 0, BANK] = woven_at(lead + S, BANK)
+        rounded[1, BANK, 2 * BANK] = woven_at(0, BANK)
+        rounded[1, 2 * BANK, S] = woven_at(lead + S, BANK)
 
+        plain = keep.tile([P, PACK * SPLIT], F32, name="plain")
+        gated = keep.tile([P, PACK * (S - SPLIT)], F32, name="gated")
+        first = keep.tile([P, PACK * cuts[1]], F32, name="first")
+        gathered[0, 0, SPLIT] = by_plane(plain[:])
+        gathered[0, SPLIT, S] = by_plane(gated[:])
+        gathered[1, cuts[0], cuts[1]] = by_plane(first[:])
+        gathered[1, cuts[1], cuts[2]] = by_plane(second[:])
+        third = PACK * (cuts[3] - cuts[2])
+        gathered[1, cuts[2], cuts[3]] = by_plane(plain[:, 0:third])
+        gathered[1, cuts[3], cuts[4]] = by_plane(plain[:, third : third + PACK * C])
 
-        def reuse(tile, pieces):
-            flat, at = tile[:].rearrange("p d s -> p (d s)"), 0
-            for lo, hi in pieces:
-                gathered[1, lo, hi] = flat[:, at : at + PACK * (hi - lo)].rearrange("p (d s) -> p d s", d=PACK)
-                at = at + PACK * (hi - lo)
-
-
-        place(0, 0, S, 512)
-        piece(0, 0, 896)
-        piece(0, 896, S)
-        piece(1, 0, 640)
-        gather_vector(0, 0, 896, 1024)
+        nc.vector.tensor_copy(part(gathered, 0, 0, HELP)[:, 0, :], window(0, 0, 0, HELP))
         for d in range(PACK):
-            gather_scalar(0, d, 896 if d else 1024, S)
-        for lo, hi in ((0, 384), (384, 896)):
+            gather_scalar(0, d, 0 if d else HELP, SPLIT)
+        for lo, hi in ((SPLIT, SPLIT + EARLY), (SPLIT + EARLY, S)):
             for d in range(PACK - 1):
-                gather_gated(0, d, lo, hi)
-        gather_gated(0, PACK - 1, 0, 896)
-        weave_gpsimd(0, 0, 896)
-        weave_gated(0, 896, 1024)
-        weave_gated(0, 1024, S)
-        gathered[1, 640, 1024] = second
-        reuse(gathered[0, 896, S], ((1024, 1408), (1408, S)))
-        for lo, hi in ((0, 640), (640, 1024), (1024, 1408), (1408, S)):
+                gather_gated(d, lo, hi)
+        gather_gated(PACK - 1, SPLIT, S)
+        weave_gpsimd(0, SPLIT, S, True)
+        weave_vector(0, BANK, SPLIT)
+        weave_vector(0, 0, BANK)
+
+        for lo, hi in zip(cuts, cuts[1:]):
             for d in range(PACK):
                 gather_scalar(1, d, lo, hi)
-        place(1, 0, 512, 0)
-        tail = 512 + S - 80
-        place(1, 640, 1024, tail)
-        place(1, 512, 640, tail + 384)
-        gate_gpsimd(1, 512, 640)
-        weave_gated(1, 0, 512)
-        quantise(0, 512, S)
-        products(0, 4, E)
-        gate_gpsimd(1, 640, 720)
-        weave_gated(1, 720, 1024)
-        quantise_parts(((1, 0, 512), (0, 0, 512)), woven[:, 0 : 1024 * PACK])
-        products(1, 0, 4)
-        products(0, 0, 4)
-        quantise_parts(((1, 640, 1024), (1, 512, 640)), woven[:, tail * PACK :])
-        products(1, 4, 8)
-        rounded[1, 1024, S] = woven[:, 0 : 512 * PACK]
-        gate_gpsimd(1, 1280, 1408)
-        weave_gated(1, 1024, 1280)
-        weave_gated(1, 1408, S)
-        quantise(1, 1024, 1408)
-        products(1, 8, 11)
-        quantise(1, 1408, S)
-        products(1, 11, 12)
-        for low, high in BANKS:
-            drain(low, high, "vector" if low == 8 else "scalar")
+        weave_gpsimd(1, BANK, cuts[1], False)
+        weave_vector(1, 0, BANK)
+        quantise(woven_at(lead, 2 * BANK), (0, 0, 2 * BANK))
+        weave_gpsimd(1, cuts[2] - SHARES[1], cuts[2], False)
+        weave_vector(1, cuts[1], cuts[2] - SHARES[1])
+        quantise(woven_at(lead + 2 * BANK, 2 * BANK), (0, 2 * BANK, S), (1, 0, BANK))
+        quantise(woven_at(0, BANK), (1, BANK, 2 * BANK))
+        weave_gpsimd(1, cuts[3] - SHARES[2], cuts[3], False)
+        weave_vector(1, cuts[2], cuts[3] - SHARES[2])
+        weave_vector(1, cuts[3], S)
+        quantise(woven_at(lead + S, cuts[3] - cuts[2]), (1, cuts[2], cuts[3]))
+        quantise(woven_at(lead + S + cuts[3] - cuts[2], C), (1, cuts[3], S))
+        for low, high in GROUPS:
+            copy = nc.vector.tensor_copy if low == 8 else nc.scalar.copy
+            copy(dx[:, low * C : high * C], banks[low][:, 0 : (high - low) * C])
 
         one = keep.tile([P, T], F32, name="one")
         both = keep.tile([P, T], F32, name="both")

@@ -25,10 +25,10 @@ BANK = 512
 FLOPS = 2 * N * K * S
 BYTES = 4 * N * T + E * N * K // 2 + E * N * K // 32 + 4 * S + 2 * P * (S + 2 * T) // 16 + 4 * K * T
 
-SPLIT = 576
+SPLIT = 608
 HELP = 128
 EARLY = 384
-SHARES = (32, 96, 128)
+SHARES = (0, 96, 112)
 WIDE = S - SPLIT + 16
 FOUR = 4
 RUN = 2
@@ -89,7 +89,6 @@ def tile_moe_bdx_lin_none_kernel(tc, dyT, w_words, w_scales, gate, offs, pos1, p
         for d in range(PACK):
             load_plane(1, d)
         nc.sync.dma_start(out=late, in_=by_bank[:, 2, :])
-        load_gate(BANK, cuts[1])
         nc.sync.dma_start(out=w_sb[:].bitcast(I32), in_=w_words.bitcast(I32).rearrange("e a p n -> p (e a) n"))
         scale_rows = w_scales.bitcast(I32).rearrange("e a f k -> f (e a) k")
         for q in range(4):
@@ -211,7 +210,6 @@ def tile_moe_bdx_lin_none_kernel(tc, dyT, w_words, w_scales, gate, offs, pos1, p
         for lo, hi in zip(cuts, cuts[1:]):
             for d in range(PACK):
                 gather_scalar(1, d, lo, hi)
-        weave_gpsimd(1, BANK, cuts[1], False)
         weave_vector(1, 0, BANK)
         quantise(woven_at(lead, 2 * BANK), (0, 0, 2 * BANK))
         weave_gpsimd(1, cuts[2] - SHARES[1], cuts[2], False)

@@ -77,7 +77,6 @@ def tile_moe_bdx_lin_none_kernel(tc, dyT, w_words, w_scales, gate, offs, pos1, p
         astride = 2 * (cuts[2] - cuts[1]) - FOUR // 2
         late = second[:, astride : astride + FOUR]
         columns = {0: early[:, 0, :], 1: early[:, 1, :], 2: late}
-        nc.scalar.dma_start(out=early[:, :, 0:FOUR], in_=by_bank[:, 0:2, :])
 
         load_plane(0, 0)
         nc.sync.dma_start(offs_sb[:], offs)
@@ -86,6 +85,7 @@ def tile_moe_bdx_lin_none_kernel(tc, dyT, w_words, w_scales, gate, offs, pos1, p
         load_plane(0, 2)
         load_gate(SPLIT + EARLY, S)
         load_plane(0, 3)
+        nc.sync.dma_start(out=early[:, :, 0:FOUR], in_=by_bank[:, 0:2, :])
         for d in range(PACK):
             load_plane(1, d)
         nc.sync.dma_start(out=late, in_=by_bank[:, 2, :])

from contextlib import ExitStack

import concourse.mybir as mybir
from concourse.masks import make_identity

F32 = mybir.dt.float32
BF16 = mybir.dt.bfloat16
U32 = mybir.dt.uint32
I32 = mybir.dt.int32
U16 = mybir.dt.uint16
U8 = mybir.dt.uint8
FP8X4 = mybir.dt.float8_e4m3fn_x4
FP4X4 = mybir.dt.float4_e2m1fn_x4
MULT = mybir.AluOpType.mult
ADD = mybir.AluOpType.add
COPY = mybir.ActivationFunctionType.Copy

P = 128
K, T, E, C, N = 128, 768, 12, 128, 1024
S = E * C
PASSES = N // 512
PACK = 4
BANK = 512

FLOPS = 2 * N * K * S
BYTES = 4 * N * T + E * N * K // 2 + E * N * K // 32 + 4 * S + 2 * P * (S + 2 * T) // 16 + 4 * K * T

SPLIT = 608
HELP = 128
EARLY = 384
SHARES = (0, 96, 112)
WIDE = S - SPLIT + 16
FOUR = 4
RUN = 2
GROUPS = ((0, 4), (4, 8), (8, 10), (10, 11), (11, 12))


def tile_moe_bdx_lin_none_kernel(tc, dyT, w_words, w_scales, gate, offs, pos1, pos2, out):
    nc = tc.nc
    with ExitStack() as ctx:
        lists = ctx.enter_context(tc.tile_pool(name="lists", bufs=1))
        keep = ctx.enter_context(tc.tile_pool(name="keep", bufs=1))
        psum = ctx.enter_context(tc.psum_pool(name="psum", bufs=1))

        offs_sb = lists.tile([P, S // 16], U16, name="offs_sb")
        pos1_sb = lists.tile([P, T // 16], U16, name="pos1_sb")
        pos2_sb = lists.tile([P, T // 16], U16, name="pos2_sb")

        w_sb = keep.tile([P, E * PASSES, 2 * K], U8, name="w_sb", align_bytes=64)
        ws_sb = keep.tile([P, E * PASSES, K], U8, name="ws_sb", align_bytes=64)
        gate_sb = keep.tile([P, S], F32, name="gate_sb")
        planes = {
            (a, d): keep.tile([P, WIDE if a == 0 and d else T], F32, name=f"plane_{a}_{d}")
            for a in range(PASSES)
            for d in range(PACK)
        }
        cuts = (0, BANK + SHARES[0], 2 * BANK, S - C, S)
        second = keep.tile([P, PACK * (cuts[2] - cuts[1])], F32, name="second")

        ident = keep.tile([P, P], F32, name="ident", align_bytes=64)
        make_identity(nc, ident[:])
        for d in (3, 2):
            nc.vector.memset(planes[0, d][:, T:], 0.0)
        nc.scalar.activation(planes[0, 1][:, T:], planes[0, 3][:, T:], COPY)
        nc.vector.memset(ws_sb[:].rearrange("p g k -> p (g k)").bitcast(I32), 0)

        rows = dyT.rearrange("(a p d) t -> a d p t", a=PASSES, d=PACK)

        def load_plane(a, d):
            nc.sync.dma_start(out=planes[a, d][:, 0:T], in_=rows[a, d])

        def load_gate(lo, hi):
            nc.sync.dma_start(out=gate_sb[:, lo:hi], in_=gate[0:P, lo:hi])

        by_bank = gate[0, :].rearrange("(b p i) -> p b i", p=P, i=FOUR)
        early = keep.tile([P, 2, 8], F32, name="early")
        astride = 2 * (cuts[2] - cuts[1]) - FOUR // 2
        late = second[:, astride : astride + FOUR]
        columns = {0: early[:, 0, :], 1: early[:, 1, :], 2: late}

        load_plane(0, 0)
        nc.sync.dma_start(offs_sb[:], offs)
        load_gate(SPLIT, SPLIT + EARLY)
        load_plane(0, 1)
        load_plane(0, 2)
        load_gate(SPLIT + EARLY, S)
        load_plane(0, 3)
        nc.sync.dma_start(out=early[:, :, 0:FOUR], in_=by_bank[:, 0:2, :])
        for d in range(PACK):
            load_plane(1, d)
        nc.sync.dma_start(out=late, in_=by_bank[:, 2, :])
        nc.sync.dma_start(out=w_sb[:].bitcast(I32), in_=w_words.bitcast(I32).rearrange("e a p n -> p (e a) n"))
        scale_rows = w_scales.bitcast(I32).rearrange("e a f k -> f (e a) k")
        for q in range(4):
            nc.sync.dma_start(out=ws_sb[:].bitcast(I32)[32 * q : 32 * q + 4], in_=scale_rows[4 * q : 4 * q + 4])
        nc.sync.dma_start(pos1_sb[:], pos1)
        nc.sync.dma_start(pos2_sb[:], pos2)

        gate_banks = {}
        for b in (1, 0, 2):
            gate_banks[b] = psum.tile([P, BANK], F32, name=f"gate_bank_{b}")
            for i in range(FOUR):
                nc.tensor.transpose(
                    gate_banks[b][:, i::FOUR], columns[b][:, i : i + 1].to_broadcast([P, P]), ident[:]
                )

        gathered, rounded, codes, scales, banks = {}, {}, {}, {}, {}
        dx = keep.tile([P, S], F32, name="dx")

        def part(table, a, lo, hi, each=1):
            first = [at for b, at, end in table if b == a and at <= lo < end][0]
            whole = [ap for (b, at, end), ap in table.items() if b == a and at == first][0]
            cut = slice((lo - first) * each, (hi - first) * each)
            return whole[:, cut] if whole.ndim == 2 else whole[:, :, cut]

        def by_plane(flat):
            return flat.rearrange("p (d s) -> p d s", d=PACK)

        def window(a, d, lo, hi):
            return planes[a, d][:].indirect(offs_sb[:, lo // 16 : hi // 16])

        def gather_scalar(a, d, lo, hi):
            nc.scalar.activation(part(gathered, a, lo, hi)[:, d, :], window(a, d, lo, hi), COPY)

        def gather_gated(d, lo, hi):
            nc.vector.tensor_tensor(part(gathered, 0, lo, hi)[:, d, :], window(0, d, lo, hi), gate_sb[:, lo:hi], MULT)

        def weave_vector(a, lo, hi):
            runs = slice(lo % BANK // RUN, (lo % BANK + hi - lo) // RUN)
            gates = gate_banks[lo // BANK][:].rearrange("p (n i) -> p n i", i=RUN)[:, runs, :]
            nc.vector.tensor_tensor(
                part(rounded, a, lo, hi, PACK).rearrange("p (n i d) -> p n d i", i=RUN, d=PACK),
                part(gathered, a, lo, hi).rearrange("p d (n i) -> p n d i", i=RUN),
                gates.unsqueeze(2).to_broadcast([P, (hi - lo) // RUN, PACK, RUN]),
                MULT,
            )

        def weave_gpsimd(a, lo, hi, gated):
            into = part(rounded, a, lo, hi, PACK).rearrange("p (s d) -> p s d", d=PACK)
            values = part(gathered, a, lo, hi).rearrange("p d s -> p s d")
            if gated:
                nc.gpsimd.tensor_scalar(into, values, 1.0, 0.0, MULT, ADD)
            else:
                nc.gpsimd.tensor_tensor(into, values, gate_sb[:, lo:hi].unsqueeze(2).to_broadcast([P, hi - lo, PACK]), MULT)

        def quantise(values, *parts):
            width = sum(hi - lo for a, lo, hi in parts)
            made = keep.tile([P, width], U32, name=f"codes_{parts[0][0]}_{parts[0][1]}", align_bytes=64)
            plane = keep.tile([P, width], U8, name=f"scales_{parts[0][0]}_{parts[0][1]}", align_bytes=64)
            nc.vector.quantize_mx(out=made[:].bitcast(FP8X4), scales=plane[:], in_=values)
            at = 0
            for a, lo, hi in parts:
                codes[a, lo, hi] = made[:, at : at + hi - lo]
                scales[a, lo, hi] = plane[:, at : at + hi - lo]
                at = at + hi - lo
                for e in range(lo // C, hi // C):
                    multiply(a, e)

        done = []

        def multiply(a, e):
            low, high = [group for group in GROUPS if group[0] <= e < group[1]][0]
            before = len([other for other in done if low <= other < high])
            if before == 0:
                banks[low] = psum.tile([P, BANK], F32, name=f"bank_{low}")
            nc.tensor.matmul_mx(
                out=banks[low][:, (e - low) * C : (e - low + 1) * C],
                lhsT=w_sb[:, PASSES * e + a, :].bitcast(FP4X4),
                lhsT_scale=ws_sb[:, PASSES * e + a, :],
                rhs=part(codes, a, e * C, (e + 1) * C).bitcast(FP8X4),
                rhs_scale=part(scales, a, e * C, (e + 1) * C),
                start=before == 0,
                stop=before == PASSES * (high - low) - 1,
            )
            done.append(e)

        lead = BANK - SHARES[1]
        woven = keep.tile([P, (lead + S + BANK) * PACK], BF16, name="woven", align_bytes=64)

        def woven_at(at, width):
            return woven[:, at * PACK : (at + width) * PACK]

        rounded[0, 0, S] = woven_at(lead, S)
        rounded[1, 0, BANK] = woven_at(lead + S, BANK)
        rounded[1, BANK, 2 * BANK] = woven_at(0, BANK)
        rounded[1, 2 * BANK, S] = woven_at(lead + S, BANK)

        plain = keep.tile([P, PACK * SPLIT], F32, name="plain")
        gated = keep.tile([P, PACK * (S - SPLIT)], F32, name="gated")
        first = keep.tile([P, PACK * cuts[1]], F32, name="first")
        gathered[0, 0, SPLIT] = by_plane(plain[:])
        gathered[0, SPLIT, S] = by_plane(gated[:])
        gathered[1, cuts[0], cuts[1]] = by_plane(first[:])
        gathered[1, cuts[1], cuts[2]] = by_plane(second[:])
        third = PACK * (cuts[3] - cuts[2])
        gathered[1, cuts[2], cuts[3]] = by_plane(plain[:, 0:third])
        gathered[1, cuts[3], cuts[4]] = by_plane(plain[:, third : third + PACK * C])

        nc.vector.tensor_copy(part(gathered, 0, 0, HELP)[:, 0, :], window(0, 0, 0, HELP))
        for d in range(PACK):
            gather_scalar(0, d, 0 if d else HELP, SPLIT)
        for lo, hi in ((SPLIT, SPLIT + EARLY), (SPLIT + EARLY, S)):
            for d in range(PACK - 1):
                gather_gated(d, lo, hi)
        gather_gated(PACK - 1, SPLIT, S)
        weave_gpsimd(0, SPLIT, S, True)
        weave_vector(0, BANK, SPLIT)
        weave_vector(0, 0, BANK)

        for lo, hi in zip(cuts, cuts[1:]):
            for d in range(PACK):
                gather_scalar(1, d, lo, hi)
        weave_vector(1, 0, BANK)
        quantise(woven_at(lead, 2 * BANK), (0, 0, 2 * BANK))
        weave_gpsimd(1, cuts[2] - SHARES[1], cuts[2], False)
        weave_vector(1, cuts[1], cuts[2] - SHARES[1])
        quantise(woven_at(lead + 2 * BANK, 2 * BANK), (0, 2 * BANK, S), (1, 0, BANK))
        quantise(woven_at(0, BANK), (1, BANK, 2 * BANK))
        weave_gpsimd(1, cuts[3] - SHARES[2], cuts[3], False)
        weave_vector(1, cuts[2], cuts[3] - SHARES[2])
        weave_vector(1, cuts[3], S)
        quantise(woven_at(lead + S, cuts[3] - cuts[2]), (1, cuts[2], cuts[3]))
        quantise(woven_at(lead + S + cuts[3] - cuts[2], C), (1, cuts[3], S))
        for low, high in GROUPS:
            copy = nc.vector.tensor_copy if low == 8 else nc.scalar.copy
            copy(dx[:, low * C : high * C], banks[low][:, 0 : (high - low) * C])

        one = keep.tile([P, T], F32, name="one")
        both = keep.tile([P, T], F32, name="both")
        nc.vector.tensor_copy(one[:, 0:128], dx[:].indirect(pos1_sb[:, 0:8]))
        for lo, hi in ((128, 256), (256, 512), (512, T)):
            nc.scalar.activation(one[:, lo:hi], dx[:].indirect(pos1_sb[:, lo // 16 : hi // 16]), COPY)
        for lo, hi in ((128, 256), (0, 128), (256, 512), (512, 640), (640, T)):
            nc.vector.tensor_tensor(both[:, lo:hi], dx[:].indirect(pos2_sb[:, lo // 16 : hi // 16]), one[:, lo:hi], ADD)
            if lo >= 256:
                at = 0 if lo == 256 else lo
                nc.sync.dma_start(out=out[:, at:hi], in_=both[:, at:hi])
